import numpy as np
import ml_dtypes


def mxq(x, axis, fmt="e4m3"):
    dtype, down = {"e4m3": (ml_dtypes.float8_e4m3fn, 7), "e5m2": (ml_dtypes.float8_e5m2, 14)}[fmt]
    v = np.moveaxis(np.asarray(x, np.float32).astype(ml_dtypes.bfloat16).astype(np.float64), axis, -1)
    blocks = v.reshape(v.shape[:-1] + (-1, 32))
    amax = np.abs(blocks).max(-1, keepdims=True)
    byte = np.maximum(np.where(amax > 0, np.frexp(amax)[1] - 1 + 127, 0) - down, 1)
    scale = np.exp2(byte - 127.0)
    codes = (blocks / scale).astype(np.float32).astype(dtype).astype(np.float64)
    return np.moveaxis((codes * scale).reshape(v.shape), -1, axis)


WIDE = False


def mx_kscale(k):
    if not WIDE:
        return np.ones(k)
    levels = np.array([10, -10, 5, -5, 0])
    if k % 512:
        return np.exp2(np.random.permutation(np.resize(levels, k // 32))).repeat(32)
    a = np.empty((k // 512, 16))
    for p in range(k // 512):
        a[p, :8] = np.random.permutation(np.resize(levels, 8))
        for g in range(8):
            far = levels[np.abs(levels - a[p, g]) >= 10]
            a[p, g + 8] = far[np.random.randint(len(far))]
    return np.exp2(a.ravel()).repeat(32)


def f64(x):
    return np.asarray(x).astype(np.float64)


def striped(idx):
    return np.tile(idx.reshape(-1, 16).T, (8, 1)).astype(np.uint16)


def unstriped(offs):
    return offs[:16].T.reshape(-1).astype(np.int64)


def pack_weight(w):
    k, n = w.shape
    w = f64(np.asarray(w, np.float32).astype(ml_dtypes.bfloat16)).reshape(k // 32, 32, n)
    amax = np.abs(w).max(1)
    byte = np.clip(np.where(amax > 0, np.frexp(amax)[1] - 1 + 127 - 7, 1), 1, 254)
    scaled = (w * np.exp2(127.0 - byte)[:, None, :]).reshape(k, n).astype(np.float32)
    words = np.ascontiguousarray(scaled.reshape(k // 512, 128, 4, n).transpose(0, 1, 3, 2)).astype(ml_dtypes.float8_e4m3fn).view(np.uint8)
    return words, np.ascontiguousarray(byte.astype(np.uint8).reshape(k // 512, 16, n))


def unpack_weight(words, scales):
    g, p, n, _ = words.shape
    vals = np.ascontiguousarray(words).view(ml_dtypes.float8_e4m3fn).astype(np.float64) * np.repeat(np.exp2(scales.astype(np.float64) - 127.0), 8, axis=1)[..., None]
    return vals.transpose(0, 1, 3, 2).reshape(g * 512, n)


def relu(v):
    return np.maximum(v, 0.0)

def planes(y):
    n, m = y.shape
    v = y.astype(np.float32).astype(ml_dtypes.bfloat16).astype(np.float64).reshape(n // 32, 32, m)
    top = np.abs(v).max(1)
    byte = np.clip(np.where(top > 0, np.frexp(top)[1] - 1 + 127 - 7, 1), 1, 254)
    codes = (v * np.exp2(127.0 - byte)[:, None, :]).reshape(n, m).astype(np.float32).astype(ml_dtypes.float8_e4m3fn).view(np.uint8)
    words = codes.reshape(n // 512, 128, 4, m).transpose(0, 1, 3, 2)
    return np.ascontiguousarray(words), np.ascontiguousarray(byte.astype(np.uint8).reshape(n // 512, 16, m))


K, T, S, H, U = 512, 2048, 1024, 512, 1024


def setup_inputs():
    n = np.random.standard_normal
    s = mx_kscale(K)[:, None]
    u = mx_kscale(H)
    packed_xT = pack_weight(n((K, T)) * s)
    packed_w3 = pack_weight(n((H, H)) / np.sqrt(H) / u[:, None])
    return {
        "x_words": packed_xT[0],
        "x_scales": packed_xT[1],
        "w1": (n((K, H)) / np.sqrt(2 * K) / s * u).astype(np.float32),
        "w2": (n((K, H)) / np.sqrt(2 * K) / s * u).astype(np.float32),
        "w3_words": packed_w3[0],
        "w3_scales": packed_w3[1],
        "offs": striped(np.random.permutation(T)[:S]),
        "src": striped(np.random.permutation(S)[(S * np.random.uniform(0, 1, U) ** 4).astype(np.int64)]),
        "dst": striped(np.random.permutation(S)),
    }


def reference(x_words, x_scales, w1, w2, w3_words, w3_scales, offs, src, dst):
    xq = unpack_weight(x_words, x_scales)[:, unstriped(offs)]
    y = mxq(f64(w1), 0, "e4m3").T @ xq
    e = mxq(f64(w2), 0, "e4m3").T @ xq
    z = relu(y[:, unstriped(src)] + e[:, unstriped(dst)])
    out_0 = unpack_weight(w3_words, w3_scales).T @ mxq(z, 0, "e4m3")
    return (out_0,) + planes(out_0)

@@ -1,0 +1,295 @@
+from contextlib import ExitStack
+
+import concourse.mybir as mybir
+
+K, T, S, H = 512, 2048, 1024, 512
+FLOPS = 2 * K * H * S * 2 + 2 * H * H * S
+
+F32 = mybir.dt.float32
+BF16 = mybir.dt.bfloat16
+I32 = mybir.dt.int32
+U32 = mybir.dt.uint32
+U16 = mybir.dt.uint16
+U8 = mybir.dt.uint8
+FP8X4 = mybir.dt.float8_e4m3fn_x4
+ADD = mybir.AluOpType.add
+RELU = mybir.ActivationFunctionType.Relu
+
+P = 128
+PACK = 4
+BANK = 512
+LIST_ROWS = 16
+CHUNKS = (256, 256, 256, 128, 128)
+
+
+def load_scale_rows(queue, plane, scales):
+    for q in range(4):
+        queue.dma_start(out=plane[32 * q : 32 * q + 4, :].bitcast(I32), in_=scales[0, 4 * q : 4 * q + 4, :].bitcast(I32))
+
+
+def interleaved(planes, words):
+    return (
+        words.rearrange("p (c i) t -> p c t i", i=4),
+        planes.rearrange("p t (c i) -> p c t i", i=4),
+    )
+
+
+def tile_picked_hub_relu_po_kernel(
+    tc, x_words, x_scales, w1, w2, w3_words, w3_scales, offs, src, dst, out_0, out_1, out_2
+):
+    nc = tc.nc
+    with ExitStack() as ctx:
+        keep = ctx.enter_context(tc.tile_pool(name="keep", bufs=1))
+        turns = ctx.enter_context(tc.tile_pool(name="turns", bufs=1))
+        psum = ctx.enter_context(tc.psum_pool(name="psum", bufs=1))
+
+        offs_sb = keep.tile([P, S // LIST_ROWS], U16, name="offs_sb")
+        src_sb = keep.tile([P, S // LIST_ROWS], U16, name="src_sb")
+        dst_sb = keep.tile([P, S // LIST_ROWS], U16, name="dst_sb")
+        x_table = keep.tile([P, T], I32, name="x_table", align_bytes=64)
+        x_plane = turns.tile([P, T], U8, name="x_plane", tag="x_turn0", align_bytes=64)
+        w3_table = keep.tile([P, H], I32, name="w3_table", align_bytes=64)
+        w3_plane = keep.tile([P, H], U8, name="w3_plane", align_bytes=64)
+        w_raw = [keep.tile([P, PACK, H], F32, name="w_raw%d" % i, align_bytes=64) for i in range(2)]
+        warm = keep.tile([P, 8], F32, name="warm")
+        warm_out = keep.tile([P, 8], F32, name="warm_out")
+
+        nc.vector.memset(x_plane[:].bitcast(I32), 0)
+        nc.vector.memset(warm[:], 0.0)
+        nc.vector.memset(w3_plane[:].bitcast(I32), 0)
+        load_scale_rows(nc.scalar, x_plane, x_scales)
+        nc.scalar.activation(warm_out[:], warm[:], RELU)
+        nc.sync.dma_start(offs_sb[:], offs)
+        nc.sync.dma_start(src_sb[:], src)
+        nc.sync.dma_start(dst_sb[:], dst)
+        nc.sync.dma_start(out=w_raw[0][:], in_=w1.rearrange("(p j) c -> p j c", j=PACK))
+        nc.sync.dma_start(out=x_table[:], in_=x_words[0].rearrange("p n r -> p (n r)").bitcast(I32))
+        nc.sync.dma_start(out=w_raw[1][:], in_=w2.rearrange("(p j) c -> p j c", j=PACK))
+        nc.sync.dma_start(out=w3_table[:], in_=w3_words[0].rearrange("p n r -> p (n r)").bitcast(I32))
+        load_scale_rows(nc.sync, w3_plane, w3_scales)
+
+        def entries(lst, first, count):
+            return lst[:, first // LIST_ROWS : (first + count) // LIST_ROWS]
+
+        x_bytes = keep.tile([P, S], U8, name="x_bytes", align_bytes=64)
+        nc.vector.tensor_copy(x_bytes[:], x_plane[:].indirect(offs_sb[:]))
+
+        def quantise_weight(i, copy):
+            grouped = keep.tile([P, PACK, P, PACK], BF16, name="w_grouped%d" % i, align_bytes=64)
+            copy(
+                grouped[:].rearrange("p t m j -> p m j t"),
+                w_raw[i][:].rearrange("p j (m t) -> p m j t", t=PACK),
+            )
+            codes = keep.tile([P, H], U32, name="w_codes%d" % i, align_bytes=64)
+            plane = keep.tile([P, H], U8, name="w_plane%d" % i, align_bytes=64)
+            nc.vector.quantize_mx(
+                out=codes[:].bitcast(FP8X4), scales=plane[:], in_=grouped[:].rearrange("p t m j -> p (t m j)")
+            )
+            return codes, plane
+
+        weights = [quantise_weight(0, nc.scalar.copy)]
+
+        x_codes = []
+        for half in range(S // BANK):
+            codes = turns.tile([P, BANK], U32, name="x_codes%d" % half, tag="x_turn%d" % half, align_bytes=64)
+            nc.vector.tensor_copy(codes[:], x_table[:].bitcast(U32).indirect(entries(offs_sb, half * BANK, BANK)))
+            x_codes.append(codes)
+
+        weights.append(quantise_weight(1, nc.vector.tensor_copy))
+
+        windows = {}
+        bank_turn = [0]
+
+        def next_bank(shape):
+            tag = "bank%d" % (bank_turn[0] % 8)
+            bank_turn[0] = bank_turn[0] + 1
+            return psum.tile(shape, F32, name=tag, tag=tag)
+
+        def node_product(i, t, half):
+            codes, plane = weights[i]
+            cols = slice(t * P, (t + 1) * P)
+            nodes = slice(half * BANK, (half + 1) * BANK)
+            if (i, t) not in windows:
+                windows[(i, t)] = keep.tile([P, S], F32, name="window%d_%d" % (i, t), align_bytes=64)
+            acc = next_bank([P, BANK])
+            nc.tensor.matmul_mx(
+                out=acc[:],
+                lhsT=codes[:, cols].bitcast(FP8X4),
+                lhsT_scale=plane[:, cols],
+                rhs=x_codes[half][:].bitcast(FP8X4),
+                rhs_scale=x_bytes[:, nodes],
+                start=True,
+                stop=True,
+            )
+            nc.scalar.copy(windows[(i, t)][:, nodes], acc[:])
+
+        for half in range(2):
+            for t in range(2):
+                node_product(0, t, half)
+        for i, t in ((1, 0), (0, 2), (1, 1), (0, 3), (1, 2), (1, 3)):
+            for half in range(2):
+                node_product(i, t, half)
+
+        w3_codes = keep.tile([P, H], I32, name="w3_codes", align_bytes=64)
+        w3_bytes = keep.tile([P, H], U8, name="w3_bytes", align_bytes=64)
+
+        def deal_w3():
+            nc.vector.tensor_copy(
+                w3_codes[:].rearrange("p (t m) -> p m t", t=PACK), w3_table[:].rearrange("p (m t) -> p m t", t=PACK)
+            )
+            nc.vector.tensor_copy(
+                w3_bytes[:].rearrange("p (t m) -> p m t", t=PACK), w3_plane[:].rearrange("p (m t) -> p m t", t=PACK)
+            )
+
+        firsts = [sum(CHUNKS[:c]) for c in range(len(CHUNKS))]
+        picked, sums, rounded, results, z_ops = {}, {}, {}, {}, {}
+        out_codes = keep.tile([P, S], U32, name="out_codes", align_bytes=64)
+        out_plane = keep.tile([P, S], U8, name="out_plane", align_bytes=64)
+        out_rows = out_0.rearrange("(p t) n -> p t n", t=PACK)
+        out_words = out_1[0].rearrange("p n r -> p (n r)").bitcast(I32)
+
+        tags = {}
+
+        def turn_tile(key, shape, dtype, after=None):
+            tag = tags.pop(after) if after is not None else "turn_%s%d%d" % key
+            tags[key] = tag
+            return turns.tile(shape, dtype, name=tag, tag=tag, align_bytes=64)
+
+        def pick_sources(c, t, after=None):
+            n = CHUNKS[c]
+            picked[(c, t)] = turn_tile(("y", c, t), [P, n], F32, after)
+            nc.vector.tensor_copy(picked[(c, t)][:], windows[(0, t)][:].indirect(entries(src_sb, firsts[c], n)))
+
+        def add_targets(c, t):
+            n = CHUNKS[c]
+            if c not in sums:
+                sums[c] = keep.tile([P, PACK, n], F32, name="sums%d" % c, align_bytes=64)
+            nc.vector.tensor_tensor(
+                sums[c][:, t, :], windows[(1, t)][:].indirect(entries(dst_sb, firsts[c], n)), picked[(c, t)][:], ADD
+            )
+
+        def relu_round(c, on_vector=False):
+            n = CHUNKS[c]
+            rounded[("z", c)] = turn_tile(("z", c, 0), [P, n, PACK], BF16)
+            words, planes = interleaved(sums[c][:], rounded[("z", c)][:])
+            if on_vector:
+                nc.vector.tensor_scalar_max(words, planes, 0.0)
+            else:
+                nc.scalar.activation(words, planes, RELU)
+
+        def quantise_z(c):
+            n = CHUNKS[c]
+            codes = keep.tile([P, n], U32, name="z_codes%d" % c, align_bytes=64)
+            plane = keep.tile([P, n], U8, name="z_plane%d" % c, align_bytes=64)
+            nc.vector.quantize_mx(
+                out=codes[:].bitcast(FP8X4), scales=plane[:], in_=rounded[("z", c)][:].rearrange("p n t -> p (n t)")
+            )
+            z_ops[c] = (codes, plane)
+
+        def edge_product(c):
+            n = CHUNKS[c]
+            codes, plane = z_ops[c]
+            results[c] = keep.tile([P, PACK, n], F32, name="results%d" % c, align_bytes=64)
+            per_bank = BANK // n
+            for t0 in range(0, PACK, per_bank):
+                acc = next_bank([P, per_bank, n])
+                for u in range(per_bank):
+                    cols = slice((t0 + u) * P, (t0 + u + 1) * P)
+                    nc.tensor.matmul_mx(
+                        out=acc[:, u, :],
+                        lhsT=w3_codes[:, cols].bitcast(FP8X4),
+                        lhsT_scale=w3_bytes[:, cols],
+                        rhs=codes[:].bitcast(FP8X4),
+                        rhs_scale=plane[:],
+                        start=True,
+                        stop=True,
+                    )
+                nc.scalar.copy(results[c][:, t0 : t0 + per_bank, :], acc[:])
+            nc.sync.dma_start(out=out_rows[:, :, firsts[c] : firsts[c] + n], in_=results[c][:])
+
+        def round_out(c, on_vector=False):
+            n = CHUNKS[c]
+            rounded[("o", c)] = turn_tile(("o", c, 0), [P, n, PACK], BF16)
+            words, planes = interleaved(results[c][:], rounded[("o", c)][:])
+            if on_vector:
+                nc.vector.tensor_copy(words, planes)
+            else:
+                nc.scalar.copy(words, planes)
+
+        def quantise_out(c):
+            cols = slice(firsts[c], firsts[c] + CHUNKS[c])
+            nc.vector.quantize_mx(
+                out=out_codes[:, cols].bitcast(FP8X4),
+                scales=out_plane[:, cols],
+                in_=rounded[("o", c)][:].rearrange("p n t -> p (n t)"),
+            )
+            nc.sync.dma_start(out=out_words[:, cols], in_=out_codes[:, cols].bitcast(I32))
+
+        for t in range(2):
+            pick_sources(0, t)
+            pick_sources(1, t)
+        add_targets(0, 0)
+        add_targets(1, 0)
+        pick_sources(0, 2)
+        add_targets(0, 1)
+        add_targets(1, 1)
+        pick_sources(0, 3)
+        deal_w3()
+        add_targets(0, 2)
+        add_targets(0, 3)
+        relu_round(0)
+        pick_sources(1, 2, ("y", 0, 2))
+        pick_sources(1, 3, ("y", 0, 3))
+        add_targets(1, 2)
+        add_targets(1, 3)
+        relu_round(1)
+        quantise_z(0)
+        edge_product(0)
+        pick_sources(2, 0, ("z", 0, 0))
+        pick_sources(2, 1, ("y", 1, 3))
+        add_targets(2, 0)
+        quantise_z(1)
+        round_out(0)
+        edge_product(1)
+        round_out(1)
+        pick_sources(2, 2, ("z", 1, 0))
+        add_targets(2, 1)
+        pick_sources(2, 3, ("y", 2, 0))
+        add_targets(2, 2)
+        add_targets(2, 3)
+        relu_round(2)
+        quantise_out(0)
+        pick_sources(3, 0, ("o", 0, 0))
+        pick_sources(3, 1, ("y", 2, 2))
+        add_targets(3, 0)
+        pick_sources(3, 2, ("y", 2, 3))
+        add_targets(3, 1)
+        quantise_z(2)
+        edge_product(2)
+        pick_sources(3, 3, ("z", 2, 0))
+        add_targets(3, 2)
+        add_targets(3, 3)
+        relu_round(3)
+        round_out(2)
+        quantise_out(1)
+        pick_sources(4, 0, ("o", 1, 0))
+        pick_sources(4, 1, ("y", 3, 2))
+        add_targets(4, 0)
+        pick_sources(4, 2, ("y", 3, 3))
+        add_targets(4, 1)
+        quantise_z(3)
+        edge_product(3)
+        pick_sources(4, 3, ("z", 3, 0))
+        add_targets(4, 2)
+        add_targets(4, 3)
+        round_out(3)
+        relu_round(4, True)
+        quantise_out(2)
+        quantise_z(4)
+        edge_product(4)
+        quantise_out(3)
+        round_out(4, True)
+        quantise_out(4)
+        for q in range(4):
+            queue = nc.scalar if q % 2 else nc.sync
+            queue.dma_start(out=out_2[0, 4 * q : 4 * q + 4, :].bitcast(I32), in_=out_plane[32 * q : 32 * q + 4, :].bitcast(I32))

@@ -48,54 +48,54 @@ def tile_picked_hub_relu_po_kernel(
         dst_sb = keep.tile([P, S // LIST_ROWS], U16, name="dst_sb")
         x_table = keep.tile([P, T], I32, name="x_table", align_bytes=64)
         x_plane = turns.tile([P, T], U8, name="x_plane", tag="x_turn0", align_bytes=64)
-        w3_table = keep.tile([P, H], I32, name="w3_table", align_bytes=64)
-        w3_plane = keep.tile([P, H], U8, name="w3_plane", align_bytes=64)
         w_raw = [keep.tile([P, PACK, H], F32, name="w_raw%d" % i, align_bytes=64) for i in range(2)]
-        warm = keep.tile([P, 8], F32, name="warm")
-        warm_out = keep.tile([P, 8], F32, name="warm_out")
+        warm = turns.tile([P, 8], F32, name="warm", tag="warm", align_bytes=64)
+        warm_out = turns.tile([P, 8], F32, name="warm_out", tag="warm_out", align_bytes=64)
 
         nc.vector.memset(x_plane[:].bitcast(I32), 0)
         nc.vector.memset(warm[:], 0.0)
-        nc.vector.memset(w3_plane[:].bitcast(I32), 0)
         load_scale_rows(nc.scalar, x_plane, x_scales)
         nc.scalar.activation(warm_out[:], warm[:], RELU)
         nc.sync.dma_start(offs_sb[:], offs)
         nc.sync.dma_start(src_sb[:], src)
-        nc.sync.dma_start(dst_sb[:], dst)
-        nc.sync.dma_start(out=w_raw[0][:], in_=w1.rearrange("(p j) c -> p j c", j=PACK))
         nc.sync.dma_start(out=x_table[:], in_=x_words[0].rearrange("p n r -> p (n r)").bitcast(I32))
+        nc.sync.dma_start(out=w_raw[0][:], in_=w1.rearrange("(p j) c -> p j c", j=PACK))
+        nc.sync.dma_start(dst_sb[:], dst)
         nc.sync.dma_start(out=w_raw[1][:], in_=w2.rearrange("(p j) c -> p j c", j=PACK))
+        w3_table = turns.tile([P, H], I32, name="w3_table", tag="warm_out", align_bytes=64)
         nc.sync.dma_start(out=w3_table[:], in_=w3_words[0].rearrange("p n r -> p (n r)").bitcast(I32))
+        w3_plane = turns.tile([P, H], U8, name="w3_plane", tag="warm", align_bytes=64)
+        nc.vector.memset(w3_plane[:].bitcast(I32), 0)
         load_scale_rows(nc.sync, w3_plane, w3_scales)
 
         def entries(lst, first, count):
             return lst[:, first // LIST_ROWS : (first + count) // LIST_ROWS]
 
-        x_bytes = keep.tile([P, S], U8, name="x_bytes", align_bytes=64)
-        nc.vector.tensor_copy(x_bytes[:], x_plane[:].indirect(offs_sb[:]))
+        x_codes = keep.tile([P, S], U32, name="x_codes", align_bytes=64)
+        nc.vector.tensor_copy(x_codes[:], x_table[:].bitcast(U32).indirect(offs_sb[:]))
 
-        def quantise_weight(i, copy):
-            grouped = keep.tile([P, PACK, P, PACK], BF16, name="w_grouped%d" % i, align_bytes=64)
+        weights = {}
+
+        def quantise_weight(i, pair, copy=nc.scalar.copy):
+            name = "w_grouped%d%d" % (i, pair)
+            grouped = turns.tile([P, 2, P, PACK], BF16, name=name, tag=name, align_bytes=64)
             copy(
                 grouped[:].rearrange("p t m j -> p m j t"),
-                w_raw[i][:].rearrange("p j (m t) -> p m j t", t=PACK),
+                w_raw[i][:].rearrange("p j (m t) -> p m j t", t=PACK)[:, :, :, 2 * pair : 2 * pair + 2],
             )
-            codes = keep.tile([P, H], U32, name="w_codes%d" % i, align_bytes=64)
-            plane = keep.tile([P, H], U8, name="w_plane%d" % i, align_bytes=64)
+            codes = keep.tile([P, 2 * P], U32, name="w_codes%d%d" % (i, pair), align_bytes=64)
+            name = "w_plane%d%d" % (i, pair)
+            plane = turns.tile([P, 2 * P], U8, name=name, tag=name, align_bytes=64)
             nc.vector.quantize_mx(
                 out=codes[:].bitcast(FP8X4), scales=plane[:], in_=grouped[:].rearrange("p t m j -> p (t m j)")
             )
-            return codes, plane
+            weights[(i, pair)] = (codes, plane)
 
-        weights = [quantise_weight(0, nc.scalar.copy)]
-
-        x_codes = []
-        for half in range(S // BANK):
-            codes = turns.tile([P, BANK], U32, name="x_codes%d" % half, tag="x_turn%d" % half, align_bytes=64)
-            nc.vector.tensor_copy(codes[:], x_table[:].bitcast(U32).indirect(entries(offs_sb, half * BANK, BANK)))
-            x_codes.append(codes)
-
-        weights.append(quantise_weight(1, nc.vector.tensor_copy))
+        x_bytes = []
+        for half, tag in enumerate(("x_bytes", "w_grouped00")):
+            x_bytes.append(turns.tile([P, BANK], U8, name="x_bytes%d" % half, tag=tag, align_bytes=64))
+            nc.vector.tensor_copy(x_bytes[half][:], x_plane[:].indirect(entries(offs_sb, half * BANK, BANK)))
+            quantise_weight(0, half)
 
         windows = {}
         bank_turn = [0]
@@ -106,8 +106,8 @@ def tile_picked_hub_relu_po_kernel(
             return psum.tile(shape, F32, name=tag, tag=tag)
 
         def node_product(i, t, half):
-            codes, plane = weights[i]
-            cols = slice(t * P, (t + 1) * P)
+            codes, plane = weights[(i, t // 2)]
+            cols = slice(t % 2 * P, (t % 2 + 1) * P)
             nodes = slice(half * BANK, (half + 1) * BANK)
             if (i, t) not in windows:
                 windows[(i, t)] = keep.tile([P, S], F32, name="window%d_%d" % (i, t), align_bytes=64)
@@ -116,19 +116,22 @@ def tile_picked_hub_relu_po_kernel(
                 out=acc[:],
                 lhsT=codes[:, cols].bitcast(FP8X4),
                 lhsT_scale=plane[:, cols],
-                rhs=x_codes[half][:].bitcast(FP8X4),
-                rhs_scale=x_bytes[:, nodes],
+                rhs=x_codes[:, nodes].bitcast(FP8X4),
+                rhs_scale=x_bytes[half][:],
                 start=True,
                 stop=True,
             )
             nc.scalar.copy(windows[(i, t)][:, nodes], acc[:])
 
+        quantise_weight(1, 0, nc.vector.tensor_copy)
         for half in range(2):
             for t in range(2):
                 node_product(0, t, half)
-        for i, t in ((1, 0), (0, 2), (1, 1), (0, 3), (1, 2), (1, 3)):
+        for i, t in ((0, 2), (1, 0), (1, 1), (0, 3), (1, 2), (1, 3)):
             for half in range(2):
                 node_product(i, t, half)
+            if (i, t) == (1, 0):
+                quantise_weight(1, 1)
 
         w3_codes = keep.tile([P, H], I32, name="w3_codes", align_bytes=64)
         w3_bytes = keep.tile([P, H], U8, name="w3_bytes", align_bytes=64)
@@ -148,24 +151,28 @@ def tile_picked_hub_relu_po_kernel(
         out_rows = out_0.rearrange("(p t) n -> p t n", t=PACK)
         out_words = out_1[0].rearrange("p n r -> p (n r)").bitcast(I32)
 
-        tags = {}
+        tags = {("w", 1, 0): "w_grouped10", ("w", 1, 1): "w_grouped11"}
 
         def turn_tile(key, shape, dtype, after=None):
             tag = tags.pop(after) if after is not None else "turn_%s%d%d" % key
             tags[key] = tag
-            return turns.tile(shape, dtype, name=tag, tag=tag, align_bytes=64)
+            return turns.tile(shape, dtype, name="%s%d%d" % key, tag=tag, align_bytes=64)
 
-        def pick_sources(c, t, after=None):
-            n = CHUNKS[c]
-            picked[(c, t)] = turn_tile(("y", c, t), [P, n], F32, after)
-            nc.vector.tensor_copy(picked[(c, t)][:], windows[(0, t)][:].indirect(entries(src_sb, firsts[c], n)))
+        def pick_sources(chunks, tiles, after=None):
+            first = firsts[chunks[0]]
+            n = sum(CHUNKS[c] for c in chunks)
+            held = turn_tile(("y", chunks[0], tiles[0]), [P, len(tiles), n], F32, after)
+            for u, t in enumerate(tiles):
+                nc.vector.tensor_copy(held[:, u, :], windows[(0, t)][:].indirect(entries(src_sb, first, n)))
+                for c in chunks:
+                    picked[(c, t)] = held[:, u, firsts[c] - first : firsts[c] - first + CHUNKS[c]]
 
-        def add_targets(c, t):
+        def add_targets(c, t, after=None):
             n = CHUNKS[c]
             if c not in sums:
-                sums[c] = keep.tile([P, PACK, n], F32, name="sums%d" % c, align_bytes=64)
+                sums[c] = turn_tile(("s", c, 0), [P, PACK, n], F32, after)
             nc.vector.tensor_tensor(
-                sums[c][:, t, :], windows[(1, t)][:].indirect(entries(dst_sb, firsts[c], n)), picked[(c, t)][:], ADD
+                sums[c][:, t, :], windows[(1, t)][:].indirect(entries(dst_sb, firsts[c], n)), picked[(c, t)], ADD
             )
 
         def relu_round(c, on_vector=False):
@@ -186,7 +193,7 @@ def tile_picked_hub_relu_po_kernel(
             )
             z_ops[c] = (codes, plane)
 
-        def edge_product(c):
+        def edge_product(c, last=False):
             n = CHUNKS[c]
             codes, plane = z_ops[c]
             results[c] = keep.tile([P, PACK, n], F32, name="results%d" % c, align_bytes=64)
@@ -204,8 +211,12 @@ def tile_picked_hub_relu_po_kernel(
                         start=True,
                         stop=True,
                     )
+                if last:
+                    rounded[("o", c)] = turn_tile(("o", c, 0), [P, n, PACK], BF16)
+                    nc.vector.tensor_copy(rounded[("o", c)][:], acc[:].rearrange("p t n -> p n t"))
                 nc.scalar.copy(results[c][:, t0 : t0 + per_bank, :], acc[:])
-            nc.sync.dma_start(out=out_rows[:, :, firsts[c] : firsts[c] + n], in_=results[c][:])
+            queue = nc.scalar if last else nc.sync
+            queue.dma_start(out=out_rows[:, :, firsts[c] : firsts[c] + n], in_=results[c][:])
 
         def round_out(c, on_vector=False):
             n = CHUNKS[c]
@@ -225,70 +236,51 @@ def tile_picked_hub_relu_po_kernel(
             )
             nc.sync.dma_start(out=out_words[:, cols], in_=out_codes[:, cols].bitcast(I32))
 
-        for t in range(2):
-            pick_sources(0, t)
-            pick_sources(1, t)
-        add_targets(0, 0)
-        add_targets(1, 0)
-        pick_sources(0, 2)
-        add_targets(0, 1)
-        add_targets(1, 1)
-        pick_sources(0, 3)
         deal_w3()
+        pick_sources((0, 1), (0,))
+        pick_sources((2, 3, 4), (0,))
+        pick_sources((0, 1), (1,))
+        pick_sources((2, 3, 4), (1,))
+        pick_sources((0, 1), (2,), ("w", 1, 1))
+        add_targets(0, 0)
+        add_targets(0, 1)
+        pick_sources((0,), (3,))
         add_targets(0, 2)
         add_targets(0, 3)
         relu_round(0)
-        pick_sources(1, 2, ("y", 0, 2))
-        pick_sources(1, 3, ("y", 0, 3))
-        add_targets(1, 2)
-        add_targets(1, 3)
-        relu_round(1)
+        pick_sources((1, 2), (3,), ("y", 0, 3))
         quantise_z(0)
         edge_product(0)
-        pick_sources(2, 0, ("z", 0, 0))
-        pick_sources(2, 1, ("y", 1, 3))
-        add_targets(2, 0)
-        quantise_z(1)
         round_out(0)
+        for t in range(PACK):
+            add_targets(1, t, ("z", 0, 0))
+        relu_round(1)
+        pick_sources((2, 3, 4), (2,), ("y", 0, 2))
+        quantise_out(0)
+        quantise_z(1)
         edge_product(1)
         round_out(1)
-        pick_sources(2, 2, ("z", 1, 0))
-        add_targets(2, 1)
-        pick_sources(2, 3, ("y", 2, 0))
-        add_targets(2, 2)
-        add_targets(2, 3)
+        for t in range(PACK):
+            add_targets(2, t, ("s", 1, 0))
         relu_round(2)
-        quantise_out(0)
-        pick_sources(3, 0, ("o", 0, 0))
-        pick_sources(3, 1, ("y", 2, 2))
-        add_targets(3, 0)
-        pick_sources(3, 2, ("y", 2, 3))
-        add_targets(3, 1)
+        pick_sources((3, 4), (3,), ("y", 1, 3))
+        for t in range(PACK):
+            add_targets(3, t, ("z", 1, 0))
         quantise_z(2)
-        edge_product(2)
-        pick_sources(3, 3, ("z", 2, 0))
-        add_targets(3, 2)
-        add_targets(3, 3)
-        relu_round(3)
-        round_out(2)
         quantise_out(1)
-        pick_sources(4, 0, ("o", 1, 0))
-        pick_sources(4, 1, ("y", 3, 2))
-        add_targets(4, 0)
-        pick_sources(4, 2, ("y", 3, 3))
-        add_targets(4, 1)
+        relu_round(3)
+        edge_product(2)
         quantise_z(3)
         edge_product(3)
-        pick_sources(4, 3, ("z", 3, 0))
-        add_targets(4, 2)
-        add_targets(4, 3)
-        round_out(3)
+        round_out(2)
+        for t in range(PACK):
+            add_targets(4, t, ("z", 3, 0))
         relu_round(4, True)
-        quantise_out(2)
         quantise_z(4)
-        edge_product(4)
+        round_out(3, True)
         quantise_out(3)
-        round_out(4, True)
+        quantise_out(2)
+        edge_product(4, True)
         quantise_out(4)
         for q in range(4):
             queue = nc.scalar if q % 2 else nc.sync

@@ -29,8 +29,8 @@ def load_scale_rows(queue, plane, scales):
 
 def interleaved(planes, words):
     return (
-        words.rearrange("p (c i) t -> p c t i", i=4),
-        planes.rearrange("p t (c i) -> p c t i", i=4),
+        words.rearrange("p (c i) t -> p c t i", i=2),
+        planes.rearrange("p t (c i) -> p c t i", i=2),
     )
 
 
@@ -46,7 +46,7 @@ def tile_picked_hub_relu_po_kernel(
         offs_sb = keep.tile([P, S // LIST_ROWS], U16, name="offs_sb")
         src_sb = keep.tile([P, S // LIST_ROWS], U16, name="src_sb")
         dst_sb = keep.tile([P, S // LIST_ROWS], U16, name="dst_sb")
-        x_table = keep.tile([P, T], I32, name="x_table", align_bytes=64)
+        x_table = turns.tile([P, T], I32, name="x_table", tag="x_table", align_bytes=64)
         x_plane = turns.tile([P, T], U8, name="x_plane", tag="x_turn0", align_bytes=64)
         w_raw = [keep.tile([P, PACK, H], F32, name="w_raw%d" % i, align_bytes=64) for i in range(2)]
         warm = turns.tile([P, 8], F32, name="warm", tag="warm", align_bytes=64)
@@ -58,9 +58,9 @@ def tile_picked_hub_relu_po_kernel(
         nc.scalar.activation(warm_out[:], warm[:], RELU)
         nc.sync.dma_start(offs_sb[:], offs)
         nc.sync.dma_start(src_sb[:], src)
-        nc.sync.dma_start(out=x_table[:], in_=x_words[0].rearrange("p n r -> p (n r)").bitcast(I32))
-        nc.sync.dma_start(out=w_raw[0][:], in_=w1.rearrange("(p j) c -> p j c", j=PACK))
         nc.sync.dma_start(dst_sb[:], dst)
+        nc.sync.dma_start(out=w_raw[0][:], in_=w1.rearrange("(p j) c -> p j c", j=PACK))
+        nc.sync.dma_start(out=x_table[:], in_=x_words[0].rearrange("p n r -> p (n r)").bitcast(I32))
         nc.sync.dma_start(out=w_raw[1][:], in_=w2.rearrange("(p j) c -> p j c", j=PACK))
         w3_table = turns.tile([P, H], I32, name="w3_table", tag="warm_out", align_bytes=64)
         nc.sync.dma_start(out=w3_table[:], in_=w3_words[0].rearrange("p n r -> p (n r)").bitcast(I32))
@@ -71,31 +71,34 @@ def tile_picked_hub_relu_po_kernel(
         def entries(lst, first, count):
             return lst[:, first // LIST_ROWS : (first + count) // LIST_ROWS]
 
-        x_codes = keep.tile([P, S], U32, name="x_codes", align_bytes=64)
-        nc.vector.tensor_copy(x_codes[:], x_table[:].bitcast(U32).indirect(offs_sb[:]))
+        x_bytes = keep.tile([P, S], U8, name="x_bytes", align_bytes=64)
+        nc.vector.tensor_copy(x_bytes[:], x_plane[:].indirect(offs_sb[:]))
 
         weights = {}
 
-        def quantise_weight(i, pair, copy=nc.scalar.copy):
+        def quantise_weight(i, pair, copy=nc.scalar.copy, tag=None):
             name = "w_grouped%d%d" % (i, pair)
-            grouped = turns.tile([P, 2, P, PACK], BF16, name=name, tag=name, align_bytes=64)
+            grouped = turns.tile([P, 2, P, PACK], BF16, name=name, tag=tag or name, align_bytes=64)
             copy(
                 grouped[:].rearrange("p t m j -> p m j t"),
                 w_raw[i][:].rearrange("p j (m t) -> p m j t", t=PACK)[:, :, :, 2 * pair : 2 * pair + 2],
             )
-            codes = keep.tile([P, 2 * P], U32, name="w_codes%d%d" % (i, pair), align_bytes=64)
+            name = "w_codes%d%d" % (i, pair)
+            codes = turns.tile([P, 2 * P], U32, name=name, tag=name, align_bytes=64)
             name = "w_plane%d%d" % (i, pair)
-            plane = turns.tile([P, 2 * P], U8, name=name, tag=name, align_bytes=64)
+            plane = turns.tile([P, 2 * P], U8, name=name, tag="x_turn0" if (i, pair) == (0, 0) else name, align_bytes=64)
             nc.vector.quantize_mx(
                 out=codes[:].bitcast(FP8X4), scales=plane[:], in_=grouped[:].rearrange("p t m j -> p (t m j)")
             )
             weights[(i, pair)] = (codes, plane)
 
-        x_bytes = []
-        for half, tag in enumerate(("x_bytes", "w_grouped00")):
-            x_bytes.append(turns.tile([P, BANK], U8, name="x_bytes%d" % half, tag=tag, align_bytes=64))
-            nc.vector.tensor_copy(x_bytes[half][:], x_plane[:].indirect(entries(offs_sb, half * BANK, BANK)))
-            quantise_weight(0, half)
+        quantise_weight(0, 0)
+        x_codes = turns.tile([P, S], U32, name="x_codes", tag="w_grouped00", align_bytes=64)
+        for half in range(S // BANK):
+            nodes = slice(half * BANK, (half + 1) * BANK)
+            nc.vector.tensor_copy(x_codes[:, nodes], x_table[:].bitcast(U32).indirect(entries(offs_sb, half * BANK, BANK)))
+            if half == 0:
+                quantise_weight(0, 1)
 
         windows = {}
         bank_turn = [0]
@@ -117,31 +120,31 @@ def tile_picked_hub_relu_po_kernel(
                 lhsT=codes[:, cols].bitcast(FP8X4),
                 lhsT_scale=plane[:, cols],
                 rhs=x_codes[:, nodes].bitcast(FP8X4),
-                rhs_scale=x_bytes[half][:],
+                rhs_scale=x_bytes[:, nodes],
                 start=True,
                 stop=True,
             )
             nc.scalar.copy(windows[(i, t)][:, nodes], acc[:])
 
-        quantise_weight(1, 0, nc.vector.tensor_copy)
+        quantise_weight(1, 0, nc.vector.tensor_copy, "x_table")
         for half in range(2):
             for t in range(2):
                 node_product(0, t, half)
+        quantise_weight(1, 1, nc.scalar.copy, "w_codes00")
         for i, t in ((0, 2), (1, 0), (1, 1), (0, 3), (1, 2), (1, 3)):
             for half in range(2):
                 node_product(i, t, half)
-            if (i, t) == (1, 0):
-                quantise_weight(1, 1)
 
-        w3_codes = keep.tile([P, H], I32, name="w3_codes", align_bytes=64)
-        w3_bytes = keep.tile([P, H], U8, name="w3_bytes", align_bytes=64)
+        w3_codes = turns.tile([P, H], I32, name="w3_codes", tag="x_table", align_bytes=64)
+        w3_bytes = turns.tile([P, H], U8, name="w3_bytes", tag="w_codes00", align_bytes=64)
 
         def deal_w3():
             nc.vector.tensor_copy(
-                w3_codes[:].rearrange("p (t m) -> p m t", t=PACK), w3_table[:].rearrange("p (m t) -> p m t", t=PACK)
+                w3_codes[:].rearrange("p (t g i) -> p g t i", t=PACK, i=4),
+                w3_table[:].rearrange("p (g i t) -> p g t i", t=PACK, i=4),
             )
             nc.vector.tensor_copy(
-                w3_bytes[:].rearrange("p (t m) -> p m t", t=PACK), w3_plane[:].rearrange("p (m t) -> p m t", t=PACK)
+                w3_bytes[:].rearrange("p (t m) -> p t m", t=PACK), w3_plane[:].rearrange("p (m t) -> p t m", t=PACK)
             )
 
         firsts = [sum(CHUNKS[:c]) for c in range(len(CHUNKS))]
@@ -151,7 +154,7 @@ def tile_picked_hub_relu_po_kernel(
         out_rows = out_0.rearrange("(p t) n -> p t n", t=PACK)
         out_words = out_1[0].rearrange("p n r -> p (n r)").bitcast(I32)
 
-        tags = {("w", 1, 0): "w_grouped10", ("w", 1, 1): "w_grouped11"}
+        tags = {}
 
         def turn_tile(key, shape, dtype, after=None):
             tag = tags.pop(after) if after is not None else "turn_%s%d%d" % key
@@ -213,7 +216,7 @@ def tile_picked_hub_relu_po_kernel(
                     )
                 if last:
                     rounded[("o", c)] = turn_tile(("o", c, 0), [P, n, PACK], BF16)
-                    nc.vector.tensor_copy(rounded[("o", c)][:], acc[:].rearrange("p t n -> p n t"))
+                    nc.vector.tensor_copy(*interleaved(acc[:], rounded[("o", c)][:]))
                 nc.scalar.copy(results[c][:, t0 : t0 + per_bank, :], acc[:])
             queue = nc.scalar if last else nc.sync
             queue.dma_start(out=out_rows[:, :, firsts[c] : firsts[c] + n], in_=results[c][:])
@@ -241,7 +244,7 @@ def tile_picked_hub_relu_po_kernel(
         pick_sources((2, 3, 4), (0,))
         pick_sources((0, 1), (1,))
         pick_sources((2, 3, 4), (1,))
-        pick_sources((0, 1), (2,), ("w", 1, 1))
+        pick_sources((0, 1), (2,))
         add_targets(0, 0)
         add_targets(0, 1)
         pick_sources((0,), (3,))

@@ -17,21 +17,41 @@ RELU = mybir.ActivationFunctionType.Relu
 
 P = 128
 PACK = 4
+PAIR = 2
+QUADRANTS = 4
 BANK = 512
+BANKS = 8
 LIST_ROWS = 16
+LINE_COLUMNS = 2
+LINE_WORDS = 4
+ALIGN = 64
+SOURCE, TARGET = 0, 1
 CHUNKS = (256, 256, 256, 128, 128)
+FIRSTS = [sum(CHUNKS[:c]) for c in range(len(CHUNKS))]
+LAST = len(CHUNKS) - 1
 
 
-def load_scale_rows(queue, plane, scales):
-    for q in range(4):
-        queue.dma_start(out=plane[32 * q : 32 * q + 4, :].bitcast(I32), in_=scales[0, 4 * q : 4 * q + 4, :].bitcast(I32))
+def scale_rows(plane, scales, q):
+    return plane[32 * q : 32 * q + 4, :].bitcast(I32), scales[0, 4 * q : 4 * q + 4, :].bitcast(I32)
 
 
-def interleaved(planes, words):
+def as_words(packed):
+    return packed[0].rearrange("p n j -> p (n j)").bitcast(I32)
+
+
+def interleaved(by_tile, by_column):
     return (
-        words.rearrange("p (c i) t -> p c t i", i=2),
-        planes.rearrange("p t (c i) -> p c t i", i=2),
+        by_column.rearrange("p (g i) t -> p g t i", i=LINE_COLUMNS),
+        by_tile.rearrange("p t (g i) -> p g t i", i=LINE_COLUMNS),
     )
+
+
+def entries(offsets, first, count):
+    return offsets[:, first // LIST_ROWS : (first + count) // LIST_ROWS]
+
+
+def span(chunks):
+    return FIRSTS[chunks[0]], sum(CHUNKS[c] for c in chunks)
 
 
 def tile_picked_hub_relu_po_kernel(
@@ -43,77 +63,74 @@ def tile_picked_hub_relu_po_kernel(
         turns = ctx.enter_context(tc.tile_pool(name="turns", bufs=1))
         psum = ctx.enter_context(tc.psum_pool(name="psum", bufs=1))
 
+        tags = {}
+
+        def turn_tile(name, shape, dtype, after=None):
+            tags[name] = name if after is None else tags.pop(after)
+            return turns.tile(shape, dtype, name=name, tag=tags[name], align_bytes=ALIGN)
+
+        banks_taken = []
+
+        def next_bank(shape):
+            name = "bank%d" % (len(banks_taken) % BANKS)
+            banks_taken.append(name)
+            return psum.tile(shape, F32, name=name, tag=name)
+
         offs_sb = keep.tile([P, S // LIST_ROWS], U16, name="offs_sb")
         src_sb = keep.tile([P, S // LIST_ROWS], U16, name="src_sb")
         dst_sb = keep.tile([P, S // LIST_ROWS], U16, name="dst_sb")
-        x_table = turns.tile([P, T], I32, name="x_table", tag="x_table", align_bytes=64)
-        x_plane = turns.tile([P, T], U8, name="x_plane", tag="x_turn0", align_bytes=64)
-        w_raw = [keep.tile([P, PACK, H], F32, name="w_raw%d" % i, align_bytes=64) for i in range(2)]
-        warm = turns.tile([P, 8], F32, name="warm", tag="warm", align_bytes=64)
-        warm_out = turns.tile([P, 8], F32, name="warm_out", tag="warm_out", align_bytes=64)
+        x_table = turn_tile("x_table", [P, T], I32)
+        x_plane = turn_tile("x_plane", [P, T], U8)
+        w_raw = [turn_tile("w_raw%d" % side, [P, PACK, H], F32) for side in (SOURCE, TARGET)]
+        w3_table = keep.tile([P, H], I32, name="w3_table", align_bytes=ALIGN)
+        w3_plane = keep.tile([P, H], U8, name="w3_plane", align_bytes=ALIGN)
 
         nc.vector.memset(x_plane[:].bitcast(I32), 0)
-        nc.vector.memset(warm[:], 0.0)
-        load_scale_rows(nc.scalar, x_plane, x_scales)
-        nc.scalar.activation(warm_out[:], warm[:], RELU)
+        for q in range(QUADRANTS):
+            nc.scalar.dma_start(*scale_rows(x_plane, x_scales, q))
         nc.sync.dma_start(offs_sb[:], offs)
         nc.sync.dma_start(src_sb[:], src)
         nc.sync.dma_start(dst_sb[:], dst)
-        nc.sync.dma_start(out=w_raw[0][:], in_=w1.rearrange("(p j) c -> p j c", j=PACK))
-        nc.sync.dma_start(out=x_table[:], in_=x_words[0].rearrange("p n r -> p (n r)").bitcast(I32))
-        nc.sync.dma_start(out=w_raw[1][:], in_=w2.rearrange("(p j) c -> p j c", j=PACK))
-        w3_table = turns.tile([P, H], I32, name="w3_table", tag="warm_out", align_bytes=64)
-        nc.sync.dma_start(out=w3_table[:], in_=w3_words[0].rearrange("p n r -> p (n r)").bitcast(I32))
-        w3_plane = turns.tile([P, H], U8, name="w3_plane", tag="warm", align_bytes=64)
+        nc.sync.dma_start(w_raw[SOURCE][:], w1.rearrange("(p j) c -> p j c", j=PACK))
+        nc.sync.dma_start(x_table[:], as_words(x_words))
+        nc.sync.dma_start(w_raw[TARGET][:], w2.rearrange("(p j) c -> p j c", j=PACK))
+        nc.sync.dma_start(w3_table[:], as_words(w3_words))
         nc.vector.memset(w3_plane[:].bitcast(I32), 0)
-        load_scale_rows(nc.sync, w3_plane, w3_scales)
-
-        def entries(lst, first, count):
-            return lst[:, first // LIST_ROWS : (first + count) // LIST_ROWS]
-
-        x_bytes = keep.tile([P, S], U8, name="x_bytes", align_bytes=64)
-        nc.vector.tensor_copy(x_bytes[:], x_plane[:].indirect(offs_sb[:]))
+        for q in range(QUADRANTS):
+            nc.sync.dma_start(*scale_rows(w3_plane, w3_scales, q))
 
         weights = {}
 
-        def quantise_weight(i, pair, copy=nc.scalar.copy, tag=None):
-            name = "w_grouped%d%d" % (i, pair)
-            grouped = turns.tile([P, 2, P, PACK], BF16, name=name, tag=tag or name, align_bytes=64)
+        def quantise_weight(side, pair, copy, rounded_after=None, codes_after=None, plane_after=None):
+            rounded = turn_tile("w_rounded%d%d" % (side, pair), [P, PAIR, P, PACK], BF16, rounded_after)
             copy(
-                grouped[:].rearrange("p t m j -> p m j t"),
-                w_raw[i][:].rearrange("p j (m t) -> p m j t", t=PACK)[:, :, :, 2 * pair : 2 * pair + 2],
+                rounded[:].rearrange("p t m j -> p m j t"),
+                w_raw[side][:].rearrange("p j (m t) -> p m j t", t=PACK)[:, :, :, PAIR * pair : PAIR * (pair + 1)],
             )
-            name = "w_codes%d%d" % (i, pair)
-            codes = turns.tile([P, 2 * P], U32, name=name, tag=name, align_bytes=64)
-            name = "w_plane%d%d" % (i, pair)
-            plane = turns.tile([P, 2 * P], U8, name=name, tag="x_turn0" if (i, pair) == (0, 0) else name, align_bytes=64)
+            codes = turn_tile("w_codes%d%d" % (side, pair), [P, PAIR * P], U32, codes_after)
+            plane = turn_tile("w_plane%d%d" % (side, pair), [P, PAIR * P], U8, plane_after)
             nc.vector.quantize_mx(
-                out=codes[:].bitcast(FP8X4), scales=plane[:], in_=grouped[:].rearrange("p t m j -> p (t m j)")
+                out=codes[:].bitcast(FP8X4), scales=plane[:], in_=rounded[:].rearrange("p t m j -> p (t m j)")
             )
-            weights[(i, pair)] = (codes, plane)
+            weights[(side, pair)] = (codes, plane)
 
-        quantise_weight(0, 0)
-        x_codes = turns.tile([P, S], U32, name="x_codes", tag="w_grouped00", align_bytes=64)
-        for half in range(S // BANK):
-            nodes = slice(half * BANK, (half + 1) * BANK)
-            nc.vector.tensor_copy(x_codes[:, nodes], x_table[:].bitcast(U32).indirect(entries(offs_sb, half * BANK, BANK)))
-            if half == 0:
-                quantise_weight(0, 1)
+        x_bytes = keep.tile([P, S], U8, name="x_bytes", align_bytes=ALIGN)
+        nc.vector.tensor_copy(x_bytes[:], x_plane[:].indirect(offs_sb[:]))
+        quantise_weight(SOURCE, 0, nc.scalar.copy, plane_after="x_plane")
+        x_codes = turn_tile("x_codes", [P, S], U32, "w_rounded00")
+        for first in range(0, S, BANK):
+            nc.vector.tensor_copy(
+                x_codes[:, first : first + BANK], x_table[:].bitcast(U32).indirect(entries(offs_sb, first, BANK))
+            )
 
         windows = {}
-        bank_turn = [0]
 
-        def next_bank(shape):
-            tag = "bank%d" % (bank_turn[0] % 8)
-            bank_turn[0] = bank_turn[0] + 1
-            return psum.tile(shape, F32, name=tag, tag=tag)
-
-        def node_product(i, t, half):
-            codes, plane = weights[(i, t // 2)]
-            cols = slice(t % 2 * P, (t % 2 + 1) * P)
+        def node_product(side, t, half):
+            codes, plane = weights[(side, t // PAIR)]
+            cols = slice(t % PAIR * P, (t % PAIR + 1) * P)
             nodes = slice(half * BANK, (half + 1) * BANK)
-            if (i, t) not in windows:
-                windows[(i, t)] = keep.tile([P, S], F32, name="window%d_%d" % (i, t), align_bytes=64)
+            if (side, t) not in windows:
+                windows[(side, t)] = keep.tile([P, S], F32, name="window%d%d" % (side, t), align_bytes=ALIGN)
             acc = next_bank([P, BANK])
             nc.tensor.matmul_mx(
                 out=acc[:],
@@ -124,82 +141,77 @@ def tile_picked_hub_relu_po_kernel(
                 start=True,
                 stop=True,
             )
-            nc.scalar.copy(windows[(i, t)][:, nodes], acc[:])
+            nc.scalar.copy(windows[(side, t)][:, nodes], acc[:])
 
-        quantise_weight(1, 0, nc.vector.tensor_copy, "x_table")
-        for half in range(2):
-            for t in range(2):
-                node_product(0, t, half)
-        quantise_weight(1, 1, nc.scalar.copy, "w_codes00")
-        for i, t in ((0, 2), (1, 0), (1, 1), (0, 3), (1, 2), (1, 3)):
-            for half in range(2):
-                node_product(i, t, half)
+        quantise_weight(TARGET, 0, nc.vector.tensor_copy)
+        quantise_weight(SOURCE, 1, nc.scalar.copy, codes_after="x_table")
+        for half in range(S // BANK):
+            for t in range(PAIR):
+                node_product(SOURCE, t, half)
+        quantise_weight(TARGET, 1, nc.scalar.copy, rounded_after="w_codes00")
+        for side, t in ((SOURCE, 2), (TARGET, 0), (TARGET, 1), (SOURCE, 3), (TARGET, 2), (TARGET, 3)):
+            for half in range(S // BANK):
+                node_product(side, t, half)
 
-        w3_codes = turns.tile([P, H], I32, name="w3_codes", tag="x_table", align_bytes=64)
-        w3_bytes = turns.tile([P, H], U8, name="w3_bytes", tag="w_codes00", align_bytes=64)
+        w3_codes = turn_tile("w3_codes", [P, H], I32, "w_raw1")
+        w3_bytes = turn_tile("w3_bytes", [P, H], U8, "w_plane00")
 
         def deal_w3():
             nc.vector.tensor_copy(
-                w3_codes[:].rearrange("p (t g i) -> p g t i", t=PACK, i=4),
-                w3_table[:].rearrange("p (g i t) -> p g t i", t=PACK, i=4),
+                w3_codes[:].rearrange("p (t g i) -> p g t i", t=PACK, i=LINE_WORDS),
+                w3_table[:].rearrange("p (g i t) -> p g t i", t=PACK, i=LINE_WORDS),
             )
             nc.vector.tensor_copy(
                 w3_bytes[:].rearrange("p (t m) -> p t m", t=PACK), w3_plane[:].rearrange("p (m t) -> p t m", t=PACK)
             )
 
-        firsts = [sum(CHUNKS[:c]) for c in range(len(CHUNKS))]
-        picked, sums, rounded, results, z_ops = {}, {}, {}, {}, {}
-        out_codes = keep.tile([P, S], U32, name="out_codes", align_bytes=64)
-        out_plane = keep.tile([P, S], U8, name="out_plane", align_bytes=64)
+        sources, sums, z_rounded, z_packed, results = {}, {}, {}, {}, {}
+        out_codes = keep.tile([P, S], U32, name="out_codes", align_bytes=ALIGN)
+        out_plane = keep.tile([P, S], U8, name="out_plane", align_bytes=ALIGN)
         out_rows = out_0.rearrange("(p t) n -> p t n", t=PACK)
-        out_words = out_1[0].rearrange("p n r -> p (n r)").bitcast(I32)
+        out_groups = [(c,) for c in range(LAST - 1)] + [(LAST - 1, LAST)]
+        out_rounded = {}
+        for group in out_groups:
+            first, count = span(group)
+            shared = keep.tile([P, count, PACK], BF16, name="out_rounded%d" % group[0], align_bytes=ALIGN)
+            out_rounded[group] = shared[:]
+            for c in group:
+                out_rounded[c] = shared[:, FIRSTS[c] - first : FIRSTS[c] - first + CHUNKS[c], :]
 
-        tags = {}
+        def gather_sources(chunks, t, after=None):
+            first, count = span(chunks)
+            picked = turn_tile("sources%d%d" % (chunks[0], t), [P, count], F32, after)
+            nc.vector.tensor_copy(picked[:], windows[(SOURCE, t)][:].indirect(entries(src_sb, first, count)))
+            for c in chunks:
+                sources[(c, t)] = picked[:, FIRSTS[c] - first : FIRSTS[c] - first + CHUNKS[c]]
 
-        def turn_tile(key, shape, dtype, after=None):
-            tag = tags.pop(after) if after is not None else "turn_%s%d%d" % key
-            tags[key] = tag
-            return turns.tile(shape, dtype, name="%s%d%d" % key, tag=tag, align_bytes=64)
-
-        def pick_sources(chunks, tiles, after=None):
-            first = firsts[chunks[0]]
-            n = sum(CHUNKS[c] for c in chunks)
-            held = turn_tile(("y", chunks[0], tiles[0]), [P, len(tiles), n], F32, after)
-            for u, t in enumerate(tiles):
-                nc.vector.tensor_copy(held[:, u, :], windows[(0, t)][:].indirect(entries(src_sb, first, n)))
-                for c in chunks:
-                    picked[(c, t)] = held[:, u, firsts[c] - first : firsts[c] - first + CHUNKS[c]]
-
-        def add_targets(c, t, after=None):
-            n = CHUNKS[c]
+        def add_targets(c, tiles, after=None):
             if c not in sums:
-                sums[c] = turn_tile(("s", c, 0), [P, PACK, n], F32, after)
-            nc.vector.tensor_tensor(
-                sums[c][:, t, :], windows[(1, t)][:].indirect(entries(dst_sb, firsts[c], n)), picked[(c, t)], ADD
-            )
+                sums[c] = turn_tile("sums%d" % c, [P, PACK, CHUNKS[c]], F32, after)
+            for t in tiles:
+                looked_up = windows[(TARGET, t)][:].indirect(entries(dst_sb, FIRSTS[c], CHUNKS[c]))
+                nc.vector.tensor_tensor(sums[c][:, t, :], looked_up, sources[(c, t)], ADD)
 
-        def relu_round(c, on_vector=False):
-            n = CHUNKS[c]
-            rounded[("z", c)] = turn_tile(("z", c, 0), [P, n, PACK], BF16)
-            words, planes = interleaved(sums[c][:], rounded[("z", c)][:])
-            if on_vector:
-                nc.vector.tensor_scalar_max(words, planes, 0.0)
+        def relu_round(c):
+            z_rounded[c] = turn_tile("z_rounded%d" % c, [P, CHUNKS[c], PACK], BF16)
+            by_column, by_tile = interleaved(sums[c][:], z_rounded[c][:])
+            if c == LAST:
+                nc.vector.tensor_scalar_max(by_column, by_tile, 0.0)
             else:
-                nc.scalar.activation(words, planes, RELU)
+                nc.scalar.activation(by_column, by_tile, RELU)
 
         def quantise_z(c):
-            n = CHUNKS[c]
-            codes = keep.tile([P, n], U32, name="z_codes%d" % c, align_bytes=64)
-            plane = keep.tile([P, n], U8, name="z_plane%d" % c, align_bytes=64)
+            codes = keep.tile([P, CHUNKS[c]], U32, name="z_codes%d" % c, align_bytes=ALIGN)
+            plane = keep.tile([P, CHUNKS[c]], U8, name="z_plane%d" % c, align_bytes=ALIGN)
             nc.vector.quantize_mx(
-                out=codes[:].bitcast(FP8X4), scales=plane[:], in_=rounded[("z", c)][:].rearrange("p n t -> p (n t)")
+                out=codes[:].bitcast(FP8X4), scales=plane[:], in_=z_rounded[c][:].rearrange("p n t -> p (n t)")
             )
-            z_ops[c] = (codes, plane)
+            z_packed[c] = (codes, plane)
 
-        def edge_product(c, last=False):
+        def edge_product(c):
             n = CHUNKS[c]
-            codes, plane = z_ops[c]
-            results[c] = keep.tile([P, PACK, n], F32, name="results%d" % c, align_bytes=64)
+            codes, plane = z_packed[c]
+            results[c] = keep.tile([P, PACK, n], F32, name="results%d" % c, align_bytes=ALIGN)
             per_bank = BANK // n
             for t0 in range(0, PACK, per_bank):
                 acc = next_bank([P, per_bank, n])
@@ -214,77 +226,70 @@ def tile_picked_hub_relu_po_kernel(
                         start=True,
                         stop=True,
                     )
-                if last:
-                    rounded[("o", c)] = turn_tile(("o", c, 0), [P, n, PACK], BF16)
-                    nc.vector.tensor_copy(*interleaved(acc[:], rounded[("o", c)][:]))
+                if c == LAST:
+                    nc.vector.tensor_copy(*interleaved(acc[:], out_rounded[c]))
                 nc.scalar.copy(results[c][:, t0 : t0 + per_bank, :], acc[:])
-            queue = nc.scalar if last else nc.sync
-            queue.dma_start(out=out_rows[:, :, firsts[c] : firsts[c] + n], in_=results[c][:])
+            queue = nc.scalar if c == LAST else nc.sync
+            queue.dma_start(out_rows[:, :, FIRSTS[c] : FIRSTS[c] + n], results[c][:])
 
-        def round_out(c, on_vector=False):
-            n = CHUNKS[c]
-            rounded[("o", c)] = turn_tile(("o", c, 0), [P, n, PACK], BF16)
-            words, planes = interleaved(results[c][:], rounded[("o", c)][:])
-            if on_vector:
-                nc.vector.tensor_copy(words, planes)
-            else:
-                nc.scalar.copy(words, planes)
+        def round_out(c, copy):
+            copy(*interleaved(results[c][:], out_rounded[c]))
 
-        def quantise_out(c):
-            cols = slice(firsts[c], firsts[c] + CHUNKS[c])
+        def quantise_out(group):
+            first, count = span(group)
+            edges = slice(first, first + count)
             nc.vector.quantize_mx(
-                out=out_codes[:, cols].bitcast(FP8X4),
-                scales=out_plane[:, cols],
-                in_=rounded[("o", c)][:].rearrange("p n t -> p (n t)"),
+                out=out_codes[:, edges].bitcast(FP8X4),
+                scales=out_plane[:, edges],
+                in_=out_rounded[group].rearrange("p n t -> p (n t)"),
             )
-            nc.sync.dma_start(out=out_words[:, cols], in_=out_codes[:, cols].bitcast(I32))
+            nc.sync.dma_start(as_words(out_1)[:, edges], out_codes[:, edges].bitcast(I32))
 
+        every_tile = range(PACK)
+
+        for t in range(PAIR):
+            gather_sources((0, 1), t)
+            gather_sources((2, 3, 4), t)
         deal_w3()
-        pick_sources((0, 1), (0,))
-        pick_sources((2, 3, 4), (0,))
-        pick_sources((0, 1), (1,))
-        pick_sources((2, 3, 4), (1,))
-        pick_sources((0, 1), (2,))
-        add_targets(0, 0)
-        add_targets(0, 1)
-        pick_sources((0,), (3,))
-        add_targets(0, 2)
-        add_targets(0, 3)
+        gather_sources((0, 1), 2)
+        add_targets(0, (0, 1))
+        gather_sources((0,), 3)
+        add_targets(0, (2, 3))
+
         relu_round(0)
-        pick_sources((1, 2), (3,), ("y", 0, 3))
+        gather_sources((1, 2), 3, after="sources03")
         quantise_z(0)
         edge_product(0)
-        round_out(0)
-        for t in range(PACK):
-            add_targets(1, t, ("z", 0, 0))
+        round_out(0, nc.scalar.copy)
+        add_targets(1, every_tile, after="sums0")
+
         relu_round(1)
-        pick_sources((2, 3, 4), (2,), ("y", 0, 2))
-        quantise_out(0)
+        gather_sources((2, 3, 4), 2, after="sources02")
+        quantise_out(out_groups[0])
         quantise_z(1)
         edge_product(1)
-        round_out(1)
-        for t in range(PACK):
-            add_targets(2, t, ("s", 1, 0))
+        round_out(1, nc.scalar.copy)
+        add_targets(2, every_tile, after="sums1")
+
         relu_round(2)
-        pick_sources((3, 4), (3,), ("y", 1, 3))
-        for t in range(PACK):
-            add_targets(3, t, ("z", 1, 0))
+        gather_sources((3, 4), 3, after="sources13")
+        add_targets(3, every_tile, after="z_rounded1")
         quantise_z(2)
-        quantise_out(1)
+        quantise_out(out_groups[1])
         relu_round(3)
         edge_product(2)
         quantise_z(3)
         edge_product(3)
-        round_out(2)
-        for t in range(PACK):
-            add_targets(4, t, ("z", 3, 0))
-        relu_round(4, True)
-        quantise_z(4)
-        round_out(3, True)
-        quantise_out(3)
-        quantise_out(2)
-        edge_product(4, True)
-        quantise_out(4)
-        for q in range(4):
+        round_out(2, nc.scalar.copy)
+        add_targets(LAST, every_tile, after="sums3")
+
+        relu_round(LAST)
+        quantise_z(LAST)
+        round_out(3, nc.vector.tensor_copy)
+        quantise_out(out_groups[2])
+        edge_product(LAST)
+        quantise_out(out_groups[3])
+        for q in range(QUADRANTS):
+            in_plane, in_dram = scale_rows(out_plane, out_2, q)
             queue = nc.scalar if q % 2 else nc.sync
-            queue.dma_start(out=out_2[0, 4 * q : 4 * q + 4, :].bitcast(I32), in_=out_plane[32 * q : 32 * q + 4, :].bitcast(I32))
+            queue.dma_start(in_dram, in_plane)

@@ -12,6 +12,7 @@ U32 = mybir.dt.uint32
 U16 = mybir.dt.uint16
 U8 = mybir.dt.uint8
 FP8X4 = mybir.dt.float8_e4m3fn_x4
+WIDTH = {F32: 4, I32: 4, U32: 4, BF16: 2, U8: 1}
 ADD = mybir.AluOpType.add
 RELU = mybir.ActivationFunctionType.Relu
 
@@ -21,6 +22,7 @@ PAIR = 2
 QUADRANTS = 4
 BANK = 512
 BANKS = 8
+PART = BANK // PACK
 LIST_ROWS = 16
 LINE_COLUMNS = 2
 LINE_WORDS = 4
@@ -59,15 +61,23 @@ def tile_picked_hub_relu_po_kernel(
 ):
     nc = tc.nc
     with ExitStack() as ctx:
-        keep = ctx.enter_context(tc.tile_pool(name="keep", bufs=1))
-        turns = ctx.enter_context(tc.tile_pool(name="turns", bufs=1))
+        lists = ctx.enter_context(tc.tile_pool(name="lists", bufs=1))
+        placed = ctx.enter_context(tc.tile_pool(name="placed", bufs=1))
         psum = ctx.enter_context(tc.psum_pool(name="psum", bufs=1))
 
-        tags = {}
+        starts = {}
+        used = [0]
 
-        def turn_tile(name, shape, dtype, after=None):
-            tags[name] = name if after is None else tags.pop(after)
-            return turns.tile(shape, dtype, name=name, tag=tags[name], align_bytes=ALIGN)
+        def place(name, shape, dtype, over=None, skip=0, lead=0, room=0):
+            if over is None:
+                starts[name] = used[0] + lead
+                size = WIDTH[dtype]
+                for extent in shape[1:]:
+                    size = size * extent
+                used[0] = starts[name] + max(room, -(-size // ALIGN) * ALIGN)
+            else:
+                starts[name] = starts[over] + skip
+            return placed.tile(shape, dtype, name=name, tag=name, align_bytes=ALIGN, offset=starts[name])
 
         banks_taken = []
 
@@ -76,87 +86,86 @@ def tile_picked_hub_relu_po_kernel(
             banks_taken.append(name)
             return psum.tile(shape, F32, name=name, tag=name)
 
-        offs_sb = keep.tile([P, S // LIST_ROWS], U16, name="offs_sb")
-        src_sb = keep.tile([P, S // LIST_ROWS], U16, name="src_sb")
-        dst_sb = keep.tile([P, S // LIST_ROWS], U16, name="dst_sb")
-        x_table = turn_tile("x_table", [P, T], I32)
-        x_plane = turn_tile("x_plane", [P, T], U8)
-        w_raw = [turn_tile("w_raw%d" % side, [P, PACK, H], F32) for side in (SOURCE, TARGET)]
-        w3_table = keep.tile([P, H], I32, name="w3_table", align_bytes=ALIGN)
-        w3_plane = keep.tile([P, H], U8, name="w3_plane", align_bytes=ALIGN)
+        offs_sb = lists.tile([P, S // LIST_ROWS], U16, name="offs_sb")
+        src_sb = lists.tile([P, S // LIST_ROWS], U16, name="src_sb")
+        dst_sb = lists.tile([P, S // LIST_ROWS], U16, name="dst_sb")
+        x_table = place("x_table", [P, T], I32)
+        x_plane = place("x_plane", [P, T], U8)
+        w_raw = [place("w_raw%d" % side, [P, PACK, H], F32) for side in (SOURCE, TARGET)]
+        w3_table = place("w3_table", [P, H], I32)
+        w3_plane = place("w3_plane", [P, H], U8)
 
         nc.vector.memset(x_plane[:].bitcast(I32), 0)
         for q in range(QUADRANTS):
             nc.scalar.dma_start(*scale_rows(x_plane, x_scales, q))
+        nc.vector.memset(w3_plane[:].bitcast(I32), 0)
         nc.sync.dma_start(offs_sb[:], offs)
         nc.sync.dma_start(src_sb[:], src)
         nc.sync.dma_start(dst_sb[:], dst)
         nc.sync.dma_start(w_raw[SOURCE][:], w1.rearrange("(p j) c -> p j c", j=PACK))
         nc.sync.dma_start(x_table[:], as_words(x_words))
-        nc.sync.dma_start(w_raw[TARGET][:], w2.rearrange("(p j) c -> p j c", j=PACK))
         nc.sync.dma_start(w3_table[:], as_words(w3_words))
-        nc.vector.memset(w3_plane[:].bitcast(I32), 0)
+        nc.sync.dma_start(w_raw[TARGET][:], w2.rearrange("(p j) c -> p j c", j=PACK))
         for q in range(QUADRANTS):
             nc.sync.dma_start(*scale_rows(w3_plane, w3_scales, q))
 
-        weights = {}
+        rounded, weights = {}, {}
 
-        def quantise_weight(side, pair, copy, rounded_after=None, codes_after=None, plane_after=None):
-            rounded = turn_tile("w_rounded%d%d" % (side, pair), [P, PAIR, P, PACK], BF16, rounded_after)
+        def round_weight(side, pair, copy, over=None):
+            rounded[(side, pair)] = place("w_rounded%d%d" % (side, pair), [P, PAIR, P, PACK], BF16, over)
             copy(
-                rounded[:].rearrange("p t m j -> p m j t"),
+                rounded[(side, pair)][:].rearrange("p t m j -> p m j t"),
                 w_raw[side][:].rearrange("p j (m t) -> p m j t", t=PACK)[:, :, :, PAIR * pair : PAIR * (pair + 1)],
             )
-            codes = turn_tile("w_codes%d%d" % (side, pair), [P, PAIR * P], U32, codes_after)
-            plane = turn_tile("w_plane%d%d" % (side, pair), [P, PAIR * P], U8, plane_after)
+
+        def quantise_weight(side, pair, room=0):
+            codes = place("w_codes%d%d" % (side, pair), [P, PAIR * P], U32, room=room)
+            plane = place("w_plane%d%d" % (side, pair), [P, PAIR * P], U8)
             nc.vector.quantize_mx(
-                out=codes[:].bitcast(FP8X4), scales=plane[:], in_=rounded[:].rearrange("p t m j -> p (t m j)")
+                out=codes[:].bitcast(FP8X4),
+                scales=plane[:],
+                in_=rounded[(side, pair)][:].rearrange("p t m j -> p (t m j)"),
             )
             weights[(side, pair)] = (codes, plane)
 
-        x_bytes = keep.tile([P, S], U8, name="x_bytes", align_bytes=ALIGN)
-        nc.vector.tensor_copy(x_bytes[:], x_plane[:].indirect(offs_sb[:]))
-        quantise_weight(SOURCE, 0, nc.scalar.copy, plane_after="x_plane")
-        x_codes = turn_tile("x_codes", [P, S], U32, "w_rounded00")
-        for first in range(0, S, BANK):
+        x_codes = {}
+        x_bytes = place("x_bytes", [P, S], U8)
+
+        def gather_words(half, over, skip=0):
+            x_codes[half] = place("x_codes%d" % half, [P, BANK], U32, over, skip)
             nc.vector.tensor_copy(
-                x_codes[:, first : first + BANK], x_table[:].bitcast(U32).indirect(entries(offs_sb, first, BANK))
+                x_codes[half][:], x_table[:].bitcast(U32).indirect(entries(offs_sb, half * BANK, BANK))
             )
+
 
         windows = {}
 
         def node_product(side, t, half):
             codes, plane = weights[(side, t // PAIR)]
             cols = slice(t % PAIR * P, (t % PAIR + 1) * P)
-            nodes = slice(half * BANK, (half + 1) * BANK)
             if (side, t) not in windows:
-                windows[(side, t)] = keep.tile([P, S], F32, name="window%d%d" % (side, t), align_bytes=ALIGN)
+                windows[(side, t)] = place("window%d%d" % (side, t), [P, S], F32)
             acc = next_bank([P, BANK])
             nc.tensor.matmul_mx(
                 out=acc[:],
                 lhsT=codes[:, cols].bitcast(FP8X4),
                 lhsT_scale=plane[:, cols],
-                rhs=x_codes[:, nodes].bitcast(FP8X4),
-                rhs_scale=x_bytes[:, nodes],
+                rhs=x_codes[half][:].bitcast(FP8X4),
+                rhs_scale=x_bytes[:, half * BANK : (half + 1) * BANK],
                 start=True,
                 stop=True,
             )
-            nc.scalar.copy(windows[(side, t)][:, nodes], acc[:])
+            nc.scalar.copy(windows[(side, t)][:, half * BANK : (half + 1) * BANK], acc[:])
 
-        quantise_weight(TARGET, 0, nc.vector.tensor_copy)
-        quantise_weight(SOURCE, 1, nc.scalar.copy, codes_after="x_table")
-        for half in range(S // BANK):
-            for t in range(PAIR):
-                node_product(SOURCE, t, half)
-        quantise_weight(TARGET, 1, nc.scalar.copy, rounded_after="w_codes00")
-        for side, t in ((SOURCE, 2), (TARGET, 0), (TARGET, 1), (SOURCE, 3), (TARGET, 2), (TARGET, 3)):
+        def node_tile(side, t):
             for half in range(S // BANK):
                 node_product(side, t, half)
 
-        w3_codes = turn_tile("w3_codes", [P, H], I32, "w_raw1")
-        w3_bytes = turn_tile("w3_bytes", [P, H], U8, "w_plane00")
+        w3_dealt = {}
 
-        def deal_w3():
+        def deal_w3(over=None, skip=0):
+            w3_codes = place("w3_codes", [P, H], I32, over, skip)
+            w3_bytes = place("w3_bytes", [P, H], U8, over, skip + H * PACK)
             nc.vector.tensor_copy(
                 w3_codes[:].rearrange("p (t g i) -> p g t i", t=PACK, i=LINE_WORDS),
                 w3_table[:].rearrange("p (g i t) -> p g t i", t=PACK, i=LINE_WORDS),
@@ -164,131 +173,175 @@ def tile_picked_hub_relu_po_kernel(
             nc.vector.tensor_copy(
                 w3_bytes[:].rearrange("p (t m) -> p t m", t=PACK), w3_plane[:].rearrange("p (m t) -> p t m", t=PACK)
             )
+            w3_dealt["codes"] = w3_codes
+            w3_dealt["bytes"] = w3_bytes
 
-        sources, sums, z_rounded, z_packed, results = {}, {}, {}, {}, {}
-        out_codes = keep.tile([P, S], U32, name="out_codes", align_bytes=ALIGN)
-        out_plane = keep.tile([P, S], U8, name="out_plane", align_bytes=ALIGN)
+        sources, sums, z_rounded, z_packed, results, accs, out_rounded = {}, {}, {}, {}, {}, {}, {}
+        out_codes = place("out_codes", [P, S], U32)
+        out_plane = place("out_plane", [P, S], U8)
         out_rows = out_0.rearrange("(p t) n -> p t n", t=PACK)
-        out_groups = [(c,) for c in range(LAST - 1)] + [(LAST - 1, LAST)]
-        out_rounded = {}
-        for group in out_groups:
-            first, count = span(group)
-            shared = keep.tile([P, count, PACK], BF16, name="out_rounded%d" % group[0], align_bytes=ALIGN)
-            out_rounded[group] = shared[:]
-            for c in group:
-                out_rounded[c] = shared[:, FIRSTS[c] - first : FIRSTS[c] - first + CHUNKS[c], :]
 
-        def gather_sources(chunks, t, after=None):
+        def gather_sources(chunks, t, over=None, skip=0):
             first, count = span(chunks)
-            picked = turn_tile("sources%d%d" % (chunks[0], t), [P, count], F32, after)
+            picked = place("sources%d%d" % (chunks[0], t), [P, count], F32, over, skip)
             nc.vector.tensor_copy(picked[:], windows[(SOURCE, t)][:].indirect(entries(src_sb, first, count)))
             for c in chunks:
                 sources[(c, t)] = picked[:, FIRSTS[c] - first : FIRSTS[c] - first + CHUNKS[c]]
 
-        def add_targets(c, tiles, after=None):
+        def add_targets(c, tiles, over=None, skip=0, lead=0):
             if c not in sums:
-                sums[c] = turn_tile("sums%d" % c, [P, PACK, CHUNKS[c]], F32, after)
+                sums[c] = place("sums%d" % c, [P, PACK, CHUNKS[c]], F32, over, skip, lead)
             for t in tiles:
                 looked_up = windows[(TARGET, t)][:].indirect(entries(dst_sb, FIRSTS[c], CHUNKS[c]))
                 nc.vector.tensor_tensor(sums[c][:, t, :], looked_up, sources[(c, t)], ADD)
 
-        def relu_round(c):
-            z_rounded[c] = turn_tile("z_rounded%d" % c, [P, CHUNKS[c], PACK], BF16)
+        def relu_round(c, over=None, on_vector=False):
+            z_rounded[c] = place("z_rounded%d" % c, [P, CHUNKS[c], PACK], BF16, over)
             by_column, by_tile = interleaved(sums[c][:], z_rounded[c][:])
-            if c == LAST:
+            if on_vector:
                 nc.vector.tensor_scalar_max(by_column, by_tile, 0.0)
             else:
                 nc.scalar.activation(by_column, by_tile, RELU)
 
-        def quantise_z(c):
-            codes = keep.tile([P, CHUNKS[c]], U32, name="z_codes%d" % c, align_bytes=ALIGN)
-            plane = keep.tile([P, CHUNKS[c]], U8, name="z_plane%d" % c, align_bytes=ALIGN)
+        def quantise_z(c, over=None):
+            codes = place("z_codes%d" % c, [P, CHUNKS[c]], U32, over)
+            plane = place("z_plane%d" % c, [P, CHUNKS[c]], U8)
             nc.vector.quantize_mx(
                 out=codes[:].bitcast(FP8X4), scales=plane[:], in_=z_rounded[c][:].rearrange("p n t -> p (n t)")
             )
             z_packed[c] = (codes, plane)
 
-        def edge_product(c):
-            n = CHUNKS[c]
+        def edge_product(c, over=None):
             codes, plane = z_packed[c]
-            results[c] = keep.tile([P, PACK, n], F32, name="results%d" % c, align_bytes=ALIGN)
-            per_bank = BANK // n
-            for t0 in range(0, PACK, per_bank):
-                acc = next_bank([P, per_bank, n])
-                for u in range(per_bank):
-                    cols = slice((t0 + u) * P, (t0 + u + 1) * P)
+            results[c] = place("results%d" % c, [P, PACK, CHUNKS[c]], F32)
+            out_rounded[c] = place("out_rounded%d" % c, [P, CHUNKS[c], PACK], BF16, over)
+            for part in range(CHUNKS[c] // PART):
+                edges = slice(part * PART, (part + 1) * PART)
+                acc = next_bank([P, PACK, PART])
+                for t in range(PACK):
+                    cols = slice(t * P, (t + 1) * P)
                     nc.tensor.matmul_mx(
-                        out=acc[:, u, :],
-                        lhsT=w3_codes[:, cols].bitcast(FP8X4),
-                        lhsT_scale=w3_bytes[:, cols],
-                        rhs=codes[:].bitcast(FP8X4),
-                        rhs_scale=plane[:],
+                        out=acc[:, t, :],
+                        lhsT=w3_dealt["codes"][:, cols].bitcast(FP8X4),
+                        lhsT_scale=w3_dealt["bytes"][:, cols],
+                        rhs=codes[:, edges].bitcast(FP8X4),
+                        rhs_scale=plane[:, edges],
                         start=True,
                         stop=True,
                     )
-                if c == LAST:
-                    nc.vector.tensor_copy(*interleaved(acc[:], out_rounded[c]))
-                nc.scalar.copy(results[c][:, t0 : t0 + per_bank, :], acc[:])
-            queue = nc.scalar if c == LAST else nc.sync
-            queue.dma_start(out_rows[:, :, FIRSTS[c] : FIRSTS[c] + n], results[c][:])
+                accs[(c, part)] = acc
 
-        def round_out(c, copy):
-            copy(*interleaved(results[c][:], out_rounded[c]))
+        def copy_out(c, part):
+            nc.scalar.copy(results[c][:, :, part * PART : (part + 1) * PART], accs[(c, part)][:])
 
-        def quantise_out(group):
-            first, count = span(group)
-            edges = slice(first, first + count)
+        def store_out(c, queue):
+            queue.dma_start(out_rows[:, :, FIRSTS[c] : FIRSTS[c] + CHUNKS[c]], results[c][:])
+
+        def round_out(c, part, copy):
+            copy(*interleaved(accs[(c, part)][:], out_rounded[c][:, part * PART : (part + 1) * PART, :]))
+
+        def empty_bank(c, part):
+            copy_out(c, part)
+            round_out(c, part, nc.scalar.copy)
+
+        def quantise_out(c):
+            edges = slice(FIRSTS[c], FIRSTS[c] + CHUNKS[c])
             nc.vector.quantize_mx(
                 out=out_codes[:, edges].bitcast(FP8X4),
                 scales=out_plane[:, edges],
-                in_=out_rounded[group].rearrange("p n t -> p (n t)"),
+                in_=out_rounded[c][:].rearrange("p n t -> p (n t)"),
             )
+
+        def store_codes(chunks):
+            first, count = span(chunks)
+            edges = slice(first, first + count)
             nc.sync.dma_start(as_words(out_1)[:, edges], out_codes[:, edges].bitcast(I32))
 
         every_tile = range(PACK)
 
-        for t in range(PAIR):
-            gather_sources((0, 1), t)
-            gather_sources((2, 3, 4), t)
-        deal_w3()
-        gather_sources((0, 1), 2)
-        add_targets(0, (0, 1))
+        nc.vector.tensor_copy(x_bytes[:], x_plane[:].indirect(offs_sb[:]))
+        round_weight(SOURCE, 0, nc.scalar.copy)
+        quantise_weight(SOURCE, 0)
+        gather_words(0, "x_plane")
+        round_weight(SOURCE, 1, nc.scalar.copy)
+        gather_words(1, "w_raw0")
+        quantise_weight(SOURCE, 1)
+        for half in range(S // BANK):
+            for t in range(PAIR):
+                node_product(SOURCE, t, half)
+        deal_w3("w_raw0", 2048)
+        round_weight(TARGET, 0, nc.vector.tensor_copy, "x_table")
+        gather_sources((0,), 0)
+        quantise_weight(TARGET, 0)
+        gather_sources((1,), 0)
+        gather_sources((0,), 1)
+        gather_sources((1,), 1)
+        node_tile(SOURCE, 2)
+        round_weight(TARGET, 1, nc.scalar.copy, "w_rounded10")
+        gather_sources((0,), 2)
+        gather_sources((1,), 2)
+        quantise_weight(TARGET, 1)
+        node_tile(SOURCE, 3)
         gather_sources((0,), 3)
-        add_targets(0, (2, 3))
+        gather_sources((1,), 3)
+        node_tile(TARGET, 0)
+        add_targets(0, (0,), lead=2048)
+        add_targets(1, (0,))
+        for t in range(1, PACK):
+            node_tile(TARGET, t)
+            add_targets(0, (t,))
+            add_targets(1, (t,))
 
         relu_round(0)
-        gather_sources((1, 2), 3, after="sources03")
+        gather_sources((2,), 0, "sources03")
+        gather_sources((2,), 1, "sources13")
         quantise_z(0)
         edge_product(0)
-        round_out(0, nc.scalar.copy)
-        add_targets(1, every_tile, after="sums0")
-
         relu_round(1)
-        gather_sources((2, 3, 4), 2, after="sources02")
-        quantise_out(out_groups[0])
+        gather_sources((2,), 2, "sums0", 3072)
+        gather_sources((2,), 3, "z_rounded0")
+        add_targets(2, (0,), "sums0", -1024)
         quantise_z(1)
         edge_product(1)
-        round_out(1, nc.scalar.copy)
-        add_targets(2, every_tile, after="sums1")
-
+        add_targets(2, (1, 2, 3))
+        empty_bank(0, 0)
+        empty_bank(0, 1)
+        store_out(0, nc.sync)
         relu_round(2)
-        gather_sources((3, 4), 3, after="sources13")
-        add_targets(3, every_tile, after="z_rounded1")
+        gather_sources((3, 4), 0, "sources21")
+        gather_sources((3, 4), 1, "sources22")
+        quantise_out(0)
+        gather_sources((3, 4), 2, "sources23")
         quantise_z(2)
-        quantise_out(out_groups[1])
-        relu_round(3)
         edge_product(2)
+        empty_bank(1, 0)
+        empty_bank(1, 1)
+        store_out(1, nc.sync)
+        gather_sources((3, 4), 3, "sums2", 1024)
+        add_targets(3, every_tile, "sums2", 2048)
+        copy_out(2, 0)
+        relu_round(3)
+        round_out(2, 0, nc.scalar.copy)
+        quantise_out(1)
+        store_codes((0, 1))
+        add_targets(4, every_tile, "sums2", -1024)
         quantise_z(3)
         edge_product(3)
-        round_out(2, nc.scalar.copy)
-        add_targets(LAST, every_tile, after="sums3")
-
-        relu_round(LAST)
-        quantise_z(LAST)
-        round_out(3, nc.vector.tensor_copy)
-        quantise_out(out_groups[2])
-        edge_product(LAST)
-        quantise_out(out_groups[3])
+        empty_bank(2, 1)
+        store_out(2, nc.sync)
+        relu_round(4, "z_rounded3", on_vector=True)
+        quantise_z(4)
+        edge_product(4, "out_rounded1")
+        quantise_out(2)
+        empty_bank(3, 0)
+        store_out(3, nc.sync)
+        round_out(4, 0, nc.vector.tensor_copy)
+        quantise_out(3)
+        store_codes((2, 3))
+        copy_out(4, 0)
+        store_out(4, nc.scalar)
+        quantise_out(4)
+        store_codes((4,))
         for q in range(QUADRANTS):
             in_plane, in_dram = scale_rows(out_plane, out_2, q)
             queue = nc.scalar if q % 2 else nc.sync

@@ -176,35 +176,42 @@ def tile_picked_hub_relu_po_kernel(
             w3_dealt["codes"] = w3_codes
             w3_dealt["bytes"] = w3_bytes
 
-        sources, sums, z_rounded, z_packed, results, accs, out_rounded = {}, {}, {}, {}, {}, {}, {}
-        out_codes = place("out_codes", [P, S], U32)
+        sources, z_rounded, z_packed, results, accs, out_rounded = {}, {}, {}, {}, {}, {}
+        out_codes = {}
         out_plane = place("out_plane", [P, S], U8)
         out_rows = out_0.rearrange("(p t) n -> p t n", t=PACK)
 
-        def gather_sources(chunks, t, over=None, skip=0):
+        def gather_sources(chunks, t, over=None, skip=0, into=None):
             first, count = span(chunks)
-            picked = place("sources%d%d" % (chunks[0], t), [P, count], F32, over, skip)
-            nc.vector.tensor_copy(picked[:], windows[(SOURCE, t)][:].indirect(entries(src_sb, first, count)))
+            picked = place("sources%d%d" % (chunks[0], t), [P, count], F32, over, skip)[:] if into is None else into
+            nc.vector.tensor_copy(picked, windows[(SOURCE, t)][:].indirect(entries(src_sb, first, count)))
+            sources[(chunks, t)] = picked
             for c in chunks:
-                sources[(c, t)] = picked[:, FIRSTS[c] - first : FIRSTS[c] - first + CHUNKS[c]]
+                sources[((c,), t)] = picked[:, FIRSTS[c] - first : FIRSTS[c] - first + CHUNKS[c]]
 
-        def add_targets(c, tiles, over=None, skip=0, lead=0):
-            if c not in sums:
-                sums[c] = place("sums%d" % c, [P, PACK, CHUNKS[c]], F32, over, skip, lead)
+        sums_tile = place("sums", [P, PACK, BANK], F32)
+        wide = CHUNKS[0]
+        sums = {(0, 1): sums_tile[:], (0,): sums_tile[:, :, :wide], (1,): sums_tile[:, :, wide:]}
+        sums[(2,)] = sums[(0,)]
+
+        def add_targets(chunks, tiles, over=None):
+            first, count = span(chunks)
+            if chunks not in sums:
+                sums[chunks] = place("sums%d" % chunks[0], [P, PACK, count], F32, over)[:]
             for t in tiles:
-                looked_up = windows[(TARGET, t)][:].indirect(entries(dst_sb, FIRSTS[c], CHUNKS[c]))
-                nc.vector.tensor_tensor(sums[c][:, t, :], looked_up, sources[(c, t)], ADD)
+                looked_up = windows[(TARGET, t)][:].indirect(entries(dst_sb, first, count))
+                nc.vector.tensor_tensor(sums[chunks][:, t, :], looked_up, sources[(chunks, t)], ADD)
 
         def relu_round(c, over=None, on_vector=False):
             z_rounded[c] = place("z_rounded%d" % c, [P, CHUNKS[c], PACK], BF16, over)
-            by_column, by_tile = interleaved(sums[c][:], z_rounded[c][:])
+            by_column, by_tile = interleaved(sums[(c,)], z_rounded[c][:])
             if on_vector:
                 nc.vector.tensor_scalar_max(by_column, by_tile, 0.0)
             else:
                 nc.scalar.activation(by_column, by_tile, RELU)
 
-        def quantise_z(c, over=None):
-            codes = place("z_codes%d" % c, [P, CHUNKS[c]], U32, over)
+        def quantise_z(c, room=0):
+            codes = place("z_codes%d" % c, [P, CHUNKS[c]], U32, room=room)
             plane = place("z_plane%d" % c, [P, CHUNKS[c]], U8)
             nc.vector.quantize_mx(
                 out=codes[:].bitcast(FP8X4), scales=plane[:], in_=z_rounded[c][:].rearrange("p n t -> p (n t)")
@@ -237,32 +244,64 @@ def tile_picked_hub_relu_po_kernel(
         def store_out(c, queue):
             queue.dma_start(out_rows[:, :, FIRSTS[c] : FIRSTS[c] + CHUNKS[c]], results[c][:])
 
+        def store_part(c, part):
+            first = FIRSTS[c] + part * PART
+            nc.sync.dma_start(out_rows[:, :, first : first + PART], results[c][:, :, part * PART : (part + 1) * PART])
+
         def round_out(c, part, copy):
             copy(*interleaved(accs[(c, part)][:], out_rounded[c][:, part * PART : (part + 1) * PART, :]))
+
+        def last_product(c):
+            codes, plane = z_packed[c]
+            results[c] = place("results%d" % c, [P, PACK, CHUNKS[c]], F32)
+            out_rounded[c] = place("out_rounded%d" % c, [P, CHUNKS[c], PACK], BF16)
+            for pair in range(PACK // PAIR):
+                acc = next_bank([P, PAIR, CHUNKS[c]])
+                for u in range(PAIR):
+                    cols = slice((PAIR * pair + u) * P, (PAIR * pair + u + 1) * P)
+                    nc.tensor.matmul_mx(
+                        out=acc[:, u, :],
+                        lhsT=w3_dealt["codes"][:, cols].bitcast(FP8X4),
+                        lhsT_scale=w3_dealt["bytes"][:, cols],
+                        rhs=codes[:].bitcast(FP8X4),
+                        rhs_scale=plane[:],
+                        start=True,
+                        stop=True,
+                    )
+                nc.scalar.copy(results[c][:, PAIR * pair : PAIR * (pair + 1), :], acc[:])
+
+        def round_results(c, part):
+            edges = slice(part * PART, (part + 1) * PART)
+            nc.vector.tensor_copy(*interleaved(results[c][:, :, edges], out_rounded[c][:, edges, :]))
 
         def empty_bank(c, part):
             copy_out(c, part)
             round_out(c, part, nc.scalar.copy)
 
+        def codes_tile(chunks, over=None, skip=0):
+            first, count = span(chunks)
+            codes = place("out_codes%d" % chunks[0], [P, count], U32, over, skip)
+            out_codes[chunks] = codes[:]
+            for c in chunks:
+                out_codes[(c,)] = codes[:, FIRSTS[c] - first : FIRSTS[c] - first + CHUNKS[c]]
+
         def quantise_out(c):
-            edges = slice(FIRSTS[c], FIRSTS[c] + CHUNKS[c])
             nc.vector.quantize_mx(
-                out=out_codes[:, edges].bitcast(FP8X4),
-                scales=out_plane[:, edges],
+                out=out_codes[(c,)].bitcast(FP8X4),
+                scales=out_plane[:, FIRSTS[c] : FIRSTS[c] + CHUNKS[c]],
                 in_=out_rounded[c][:].rearrange("p n t -> p (n t)"),
             )
 
         def store_codes(chunks):
             first, count = span(chunks)
-            edges = slice(first, first + count)
-            nc.sync.dma_start(as_words(out_1)[:, edges], out_codes[:, edges].bitcast(I32))
+            nc.sync.dma_start(as_words(out_1)[:, first : first + count], out_codes[chunks].bitcast(I32))
 
         every_tile = range(PACK)
 
         nc.vector.tensor_copy(x_bytes[:], x_plane[:].indirect(offs_sb[:]))
         round_weight(SOURCE, 0, nc.scalar.copy)
         quantise_weight(SOURCE, 0)
-        gather_words(0, "x_plane")
+        gather_words(0, None)
         round_weight(SOURCE, 1, nc.scalar.copy)
         gather_words(1, "w_raw0")
         quantise_weight(SOURCE, 1)
@@ -271,26 +310,22 @@ def tile_picked_hub_relu_po_kernel(
                 node_product(SOURCE, t, half)
         deal_w3("w_raw0", 2048)
         round_weight(TARGET, 0, nc.vector.tensor_copy, "x_table")
-        gather_sources((0,), 0)
+        gather_sources((0, 1), 0)
         quantise_weight(TARGET, 0)
-        gather_sources((1,), 0)
-        gather_sources((0,), 1)
-        gather_sources((1,), 1)
+        gather_sources((0, 1), 1)
         node_tile(SOURCE, 2)
-        round_weight(TARGET, 1, nc.scalar.copy, "w_rounded10")
-        gather_sources((0,), 2)
-        gather_sources((1,), 2)
-        quantise_weight(TARGET, 1)
+        gather_sources((0, 1), 2)
         node_tile(SOURCE, 3)
+        round_weight(TARGET, 1, nc.scalar.copy, "w_rounded10")
         gather_sources((0,), 3)
         gather_sources((1,), 3)
-        node_tile(TARGET, 0)
-        add_targets(0, (0,), lead=2048)
-        add_targets(1, (0,))
-        for t in range(1, PACK):
+        quantise_weight(TARGET, 1)
+        for t in range(PACK - 1):
             node_tile(TARGET, t)
-            add_targets(0, (t,))
-            add_targets(1, (t,))
+            add_targets((0, 1), (t,))
+        node_tile(TARGET, 3)
+        add_targets((0,), (3,))
+        add_targets((1,), (3,))
 
         relu_round(0)
         gather_sources((2,), 0, "sources03")
@@ -298,50 +333,56 @@ def tile_picked_hub_relu_po_kernel(
         quantise_z(0)
         edge_product(0)
         relu_round(1)
-        gather_sources((2,), 2, "sums0", 3072)
-        gather_sources((2,), 3, "z_rounded0")
-        add_targets(2, (0,), "sums0", -1024)
+        add_targets((2,), (0,))
+        gather_sources((2,), 2, "z_rounded0")
+        gather_sources((2,), 3, "z_rounded0", 1024)
         quantise_z(1)
         edge_product(1)
-        add_targets(2, (1, 2, 3))
+        add_targets((2,), (1, 2, 3))
         empty_bank(0, 0)
         empty_bank(0, 1)
         store_out(0, nc.sync)
         relu_round(2)
         gather_sources((3, 4), 0, "sources21")
         gather_sources((3, 4), 1, "sources22")
+        codes_tile((0,))
         quantise_out(0)
+        store_codes((0,))
         gather_sources((3, 4), 2, "sources23")
-        quantise_z(2)
+        quantise_z(2, room=2048)
         edge_product(2)
         empty_bank(1, 0)
         empty_bank(1, 1)
         store_out(1, nc.sync)
-        gather_sources((3, 4), 3, "sums2", 1024)
-        add_targets(3, every_tile, "sums2", 2048)
+        gather_sources((3, 4), 3, into=sums[(2,)][:, 0, :])
+        add_targets((3,), every_tile, "z_rounded2")
         copy_out(2, 0)
+        store_part(2, 0)
         relu_round(3)
         round_out(2, 0, nc.scalar.copy)
-        quantise_out(1)
-        store_codes((0, 1))
-        add_targets(4, every_tile, "sums2", -1024)
+        add_targets((4,), every_tile, "z_codes2")
         quantise_z(3)
         edge_product(3)
         empty_bank(2, 1)
-        store_out(2, nc.sync)
-        relu_round(4, "z_rounded3", on_vector=True)
+        store_part(2, 1)
+        relu_round(4, "sums3", on_vector=True)
+        codes_tile((1,), "sums3", 1024)
+        quantise_out(1)
+        store_codes((1,))
         quantise_z(4)
-        edge_product(4, "out_rounded1")
-        quantise_out(2)
-        empty_bank(3, 0)
+        copy_out(3, 0)
         store_out(3, nc.sync)
-        round_out(4, 0, nc.vector.tensor_copy)
-        quantise_out(3)
-        store_codes((2, 3))
-        copy_out(4, 0)
+        last_product(4)
+        codes_tile((2,))
+        quantise_out(2)
+        store_codes((2,))
+        round_results(3, 0)
         store_out(4, nc.scalar)
+        round_results(4, 0)
+        codes_tile((3, 4))
+        quantise_out(3)
         quantise_out(4)
-        store_codes((4,))
+        store_codes((3, 4))
         for q in range(QUADRANTS):
             in_plane, in_dram = scale_rows(out_plane, out_2, q)
             queue = nc.scalar if q % 2 else nc.sync

@@ -91,7 +91,8 @@ def tile_picked_hub_relu_po_kernel(
         dst_sb = lists.tile([P, S // LIST_ROWS], U16, name="dst_sb")
         x_table = place("x_table", [P, T], I32)
         x_plane = place("x_plane", [P, T], U8)
-        w_raw = [place("w_raw%d" % side, [P, PACK, H], F32) for side in (SOURCE, TARGET)]
+        w_raw = {SOURCE: place("w_raw0", [P, PACK, H], F32)}
+        w2_halves = [place("w2_raw%d" % half, [P, PACK, H // 2], F32) for half in range(2)]
         w3_table = place("w3_table", [P, H], I32)
         w3_plane = place("w3_plane", [P, H], U8)
 
@@ -104,8 +105,10 @@ def tile_picked_hub_relu_po_kernel(
         nc.sync.dma_start(dst_sb[:], dst)
         nc.sync.dma_start(w_raw[SOURCE][:], w1.rearrange("(p j) c -> p j c", j=PACK))
         nc.sync.dma_start(x_table[:], as_words(x_words))
+        w2_rows = w2.rearrange("(p j) c -> p j c", j=PACK)
+        for half in range(2):
+            nc.sync.dma_start(w2_halves[half][:], w2_rows[:, :, half * H // 2 : (half + 1) * H // 2])
         nc.sync.dma_start(w3_table[:], as_words(w3_words))
-        nc.sync.dma_start(w_raw[TARGET][:], w2.rearrange("(p j) c -> p j c", j=PACK))
         for q in range(QUADRANTS):
             nc.sync.dma_start(*scale_rows(w3_plane, w3_scales, q))
 
@@ -128,34 +131,55 @@ def tile_picked_hub_relu_po_kernel(
             )
             weights[(side, pair)] = (codes, plane)
 
+        w2_rounded = place("w2_rounded", [P, PACK, P, PACK], BF16)
+
+        def round_w2(half):
+            columns = slice(half * P // 2, (half + 1) * P // 2)
+            nc.scalar.copy(
+                w2_rounded[:, :, columns, :].rearrange("p t m j -> p m j t"),
+                w2_halves[half][:].rearrange("p j (m t) -> p m j t", t=PACK),
+            )
+
+        def quantise_w2():
+            codes = place("w2_codes", [P, H], U32)
+            plane = place("w2_plane", [P, H], U8)
+            nc.vector.quantize_mx(
+                out=codes[:].bitcast(FP8X4), scales=plane[:], in_=w2_rounded[:].rearrange("p t m j -> p (t m j)")
+            )
+            for pair in range(PACK // PAIR):
+                columns = slice(pair * PAIR * P, (pair + 1) * PAIR * P)
+                weights[(TARGET, pair)] = (codes[:, columns], plane[:, columns])
+
         x_codes = {}
         x_bytes = place("x_bytes", [P, S], U8)
 
-        def gather_words(half, over, skip=0):
+        def gather_words(half, over, skip=0, piece=BANK):
             x_codes[half] = place("x_codes%d" % half, [P, BANK], U32, over, skip)
-            nc.vector.tensor_copy(
-                x_codes[half][:], x_table[:].bitcast(U32).indirect(entries(offs_sb, half * BANK, BANK))
-            )
+            for first in range(0, BANK, piece):
+                picked = entries(offs_sb, half * BANK + first, piece)
+                nc.vector.tensor_copy(x_codes[half][:, first : first + piece], x_table[:].bitcast(U32).indirect(picked))
 
 
         windows = {}
 
-        def node_product(side, t, half):
+        def node_product(side, t, half, piece=BANK):
             codes, plane = weights[(side, t // PAIR)]
             cols = slice(t % PAIR * P, (t % PAIR + 1) * P)
             if (side, t) not in windows:
                 windows[(side, t)] = place("window%d%d" % (side, t), [P, S], F32)
-            acc = next_bank([P, BANK])
-            nc.tensor.matmul_mx(
-                out=acc[:],
-                lhsT=codes[:, cols].bitcast(FP8X4),
-                lhsT_scale=plane[:, cols],
-                rhs=x_codes[half][:].bitcast(FP8X4),
-                rhs_scale=x_bytes[:, half * BANK : (half + 1) * BANK],
-                start=True,
-                stop=True,
-            )
-            nc.scalar.copy(windows[(side, t)][:, half * BANK : (half + 1) * BANK], acc[:])
+            for first in range(0, BANK, piece):
+                nodes = slice(half * BANK + first, half * BANK + first + piece)
+                acc = next_bank([P, piece])
+                nc.tensor.matmul_mx(
+                    out=acc[:],
+                    lhsT=codes[:, cols].bitcast(FP8X4),
+                    lhsT_scale=plane[:, cols],
+                    rhs=x_codes[half][:, first : first + piece].bitcast(FP8X4),
+                    rhs_scale=x_bytes[:, nodes],
+                    start=True,
+                    stop=True,
+                )
+                nc.scalar.copy(windows[(side, t)][:, nodes], acc[:])
 
         def node_tile(side, t):
             for half in range(S // BANK):
@@ -194,10 +218,10 @@ def tile_picked_hub_relu_po_kernel(
         sums = {(0, 1): sums_tile[:], (0,): sums_tile[:, :, :wide], (1,): sums_tile[:, :, wide:]}
         sums[(2,)] = sums[(0,)]
 
-        def add_targets(chunks, tiles, over=None):
+        def add_targets(chunks, tiles, over=None, skip=0):
             first, count = span(chunks)
             if chunks not in sums:
-                sums[chunks] = place("sums%d" % chunks[0], [P, PACK, count], F32, over)[:]
+                sums[chunks] = place("sums%d" % chunks[0], [P, PACK, count], F32, over, skip)[:]
             for t in tiles:
                 looked_up = windows[(TARGET, t)][:].indirect(entries(dst_sb, first, count))
                 nc.vector.tensor_tensor(sums[chunks][:, t, :], looked_up, sources[(chunks, t)], ADD)
@@ -300,26 +324,26 @@ def tile_picked_hub_relu_po_kernel(
 
         nc.vector.tensor_copy(x_bytes[:], x_plane[:].indirect(offs_sb[:]))
         round_weight(SOURCE, 0, nc.scalar.copy)
-        quantise_weight(SOURCE, 0)
+        quantise_weight(SOURCE, 0, room=4096)
         gather_words(0, None)
         round_weight(SOURCE, 1, nc.scalar.copy)
-        gather_words(1, "w_raw0")
+        gather_words(1, "w_raw0", piece=BANK // 2)
         quantise_weight(SOURCE, 1)
-        for half in range(S // BANK):
-            for t in range(PAIR):
-                node_product(SOURCE, t, half)
+        round_w2(0)
+        node_product(SOURCE, 0, 0)
+        node_product(SOURCE, 0, 1, BANK // 2)
+        node_tile(SOURCE, 1)
         deal_w3("w_raw0", 2048)
-        round_weight(TARGET, 0, nc.vector.tensor_copy, "x_table")
+        round_w2(1)
         gather_sources((0, 1), 0)
-        quantise_weight(TARGET, 0)
+        gather_sources((2,), 0)
         gather_sources((0, 1), 1)
+        quantise_w2()
         node_tile(SOURCE, 2)
         gather_sources((0, 1), 2)
         node_tile(SOURCE, 3)
-        round_weight(TARGET, 1, nc.scalar.copy, "w_rounded10")
         gather_sources((0,), 3)
         gather_sources((1,), 3)
-        quantise_weight(TARGET, 1)
         for t in range(PACK - 1):
             node_tile(TARGET, t)
             add_targets((0, 1), (t,))
@@ -328,48 +352,50 @@ def tile_picked_hub_relu_po_kernel(
         add_targets((1,), (3,))
 
         relu_round(0)
-        gather_sources((2,), 0, "sources03")
-        gather_sources((2,), 1, "sources13")
+        gather_sources((2,), 1, "sources03")
+        gather_sources((2,), 2, "sources13")
         quantise_z(0)
         edge_product(0)
         relu_round(1)
         add_targets((2,), (0,))
-        gather_sources((2,), 2, "z_rounded0")
-        gather_sources((2,), 3, "z_rounded0", 1024)
+        gather_sources((2,), 3, "z_rounded0", 512)
         quantise_z(1)
         edge_product(1)
         add_targets((2,), (1, 2, 3))
         empty_bank(0, 0)
         empty_bank(0, 1)
         store_out(0, nc.sync)
+        copy_out(1, 0)
+        store_part(1, 0)
         relu_round(2)
         gather_sources((3, 4), 0, "sources21")
         gather_sources((3, 4), 1, "sources22")
         codes_tile((0,))
         quantise_out(0)
         store_codes((0,))
-        gather_sources((3, 4), 2, "sources23")
-        quantise_z(2, room=2048)
+        gather_sources((3, 4), 2, "z_rounded0")
+        gather_sources((3, 4), 3, "z_rounded0", 1024)
+        quantise_z(2)
         edge_product(2)
-        empty_bank(1, 0)
+        round_out(1, 0, nc.scalar.copy)
         empty_bank(1, 1)
-        store_out(1, nc.sync)
-        gather_sources((3, 4), 3, into=sums[(2,)][:, 0, :])
-        add_targets((3,), every_tile, "z_rounded2")
+        store_part(1, 1)
+        add_targets((3,), every_tile, "sums")
         copy_out(2, 0)
         store_part(2, 0)
         relu_round(3)
+        copy_out(2, 1)
+        store_part(2, 1)
         round_out(2, 0, nc.scalar.copy)
-        add_targets((4,), every_tile, "z_codes2")
+        add_targets((4,), every_tile, "sums", 2048)
         quantise_z(3)
         edge_product(3)
-        empty_bank(2, 1)
-        store_part(2, 1)
         relu_round(4, "sums3", on_vector=True)
         codes_tile((1,), "sums3", 1024)
         quantise_out(1)
         store_codes((1,))
         quantise_z(4)
+        round_results(2, 1)
         copy_out(3, 0)
         store_out(3, nc.sync)
         last_product(4)

@@ -97,12 +97,13 @@ def tile_picked_hub_relu_po_kernel(
         w3_plane = place("w3_plane", [P, H], U8)
 
         nc.vector.memset(x_plane[:].bitcast(I32), 0)
-        for q in range(QUADRANTS):
-            nc.scalar.dma_start(*scale_rows(x_plane, x_scales, q))
         nc.vector.memset(w3_plane[:].bitcast(I32), 0)
         nc.sync.dma_start(offs_sb[:], offs)
         nc.sync.dma_start(src_sb[:], src)
         nc.sync.dma_start(dst_sb[:], dst)
+        for q in range(QUADRANTS):
+            queue = nc.scalar if q // 2 else nc.sync
+            queue.dma_start(*scale_rows(x_plane, x_scales, q))
         nc.sync.dma_start(w_raw[SOURCE][:], w1.rearrange("(p j) c -> p j c", j=PACK))
         nc.sync.dma_start(x_table[:], as_words(x_words))
         w2_rows = w2.rearrange("(p j) c -> p j c", j=PACK)
@@ -324,8 +325,8 @@ def tile_picked_hub_relu_po_kernel(
 
         nc.vector.tensor_copy(x_bytes[:], x_plane[:].indirect(offs_sb[:]))
         round_weight(SOURCE, 0, nc.scalar.copy)
-        quantise_weight(SOURCE, 0, room=4096)
-        gather_words(0, None)
+        quantise_weight(SOURCE, 0)
+        gather_words(0, "w_rounded00")
         round_weight(SOURCE, 1, nc.scalar.copy)
         gather_words(1, "w_raw0", piece=BANK // 2)
         quantise_weight(SOURCE, 1)

@@ -91,8 +91,7 @@ def tile_picked_hub_relu_po_kernel(
         dst_sb = lists.tile([P, S // LIST_ROWS], U16, name="dst_sb")
         x_table = place("x_table", [P, T], I32)
         x_plane = place("x_plane", [P, T], U8)
-        w_raw = {SOURCE: place("w_raw0", [P, PACK, H], F32)}
-        w2_halves = [place("w2_raw%d" % half, [P, PACK, H // 2], F32) for half in range(2)]
+        w_raw = [place("w_raw%d" % side, [P, PACK, H], F32) for side in (SOURCE, TARGET)]
         w3_table = place("w3_table", [P, H], I32)
         w3_plane = place("w3_plane", [P, H], U8)
 
@@ -104,87 +103,58 @@ def tile_picked_hub_relu_po_kernel(
         for q in range(QUADRANTS):
             queue = nc.scalar if q // 2 else nc.sync
             queue.dma_start(*scale_rows(x_plane, x_scales, q))
-        nc.sync.dma_start(w_raw[SOURCE][:], w1.rearrange("(p j) c -> p j c", j=PACK))
         nc.sync.dma_start(x_table[:], as_words(x_words))
-        w2_rows = w2.rearrange("(p j) c -> p j c", j=PACK)
-        for half in range(2):
-            nc.sync.dma_start(w2_halves[half][:], w2_rows[:, :, half * H // 2 : (half + 1) * H // 2])
+        nc.sync.dma_start(w_raw[SOURCE][:], w1.rearrange("(p j) c -> p j c", j=PACK))
         nc.sync.dma_start(w3_table[:], as_words(w3_words))
         for q in range(QUADRANTS):
             nc.sync.dma_start(*scale_rows(w3_plane, w3_scales, q))
+        nc.sync.dma_start(w_raw[TARGET][:], w2.rearrange("(p j) c -> p j c", j=PACK))
 
         rounded, weights = {}, {}
 
-        def round_weight(side, pair, copy, over=None):
-            rounded[(side, pair)] = place("w_rounded%d%d" % (side, pair), [P, PAIR, P, PACK], BF16, over)
+        def round_weight(side, pair, copy, columns=slice(0, P), over=None, skip=0):
+            if (side, pair) not in rounded:
+                rounded[(side, pair)] = place("w_rounded%d%d" % (side, pair), [P, PAIR, P, PACK], BF16, over, skip)
+            tiles = slice(PAIR * pair, PAIR * (pair + 1))
             copy(
-                rounded[(side, pair)][:].rearrange("p t m j -> p m j t"),
-                w_raw[side][:].rearrange("p j (m t) -> p m j t", t=PACK)[:, :, :, PAIR * pair : PAIR * (pair + 1)],
+                rounded[(side, pair)][:, :, columns, :].rearrange("p t m j -> p m j t"),
+                w_raw[side][:].rearrange("p j (m t) -> p m j t", t=PACK)[:, columns, :, tiles],
             )
 
-        def quantise_weight(side, pair, room=0):
-            codes = place("w_codes%d%d" % (side, pair), [P, PAIR * P], U32, room=room)
-            plane = place("w_plane%d%d" % (side, pair), [P, PAIR * P], U8)
+        def quantise_weight(side, first, count, lead=0, room=0):
+            codes = place("w_codes%d%d" % (side, first), [P, count * P], U32, lead=lead, room=room)
+            plane = place("w_plane%d%d" % (side, first), [P, count * P], U8)
+            source = rounded[(side, first // PAIR)][:, first % PAIR : first % PAIR + count]
             nc.vector.quantize_mx(
-                out=codes[:].bitcast(FP8X4),
-                scales=plane[:],
-                in_=rounded[(side, pair)][:].rearrange("p t m j -> p (t m j)"),
+                out=codes[:].bitcast(FP8X4), scales=plane[:], in_=source.rearrange("p t m j -> p (t m j)")
             )
-            weights[(side, pair)] = (codes, plane)
+            for u in range(count):
+                weights[(side, first + u)] = (codes[:, u * P : (u + 1) * P], plane[:, u * P : (u + 1) * P])
 
-        w2_rounded = place("w2_rounded", [P, PACK, P, PACK], BF16)
-
-        def round_w2(half):
-            columns = slice(half * P // 2, (half + 1) * P // 2)
-            nc.scalar.copy(
-                w2_rounded[:, :, columns, :].rearrange("p t m j -> p m j t"),
-                w2_halves[half][:].rearrange("p j (m t) -> p m j t", t=PACK),
-            )
-
-        def quantise_w2():
-            codes = place("w2_codes", [P, H], U32)
-            plane = place("w2_plane", [P, H], U8)
-            nc.vector.quantize_mx(
-                out=codes[:].bitcast(FP8X4), scales=plane[:], in_=w2_rounded[:].rearrange("p t m j -> p (t m j)")
-            )
-            for pair in range(PACK // PAIR):
-                columns = slice(pair * PAIR * P, (pair + 1) * PAIR * P)
-                weights[(TARGET, pair)] = (codes[:, columns], plane[:, columns])
-
-        x_codes = {}
+        x_codes = place("x_codes", [P, S], U32)
         x_bytes = place("x_bytes", [P, S], U8)
-
-        def gather_words(half, over, skip=0, piece=BANK):
-            x_codes[half] = place("x_codes%d" % half, [P, BANK], U32, over, skip)
-            for first in range(0, BANK, piece):
-                picked = entries(offs_sb, half * BANK + first, piece)
-                nc.vector.tensor_copy(x_codes[half][:, first : first + piece], x_table[:].bitcast(U32).indirect(picked))
-
-
         windows = {}
 
-        def node_product(side, t, half, piece=BANK):
-            codes, plane = weights[(side, t // PAIR)]
-            cols = slice(t % PAIR * P, (t % PAIR + 1) * P)
+        def node_product(side, t, first, count, copy=nc.scalar.copy):
+            codes, plane = weights[(side, t)]
             if (side, t) not in windows:
                 windows[(side, t)] = place("window%d%d" % (side, t), [P, S], F32)
-            for first in range(0, BANK, piece):
-                nodes = slice(half * BANK + first, half * BANK + first + piece)
-                acc = next_bank([P, piece])
-                nc.tensor.matmul_mx(
-                    out=acc[:],
-                    lhsT=codes[:, cols].bitcast(FP8X4),
-                    lhsT_scale=plane[:, cols],
-                    rhs=x_codes[half][:, first : first + piece].bitcast(FP8X4),
-                    rhs_scale=x_bytes[:, nodes],
-                    start=True,
-                    stop=True,
-                )
-                nc.scalar.copy(windows[(side, t)][:, nodes], acc[:])
+            nodes = slice(first, first + count)
+            acc = next_bank([P, count])
+            nc.tensor.matmul_mx(
+                out=acc[:],
+                lhsT=codes.bitcast(FP8X4),
+                lhsT_scale=plane,
+                rhs=x_codes[:, nodes].bitcast(FP8X4),
+                rhs_scale=x_bytes[:, nodes],
+                start=True,
+                stop=True,
+            )
+            copy(windows[(side, t)][:, nodes], acc[:])
 
         def node_tile(side, t):
-            for half in range(S // BANK):
-                node_product(side, t, half)
+            for first in range(0, S, BANK):
+                node_product(side, t, first, BANK)
 
         w3_dealt = {}
 
@@ -210,9 +180,10 @@ def tile_picked_hub_relu_po_kernel(
             first, count = span(chunks)
             picked = place("sources%d%d" % (chunks[0], t), [P, count], F32, over, skip)[:] if into is None else into
             nc.vector.tensor_copy(picked, windows[(SOURCE, t)][:].indirect(entries(src_sb, first, count)))
-            sources[(chunks, t)] = picked
-            for c in chunks:
-                sources[((c,), t)] = picked[:, FIRSTS[c] - first : FIRSTS[c] - first + CHUNKS[c]]
+            for low in range(len(chunks)):
+                for high in range(low + 1, len(chunks) + 1):
+                    begin, width = span(chunks[low:high])
+                    sources[(chunks[low:high], t)] = picked[:, begin - first : begin - first + width]
 
         sums_tile = place("sums", [P, PACK, BANK], F32)
         wide = CHUNKS[0]
@@ -227,8 +198,8 @@ def tile_picked_hub_relu_po_kernel(
                 looked_up = windows[(TARGET, t)][:].indirect(entries(dst_sb, first, count))
                 nc.vector.tensor_tensor(sums[chunks][:, t, :], looked_up, sources[(chunks, t)], ADD)
 
-        def relu_round(c, over=None, on_vector=False):
-            z_rounded[c] = place("z_rounded%d" % c, [P, CHUNKS[c], PACK], BF16, over)
+        def relu_round(c, over=None, on_vector=False, room=0):
+            z_rounded[c] = place("z_rounded%d" % c, [P, CHUNKS[c], PACK], BF16, over, room=room)
             by_column, by_tile = interleaved(sums[(c,)], z_rounded[c][:])
             if on_vector:
                 nc.vector.tensor_scalar_max(by_column, by_tile, 0.0)
@@ -243,10 +214,9 @@ def tile_picked_hub_relu_po_kernel(
             )
             z_packed[c] = (codes, plane)
 
-        def edge_product(c, over=None):
+        def edge_product(c):
             codes, plane = z_packed[c]
             results[c] = place("results%d" % c, [P, PACK, CHUNKS[c]], F32)
-            out_rounded[c] = place("out_rounded%d" % c, [P, CHUNKS[c], PACK], BF16, over)
             for part in range(CHUNKS[c] // PART):
                 edges = slice(part * PART, (part + 1) * PART)
                 acc = next_bank([P, PACK, PART])
@@ -274,12 +244,13 @@ def tile_picked_hub_relu_po_kernel(
             nc.sync.dma_start(out_rows[:, :, first : first + PART], results[c][:, :, part * PART : (part + 1) * PART])
 
         def round_out(c, part, copy):
+            if c not in out_rounded:
+                out_rounded[c] = place("out_rounded%d" % c, [P, CHUNKS[c], PACK], BF16)
             copy(*interleaved(accs[(c, part)][:], out_rounded[c][:, part * PART : (part + 1) * PART, :]))
 
         def last_product(c):
             codes, plane = z_packed[c]
             results[c] = place("results%d" % c, [P, PACK, CHUNKS[c]], F32)
-            out_rounded[c] = place("out_rounded%d" % c, [P, CHUNKS[c], PACK], BF16)
             for pair in range(PACK // PAIR):
                 acc = next_bank([P, PAIR, CHUNKS[c]])
                 for u in range(PAIR):
@@ -293,9 +264,12 @@ def tile_picked_hub_relu_po_kernel(
                         start=True,
                         stop=True,
                     )
-                nc.scalar.copy(results[c][:, PAIR * pair : PAIR * (pair + 1), :], acc[:])
+                tiles = slice(PAIR * pair, PAIR * (pair + 1))
+                nc.scalar.copy(results[c][:, tiles, :], acc[:])
 
-        def round_results(c, part):
+        def round_results(c, part, over=None):
+            if c not in out_rounded:
+                out_rounded[c] = place("out_rounded%d" % c, [P, CHUNKS[c], PACK], BF16, over)
             edges = slice(part * PART, (part + 1) * PART)
             nc.vector.tensor_copy(*interleaved(results[c][:, :, edges], out_rounded[c][:, edges, :]))
 
@@ -317,6 +291,13 @@ def tile_picked_hub_relu_po_kernel(
                 in_=out_rounded[c][:].rearrange("p n t -> p (n t)"),
             )
 
+        def store_scales(chunks, queues):
+            first, count = span(chunks)
+            words = slice(first // PACK, (first + count) // PACK)
+            for q in range(QUADRANTS):
+                in_plane, in_dram = scale_rows(out_plane, out_2, q)
+                queues[q % len(queues)].dma_start(in_dram[:, words], in_plane[:, words])
+
         def store_codes(chunks):
             first, count = span(chunks)
             nc.sync.dma_start(as_words(out_1)[:, first : first + count], out_codes[chunks].bitcast(I32))
@@ -324,24 +305,25 @@ def tile_picked_hub_relu_po_kernel(
         every_tile = range(PACK)
 
         nc.vector.tensor_copy(x_bytes[:], x_plane[:].indirect(offs_sb[:]))
-        round_weight(SOURCE, 0, nc.scalar.copy)
-        quantise_weight(SOURCE, 0)
-        gather_words(0, "w_rounded00")
+        nc.vector.tensor_copy(x_codes[:], x_table[:].bitcast(U32).indirect(offs_sb[:]))
+        round_weight(SOURCE, 0, nc.vector.tensor_copy, slice(0, 80))
+        round_weight(SOURCE, 0, nc.scalar.copy, slice(80, P))
         round_weight(SOURCE, 1, nc.scalar.copy)
-        gather_words(1, "w_raw0", piece=BANK // 2)
-        quantise_weight(SOURCE, 1)
-        round_w2(0)
-        node_product(SOURCE, 0, 0)
-        node_product(SOURCE, 0, 1, BANK // 2)
+        quantise_weight(SOURCE, 0, 1)
+        quantise_weight(SOURCE, 1, 1, lead=1792, room=2304)
+        quantise_weight(SOURCE, 2, 2)
+        deal_w3("w_raw0")
+        for first in range(0, S, 256):
+            node_product(SOURCE, 0, first, 256)
         node_tile(SOURCE, 1)
-        deal_w3("w_raw0", 2048)
-        round_w2(1)
-        gather_sources((0, 1), 0)
-        gather_sources((2,), 0)
-        gather_sources((0, 1), 1)
-        quantise_w2()
+        round_weight(TARGET, 0, nc.scalar.copy, over="w_codes01", skip=-1792)
+        gather_sources((0, 1, 2), 0)
+        gather_sources((0, 1, 2), 1)
+        quantise_weight(TARGET, 0, 2)
         node_tile(SOURCE, 2)
-        gather_sources((0, 1), 2)
+        round_weight(TARGET, 1, nc.scalar.copy, over="w_codes01", skip=256)
+        gather_sources((0, 1, 2), 2)
+        quantise_weight(TARGET, 2, 2)
         node_tile(SOURCE, 3)
         gather_sources((0,), 3)
         gather_sources((1,), 3)
@@ -353,64 +335,61 @@ def tile_picked_hub_relu_po_kernel(
         add_targets((1,), (3,))
 
         relu_round(0)
-        gather_sources((2,), 1, "sources03")
-        gather_sources((2,), 2, "sources13")
+        gather_sources((2,), 3, "sources03")
+        gather_sources((3, 4), 0, "sources13")
         quantise_z(0)
         edge_product(0)
         relu_round(1)
-        add_targets((2,), (0,))
-        gather_sources((2,), 3, "z_rounded0", 512)
+        add_targets((2,), (0, 1))
         quantise_z(1)
         edge_product(1)
-        add_targets((2,), (1, 2, 3))
-        empty_bank(0, 0)
-        empty_bank(0, 1)
+        add_targets((2,), (2, 3))
+        copy_out(0, 0)
+        copy_out(0, 1)
         store_out(0, nc.sync)
-        copy_out(1, 0)
-        store_part(1, 0)
+        round_out(0, 0, nc.scalar.copy)
         relu_round(2)
-        gather_sources((3, 4), 0, "sources21")
-        gather_sources((3, 4), 1, "sources22")
-        codes_tile((0,))
-        quantise_out(0)
-        store_codes((0,))
-        gather_sources((3, 4), 2, "z_rounded0")
-        gather_sources((3, 4), 3, "z_rounded0", 1024)
+        gather_sources((3, 4), 1, "sources00")
+        gather_sources((3, 4), 2, "sources01")
+        gather_sources((3, 4), 3, "sources02")
         quantise_z(2)
         edge_product(2)
-        round_out(1, 0, nc.scalar.copy)
-        empty_bank(1, 1)
-        store_part(1, 1)
+        copy_out(1, 0)
+        copy_out(1, 1)
+        store_out(1, nc.sync)
+        round_out(0, 1, nc.scalar.copy)
         add_targets((3,), every_tile, "sums")
         copy_out(2, 0)
         store_part(2, 0)
-        relu_round(3)
+        relu_round(3, room=2048)
         copy_out(2, 1)
         store_part(2, 1)
-        round_out(2, 0, nc.scalar.copy)
         add_targets((4,), every_tile, "sums", 2048)
         quantise_z(3)
         edge_product(3)
+        round_out(1, 0, nc.scalar.copy)
+        round_out(1, 1, nc.scalar.copy)
         relu_round(4, "sums3", on_vector=True)
-        codes_tile((1,), "sums3", 1024)
-        quantise_out(1)
-        store_codes((1,))
+        codes_tile((0,), "sums3", 1024)
+        quantise_out(0)
+        store_codes((0,))
         quantise_z(4)
-        round_results(2, 1)
         copy_out(3, 0)
         store_out(3, nc.sync)
+        round_results(2, 0, "z_rounded3")
+        codes_tile((1,))
+        quantise_out(1)
+        store_codes((1,))
+        round_results(2, 1)
         last_product(4)
+        store_out(4, nc.sync)
+        round_results(3, 0)
         codes_tile((2,))
         quantise_out(2)
         store_codes((2,))
-        round_results(3, 0)
-        store_out(4, nc.scalar)
         round_results(4, 0)
         codes_tile((3, 4))
         quantise_out(3)
         quantise_out(4)
         store_codes((3, 4))
-        for q in range(QUADRANTS):
-            in_plane, in_dram = scale_rows(out_plane, out_2, q)
-            queue = nc.scalar if q % 2 else nc.sync
-            queue.dma_start(in_dram, in_plane)
+        store_scales((0, 1, 2, 3, 4), (nc.scalar, nc.sync))

@@ -33,8 +33,8 @@ FIRSTS = [sum(CHUNKS[:c]) for c in range(len(CHUNKS))]
 LAST = len(CHUNKS) - 1
 
 
-def scale_rows(plane, scales, q):
-    return plane[32 * q : 32 * q + 4, :].bitcast(I32), scales[0, 4 * q : 4 * q + 4, :].bitcast(I32)
+def scale_rows(plane, scales, r):
+    return plane[r:P:32, :].bitcast(I32), scales[0, r::QUADRANTS, :].bitcast(I32)
 
 
 def as_words(packed):
@@ -101,8 +101,7 @@ def tile_picked_hub_relu_po_kernel(
         nc.sync.dma_start(src_sb[:], src)
         nc.sync.dma_start(dst_sb[:], dst)
         for q in range(QUADRANTS):
-            queue = nc.scalar if q // 2 else nc.sync
-            queue.dma_start(*scale_rows(x_plane, x_scales, q))
+            nc.sync.dma_start(*scale_rows(x_plane, x_scales, q))
         nc.sync.dma_start(x_table[:], as_words(x_words))
         nc.sync.dma_start(w_raw[SOURCE][:], w1.rearrange("(p j) c -> p j c", j=PACK))
         nc.sync.dma_start(w3_table[:], as_words(w3_words))

@@ -111,19 +111,23 @@ def tile_picked_hub_relu_po_kernel(
 
         rounded, weights = {}, {}
 
-        def round_weight(side, pair, copy, columns=slice(0, P), over=None, skip=0):
-            if (side, pair) not in rounded:
-                rounded[(side, pair)] = place("w_rounded%d%d" % (side, pair), [P, PAIR, P, PACK], BF16, over, skip)
-            tiles = slice(PAIR * pair, PAIR * (pair + 1))
-            copy(
-                rounded[(side, pair)][:, :, columns, :].rearrange("p t m j -> p m j t"),
-                w_raw[side][:].rearrange("p j (m t) -> p m j t", t=PACK)[:, columns, :, tiles],
-            )
+        def round_weight(side, first, count, over=None, skip=0):
+            dealt = place("w_rounded%d%d" % (side, first), [P, count, P, PACK], BF16, over, skip)
+            by_row = w_raw[side][:].rearrange("p j (m t) -> p m j t", t=PACK)
+            nc.scalar.copy(dealt[:].rearrange("p t m j -> p m j t"), by_row[:, :, :, first : first + count])
+            for u in range(count):
+                rounded[(side, first + u)] = dealt[:, u:]
+
+        def round_first_tile():
+            dealt = place("w_rounded00", [P, 1, P, PACK], BF16, room=H * PACK)
+            by_row = w_raw[SOURCE][:].rearrange("p j (m t) -> p m j t", t=PACK)
+            nc.vector.tensor_copy(dealt[:, 0], by_row[:, :, :, 0])
+            rounded[(SOURCE, 0)] = dealt[:]
 
         def quantise_weight(side, first, count, lead=0, room=0):
             codes = place("w_codes%d%d" % (side, first), [P, count * P], U32, lead=lead, room=room)
             plane = place("w_plane%d%d" % (side, first), [P, count * P], U8)
-            source = rounded[(side, first // PAIR)][:, first % PAIR : first % PAIR + count]
+            source = rounded[(side, first)][:, :count]
             nc.vector.quantize_mx(
                 out=codes[:].bitcast(FP8X4), scales=plane[:], in_=source.rearrange("p t m j -> p (t m j)")
             )
@@ -157,18 +161,19 @@ def tile_picked_hub_relu_po_kernel(
 
         w3_dealt = {}
 
-        def deal_w3(over=None, skip=0):
-            w3_codes = place("w3_codes", [P, H], I32, over, skip)
-            w3_bytes = place("w3_bytes", [P, H], U8, over, skip + H * PACK)
+        def deal_w3_words(over):
+            w3_dealt["codes"] = place("w3_codes", [P, H], I32, over)
             nc.vector.tensor_copy(
-                w3_codes[:].rearrange("p (t g i) -> p g t i", t=PACK, i=LINE_WORDS),
+                w3_dealt["codes"][:].rearrange("p (t g i) -> p g t i", t=PACK, i=LINE_WORDS),
                 w3_table[:].rearrange("p (g i t) -> p g t i", t=PACK, i=LINE_WORDS),
             )
+
+        def deal_w3_bytes(over):
+            w3_dealt["bytes"] = place("w3_bytes", [P, H], U8, over)
             nc.vector.tensor_copy(
-                w3_bytes[:].rearrange("p (t m) -> p t m", t=PACK), w3_plane[:].rearrange("p (m t) -> p t m", t=PACK)
+                w3_dealt["bytes"][:].rearrange("p (t m) -> p t m", t=PACK),
+                w3_plane[:].rearrange("p (m t) -> p t m", t=PACK),
             )
-            w3_dealt["codes"] = w3_codes
-            w3_dealt["bytes"] = w3_bytes
 
         sources, z_rounded, z_packed, results, accs, out_rounded = {}, {}, {}, {}, {}, {}
         out_codes = {}
@@ -305,22 +310,22 @@ def tile_picked_hub_relu_po_kernel(
 
         nc.vector.tensor_copy(x_bytes[:], x_plane[:].indirect(offs_sb[:]))
         nc.vector.tensor_copy(x_codes[:], x_table[:].bitcast(U32).indirect(offs_sb[:]))
-        round_weight(SOURCE, 0, nc.vector.tensor_copy, slice(0, 80))
-        round_weight(SOURCE, 0, nc.scalar.copy, slice(80, P))
-        round_weight(SOURCE, 1, nc.scalar.copy)
+        round_first_tile()
+        round_weight(SOURCE, 1, PACK - 1)
         quantise_weight(SOURCE, 0, 1)
+        deal_w3_words("w_rounded00")
         quantise_weight(SOURCE, 1, 1, lead=1792, room=2304)
         quantise_weight(SOURCE, 2, 2)
-        deal_w3("w_raw0")
+        deal_w3_bytes("w_raw0")
         for first in range(0, S, 256):
             node_product(SOURCE, 0, first, 256)
         node_tile(SOURCE, 1)
-        round_weight(TARGET, 0, nc.scalar.copy, over="w_codes01", skip=-1792)
+        round_weight(TARGET, 0, PAIR, over="w_codes01", skip=-1792)
         gather_sources((0, 1, 2), 0)
         gather_sources((0, 1, 2), 1)
         quantise_weight(TARGET, 0, 2)
         node_tile(SOURCE, 2)
-        round_weight(TARGET, 1, nc.scalar.copy, over="w_codes01", skip=256)
+        round_weight(TARGET, 2, PAIR, over="w_codes01", skip=256)
         gather_sources((0, 1, 2), 2)
         quantise_weight(TARGET, 2, 2)
         node_tile(SOURCE, 3)
@@ -339,24 +344,25 @@ def tile_picked_hub_relu_po_kernel(
         quantise_z(0)
         edge_product(0)
         relu_round(1)
-        add_targets((2,), (0, 1))
+        add_targets((2,), (0,))
         quantise_z(1)
         edge_product(1)
-        add_targets((2,), (2, 3))
+        add_targets((2,), (1, 2, 3))
         copy_out(0, 0)
         copy_out(0, 1)
         store_out(0, nc.sync)
         round_out(0, 0, nc.scalar.copy)
+        round_out(0, 1, nc.scalar.copy)
         relu_round(2)
-        gather_sources((3, 4), 1, "sources00")
-        gather_sources((3, 4), 2, "sources01")
-        gather_sources((3, 4), 3, "sources02")
+        gather_sources((3, 4), 1, "sources01")
+        gather_sources((3, 4), 2, "sources02")
+        gather_sources((3, 4), 3, "sources01", 1024)
         quantise_z(2)
         edge_product(2)
         copy_out(1, 0)
         copy_out(1, 1)
         store_out(1, nc.sync)
-        round_out(0, 1, nc.scalar.copy)
+        round_out(1, 0, nc.scalar.copy)
         add_targets((3,), every_tile, "sums")
         copy_out(2, 0)
         store_part(2, 0)
@@ -366,7 +372,6 @@ def tile_picked_hub_relu_po_kernel(
         add_targets((4,), every_tile, "sums", 2048)
         quantise_z(3)
         edge_product(3)
-        round_out(1, 0, nc.scalar.copy)
         round_out(1, 1, nc.scalar.copy)
         relu_round(4, "sums3", on_vector=True)
         codes_tile((0,), "sums3", 1024)
@@ -383,12 +388,10 @@ def tile_picked_hub_relu_po_kernel(
         last_product(4)
         store_out(4, nc.sync)
         round_results(3, 0)
-        codes_tile((2,))
+        codes_tile((2, 3, 4))
         quantise_out(2)
-        store_codes((2,))
         round_results(4, 0)
-        codes_tile((3, 4))
         quantise_out(3)
         quantise_out(4)
-        store_codes((3, 4))
+        store_codes((2, 3, 4))
         store_scales((0, 1, 2, 3, 4), (nc.scalar, nc.sync))

@@ -14,6 +14,7 @@ U8 = mybir.dt.uint8
 FP8X4 = mybir.dt.float8_e4m3fn_x4
 WIDTH = {F32: 4, I32: 4, U32: 4, BF16: 2, U8: 1}
 ADD = mybir.AluOpType.add
+MULT = mybir.AluOpType.mult
 RELU = mybir.ActivationFunctionType.Relu
 
 P = 128
@@ -114,7 +115,11 @@ def tile_picked_hub_relu_po_kernel(
         def round_weight(side, first, count, over=None, skip=0):
             dealt = place("w_rounded%d%d" % (side, first), [P, count, P, PACK], BF16, over, skip)
             by_row = w_raw[side][:].rearrange("p j (m t) -> p m j t", t=PACK)
-            nc.scalar.copy(dealt[:].rearrange("p t m j -> p m j t"), by_row[:, :, :, first : first + count])
+            by_tile = dealt[:].rearrange("p t m j -> p m j t")
+            if side == SOURCE:
+                nc.scalar.copy(by_tile, by_row[:, :, :, first : first + count])
+            else:
+                nc.gpsimd.tensor_scalar(by_tile, by_row[:, :, :, first : first + count], 1.0, 0.0, MULT, ADD)
             for u in range(count):
                 rounded[(side, first + u)] = dealt[:, u:]
 
@@ -320,12 +325,12 @@ def tile_picked_hub_relu_po_kernel(
         for first in range(0, S, 256):
             node_product(SOURCE, 0, first, 256)
         node_tile(SOURCE, 1)
-        round_weight(TARGET, 0, PAIR, over="w_codes01", skip=-1792)
+        round_weight(TARGET, 0, PAIR)
         gather_sources((0, 1, 2), 0)
         gather_sources((0, 1, 2), 1)
         quantise_weight(TARGET, 0, 2)
         node_tile(SOURCE, 2)
-        round_weight(TARGET, 2, PAIR, over="w_codes01", skip=256)
+        round_weight(TARGET, 2, PAIR, over="w_rounded10")
         gather_sources((0, 1, 2), 2)
         quantise_weight(TARGET, 2, 2)
         node_tile(SOURCE, 3)

@@ -92,7 +92,8 @@ def tile_picked_hub_relu_po_kernel(
         dst_sb = lists.tile([P, S // LIST_ROWS], U16, name="dst_sb")
         x_table = place("x_table", [P, T], I32)
         x_plane = place("x_plane", [P, T], U8)
-        w_raw = [place("w_raw%d" % side, [P, PACK, H], F32) for side in (SOURCE, TARGET)]
+        w1_raw = [place("w1_raw%d" % half, [P, PACK, H // 2], F32) for half in range(2)]
+        w2_raw = place("w2_raw", [P, PACK, H], F32)
         w3_table = place("w3_table", [P, H], I32)
         w3_plane = place("w3_plane", [P, H], U8)
 
@@ -104,30 +105,35 @@ def tile_picked_hub_relu_po_kernel(
         for q in range(QUADRANTS):
             nc.sync.dma_start(*scale_rows(x_plane, x_scales, q))
         nc.sync.dma_start(x_table[:], as_words(x_words))
-        nc.sync.dma_start(w_raw[SOURCE][:], w1.rearrange("(p j) c -> p j c", j=PACK))
+        for half in range(2):
+            columns = slice(half * H // 2, (half + 1) * H // 2)
+            nc.sync.dma_start(w1_raw[half][:], w1.rearrange("(p j) c -> p j c", j=PACK)[:, :, columns])
         nc.sync.dma_start(w3_table[:], as_words(w3_words))
         for q in range(QUADRANTS):
             nc.sync.dma_start(*scale_rows(w3_plane, w3_scales, q))
-        nc.sync.dma_start(w_raw[TARGET][:], w2.rearrange("(p j) c -> p j c", j=PACK))
+        nc.sync.dma_start(w2_raw[:], w2.rearrange("(p j) c -> p j c", j=PACK))
 
         rounded, weights = {}, {}
 
-        def round_weight(side, first, count, over=None, skip=0):
-            dealt = place("w_rounded%d%d" % (side, first), [P, count, P, PACK], BF16, over, skip)
-            by_row = w_raw[side][:].rearrange("p j (m t) -> p m j t", t=PACK)
-            by_tile = dealt[:].rearrange("p t m j -> p m j t")
-            if side == SOURCE:
-                nc.scalar.copy(by_tile, by_row[:, :, :, first : first + count])
-            else:
-                nc.gpsimd.tensor_scalar(by_tile, by_row[:, :, :, first : first + count], 1.0, 0.0, MULT, ADD)
-            for u in range(count):
-                rounded[(side, first + u)] = dealt[:, u:]
+        first_tile = place("w1_rounded0", [P, 1, P, PACK], BF16, room=H * PACK)
+        other_tiles = place("w1_rounded1", [P, PACK - 1, P, PACK], BF16)
+        rounded[(SOURCE, 0)] = first_tile[:]
+        for u in range(PACK - 1):
+            rounded[(SOURCE, 1 + u)] = other_tiles[:, u:]
 
-        def round_first_tile():
-            dealt = place("w_rounded00", [P, 1, P, PACK], BF16, room=H * PACK)
-            by_row = w_raw[SOURCE][:].rearrange("p j (m t) -> p m j t", t=PACK)
-            nc.vector.tensor_copy(dealt[:, 0], by_row[:, :, :, 0])
-            rounded[(SOURCE, 0)] = dealt[:]
+        def round_w1(half, first, copy):
+            by_row = w1_raw[half][:].rearrange("p j (m t) -> p m j t", t=PACK)
+            m = slice(half * P // 2, (half + 1) * P // 2)
+            if first == 0:
+                copy(first_tile[:, 0, m], by_row[:, :, :, 0])
+            else:
+                copy(other_tiles[:, :, m].rearrange("p t m j -> p m j t"), by_row[:, :, :, 1:])
+
+        def round_w2():
+            dealt = place("w2_rounded", [P, PACK, P, PACK], BF16)
+            columns = w2_raw[:].rearrange("p j (m t) -> p t m j", t=PACK)
+            nc.gpsimd.tensor_scalar(dealt[:], columns, 1.0, 0.0, MULT, ADD)
+            rounded[(TARGET, 0)] = dealt[:]
 
         def quantise_weight(side, first, count, lead=0, room=0):
             codes = place("w_codes%d%d" % (side, first), [P, count * P], U32, lead=lead, room=room)
@@ -185,24 +191,26 @@ def tile_picked_hub_relu_po_kernel(
         out_plane = place("out_plane", [P, S], U8)
         out_rows = out_0.rearrange("(p t) n -> p t n", t=PACK)
 
-        def gather_sources(chunks, t, over=None, skip=0, into=None):
+        def gather_sources(chunks, t, over=None, skip=0, into=None, room=0):
             first, count = span(chunks)
-            picked = place("sources%d%d" % (chunks[0], t), [P, count], F32, over, skip)[:] if into is None else into
+            picked = place("sources%d%d" % (chunks[0], t), [P, count], F32, over, skip, room=room)[:] if into is None else into
             nc.vector.tensor_copy(picked, windows[(SOURCE, t)][:].indirect(entries(src_sb, first, count)))
             for low in range(len(chunks)):
                 for high in range(low + 1, len(chunks) + 1):
                     begin, width = span(chunks[low:high])
                     sources[(chunks[low:high], t)] = picked[:, begin - first : begin - first + width]
 
-        sums_tile = place("sums", [P, PACK, BANK], F32)
-        wide = CHUNKS[0]
-        sums = {(0, 1): sums_tile[:], (0,): sums_tile[:, :, :wide], (1,): sums_tile[:, :, wide:]}
-        sums[(2,)] = sums[(0,)]
+        sums = {}
 
-        def add_targets(chunks, tiles, over=None, skip=0):
+        def sums_tile(chunks, over=None, skip=0):
             first, count = span(chunks)
-            if chunks not in sums:
-                sums[chunks] = place("sums%d" % chunks[0], [P, PACK, count], F32, over, skip)[:]
+            whole = place("sums%d" % chunks[0], [P, PACK, count], F32, over, skip)
+            sums[chunks] = whole[:]
+            for c in chunks:
+                sums[(c,)] = whole[:, :, FIRSTS[c] - first : FIRSTS[c] - first + CHUNKS[c]]
+
+        def add_targets(chunks, tiles):
+            first, count = span(chunks)
             for t in tiles:
                 looked_up = windows[(TARGET, t)][:].indirect(entries(dst_sb, first, count))
                 nc.vector.tensor_tensor(sums[chunks][:, t, :], looked_up, sources[(chunks, t)], ADD)
@@ -226,9 +234,10 @@ def tile_picked_hub_relu_po_kernel(
         def edge_product(c):
             codes, plane = z_packed[c]
             results[c] = place("results%d" % c, [P, PACK, CHUNKS[c]], F32)
-            for part in range(CHUNKS[c] // PART):
-                edges = slice(part * PART, (part + 1) * PART)
-                acc = next_bank([P, PACK, PART])
+            width = min(PART, CHUNKS[c])
+            for part in range(CHUNKS[c] // width):
+                edges = slice(part * width, (part + 1) * width)
+                acc = next_bank([P, PACK, width])
                 for t in range(PACK):
                     cols = slice(t * P, (t + 1) * P)
                     nc.tensor.matmul_mx(
@@ -282,9 +291,15 @@ def tile_picked_hub_relu_po_kernel(
             edges = slice(part * PART, (part + 1) * PART)
             nc.vector.tensor_copy(*interleaved(results[c][:, :, edges], out_rounded[c][:, edges, :]))
 
-        def empty_bank(c, part):
-            copy_out(c, part)
-            round_out(c, part, nc.scalar.copy)
+        def rounded_tile(chunks, over=None, skip=0):
+            first, count = span(chunks)
+            whole = place("out_rounded%d" % chunks[0], [P, count, PACK], BF16, over, skip)
+            for c in chunks:
+                out_rounded[c] = whole[:, FIRSTS[c] - first : FIRSTS[c] - first + CHUNKS[c], :]
+
+        def round_on_gpsimd(c, over=None, skip=0):
+            out_rounded[c] = place("out_rounded%d" % c, [P, CHUNKS[c], PACK], BF16, over, skip)
+            nc.gpsimd.tensor_scalar(out_rounded[c][:], results[c][:].rearrange("p t n -> p n t"), 1.0, -0.0, MULT, ADD)
 
         def codes_tile(chunks, over=None, skip=0):
             first, count = span(chunks)
@@ -315,27 +330,27 @@ def tile_picked_hub_relu_po_kernel(
 
         nc.vector.tensor_copy(x_bytes[:], x_plane[:].indirect(offs_sb[:]))
         nc.vector.tensor_copy(x_codes[:], x_table[:].bitcast(U32).indirect(offs_sb[:]))
-        round_first_tile()
-        round_weight(SOURCE, 1, PACK - 1)
+        round_w1(0, 0, nc.scalar.copy)
+        round_w1(0, 1, nc.scalar.copy)
+        round_w1(1, 0, nc.vector.tensor_copy)
+        round_w1(1, 1, nc.scalar.copy)
         quantise_weight(SOURCE, 0, 1)
-        deal_w3_words("w_rounded00")
-        quantise_weight(SOURCE, 1, 1, lead=1792, room=2304)
+        deal_w3_words("w1_rounded0")
+        quantise_weight(SOURCE, 1, 1)
         quantise_weight(SOURCE, 2, 2)
-        deal_w3_bytes("w_raw0")
+        deal_w3_bytes("w1_raw1")
         for first in range(0, S, 256):
             node_product(SOURCE, 0, first, 256)
-        node_tile(SOURCE, 1)
-        round_weight(TARGET, 0, PAIR)
-        gather_sources((0, 1, 2), 0)
-        gather_sources((0, 1, 2), 1)
-        quantise_weight(TARGET, 0, 2)
-        node_tile(SOURCE, 2)
-        round_weight(TARGET, 2, PAIR, over="w_rounded10")
-        gather_sources((0, 1, 2), 2)
-        quantise_weight(TARGET, 2, 2)
-        node_tile(SOURCE, 3)
-        gather_sources((0,), 3)
-        gather_sources((1,), 3)
+        round_w2()
+        for t in range(1, PACK):
+            node_tile(SOURCE, t)
+        sums_tile((0, 1))
+        sums[(2,)] = sums[(1,)]
+        gather_sources((0, 1, 2), 0, room=4096)
+        gather_sources((0, 1), 1)
+        quantise_weight(TARGET, 0, PACK)
+        gather_sources((0, 1), 2, "w2_raw")
+        gather_sources((0, 1, 2), 3, "w2_raw", 2048)
         for t in range(PACK - 1):
             node_tile(TARGET, t)
             add_targets((0, 1), (t,))
@@ -344,40 +359,43 @@ def tile_picked_hub_relu_po_kernel(
         add_targets((1,), (3,))
 
         relu_round(0)
-        gather_sources((2,), 3, "sources03")
-        gather_sources((3, 4), 0, "sources13")
+        gather_sources((2,), 1, into=sources[((0,), 3)])
+        gather_sources((2,), 2, into=sources[((1,), 3)])
         quantise_z(0)
         edge_product(0)
         relu_round(1)
-        add_targets((2,), (0,))
+        gather_sources((3, 4), 0, "z_rounded0")
         quantise_z(1)
         edge_product(1)
-        add_targets((2,), (1, 2, 3))
+        add_targets((2,), (1, 2, 3, 0))
         copy_out(0, 0)
         copy_out(0, 1)
         store_out(0, nc.sync)
-        round_out(0, 0, nc.scalar.copy)
-        round_out(0, 1, nc.scalar.copy)
-        relu_round(2)
-        gather_sources((3, 4), 1, "sources01")
-        gather_sources((3, 4), 2, "sources02")
-        gather_sources((3, 4), 3, "sources01", 1024)
-        quantise_z(2)
-        edge_product(2)
         copy_out(1, 0)
         copy_out(1, 1)
         store_out(1, nc.sync)
+        relu_round(2)
+        gather_sources((3, 4), 1, into=sources[((2,), 1)])
+        gather_sources((3, 4), 2, into=sources[((2,), 2)])
+        gather_sources((3, 4), 3, into=sources[((2,), 3)])
+        quantise_z(2)
+        edge_product(2)
+        round_on_gpsimd(0, "sources00")
+        rounded_tile((1,), "sources00", 2048)
         round_out(1, 0, nc.scalar.copy)
-        add_targets((3,), every_tile, "sums")
+        round_out(1, 1, nc.scalar.copy)
+        sums_tile((3,), "sums0")
+        sums_tile((4,), "sums0", 3072)
+        add_targets((3,), every_tile)
         copy_out(2, 0)
         store_part(2, 0)
         relu_round(3, room=2048)
         copy_out(2, 1)
         store_part(2, 1)
-        add_targets((4,), every_tile, "sums", 2048)
+        add_targets((4,), every_tile)
         quantise_z(3)
         edge_product(3)
-        round_out(1, 1, nc.scalar.copy)
+        round_out(2, 0, nc.scalar.copy)
         relu_round(4, "sums3", on_vector=True)
         codes_tile((0,), "sums3", 1024)
         quantise_out(0)
@@ -385,18 +403,17 @@ def tile_picked_hub_relu_po_kernel(
         quantise_z(4)
         copy_out(3, 0)
         store_out(3, nc.sync)
-        round_results(2, 0, "z_rounded3")
-        codes_tile((1,))
-        quantise_out(1)
-        store_codes((1,))
         round_results(2, 1)
+        codes_tile((1, 2), "z_rounded3")
+        quantise_out(1)
         last_product(4)
         store_out(4, nc.sync)
-        round_results(3, 0)
-        codes_tile((2, 3, 4))
         quantise_out(2)
+        store_codes((1, 2))
+        round_results(3, 0)
         round_results(4, 0)
+        codes_tile((3, 4))
         quantise_out(3)
         quantise_out(4)
-        store_codes((2, 3, 4))
+        store_codes((3, 4))
         store_scales((0, 1, 2, 3, 4), (nc.scalar, nc.sync))

@@ -21,9 +21,12 @@ P = 128
 PACK = 4
 PAIR = 2
 QUADRANTS = 4
+QUADRANT = P // QUADRANTS
 BANK = 512
 BANKS = 8
 PART = BANK // PACK
+PIECE = BANK // 2
+QUARTER = S // PACK
 LIST_ROWS = 16
 LINE_COLUMNS = 2
 LINE_WORDS = 4
@@ -31,11 +34,10 @@ ALIGN = 64
 SOURCE, TARGET = 0, 1
 CHUNKS = (256, 256, 256, 128, 128)
 FIRSTS = [sum(CHUNKS[:c]) for c in range(len(CHUNKS))]
-LAST = len(CHUNKS) - 1
 
 
 def scale_rows(plane, scales, r):
-    return plane[r:P:32, :].bitcast(I32), scales[0, r::QUADRANTS, :].bitcast(I32)
+    return plane[r:P:QUADRANT, :].bitcast(I32), scales[0, r::QUADRANTS, :].bitcast(I32)
 
 
 def as_words(packed):
@@ -69,9 +71,9 @@ def tile_picked_hub_relu_po_kernel(
         starts = {}
         used = [0]
 
-        def place(name, shape, dtype, over=None, skip=0, lead=0, room=0):
+        def place(name, shape, dtype, over=None, skip=0, room=0):
             if over is None:
-                starts[name] = used[0] + lead
+                starts[name] = used[0]
                 size = WIDTH[dtype]
                 for extent in shape[1:]:
                     size = size * extent
@@ -92,9 +94,9 @@ def tile_picked_hub_relu_po_kernel(
         dst_sb = lists.tile([P, S // LIST_ROWS], U16, name="dst_sb")
         x_table = place("x_table", [P, T], I32)
         x_plane = place("x_plane", [P, T], U8)
-        w1_raw = [place("w1_raw%d" % half, [P, PACK, H // 2], F32) for half in range(2)]
+        w1_raw = place("w1_raw", [P, PACK, H], F32)
         w2_raw = place("w2_raw", [P, PACK, H], F32)
-        w3_table = place("w3_table", [P, H], I32)
+        w3_table = place("w3_table", [P, H], I32, room=PACK * H * WIDTH[BF16])
         w3_plane = place("w3_plane", [P, H], U8)
 
         nc.vector.memset(x_plane[:].bitcast(I32), 0)
@@ -105,38 +107,32 @@ def tile_picked_hub_relu_po_kernel(
         for q in range(QUADRANTS):
             nc.sync.dma_start(*scale_rows(x_plane, x_scales, q))
         nc.sync.dma_start(x_table[:], as_words(x_words))
-        for half in range(2):
-            columns = slice(half * H // 2, (half + 1) * H // 2)
-            nc.sync.dma_start(w1_raw[half][:], w1.rearrange("(p j) c -> p j c", j=PACK)[:, :, columns])
+        nc.sync.dma_start(w1_raw[:], w1.rearrange("(p j) c -> p j c", j=PACK))
         nc.sync.dma_start(w3_table[:], as_words(w3_words))
+        nc.sync.dma_start(w2_raw[:], w2.rearrange("(p j) c -> p j c", j=PACK))
         for q in range(QUADRANTS):
             nc.sync.dma_start(*scale_rows(w3_plane, w3_scales, q))
-        nc.sync.dma_start(w2_raw[:], w2.rearrange("(p j) c -> p j c", j=PACK))
 
         rounded, weights = {}, {}
 
-        first_tile = place("w1_rounded0", [P, 1, P, PACK], BF16, room=H * PACK)
-        other_tiles = place("w1_rounded1", [P, PACK - 1, P, PACK], BF16)
-        rounded[(SOURCE, 0)] = first_tile[:]
-        for u in range(PACK - 1):
-            rounded[(SOURCE, 1 + u)] = other_tiles[:, u:]
+        def w1_tile(t, count, over=None, room=0):
+            dealt = place("w1_rounded%d" % t, [P, count, P, PACK], BF16, over, room=room)
+            rounded[(SOURCE, t)] = dealt[:]
+            return dealt[:].rearrange("p t m j -> p m j t")
 
-        def round_w1(half, first, copy):
-            by_row = w1_raw[half][:].rearrange("p j (m t) -> p m j t", t=PACK)
-            m = slice(half * P // 2, (half + 1) * P // 2)
-            if first == 0:
-                copy(first_tile[:, 0, m], by_row[:, :, :, 0])
-            else:
-                copy(other_tiles[:, :, m].rearrange("p t m j -> p m j t"), by_row[:, :, :, 1:])
+        w1_columns = w1_raw[:].rearrange("p j (m t) -> p m j t", t=PACK)
 
-        def round_w2():
-            dealt = place("w2_rounded", [P, PACK, P, PACK], BF16)
-            columns = w2_raw[:].rearrange("p j (m t) -> p t m j", t=PACK)
-            nc.gpsimd.tensor_scalar(dealt[:], columns, 1.0, 0.0, MULT, ADD)
+        def round_w2(over):
+            dealt = place("w2_rounded", [P, PACK, P, PACK], BF16, over)
+            by_row = w2_raw[:].rearrange("p j (m t) -> p m j t", t=PACK)
+            by_tile = dealt[:].rearrange("p t m j -> p m j t")
+            for first in range(0, PACK, PAIR):
+                tiles = slice(first, first + PAIR)
+                nc.gpsimd.tensor_scalar(by_tile[:, :, :, tiles], by_row[:, :, :, tiles], 1.0, 0.0, MULT, ADD)
             rounded[(TARGET, 0)] = dealt[:]
 
-        def quantise_weight(side, first, count, lead=0, room=0):
-            codes = place("w_codes%d%d" % (side, first), [P, count * P], U32, lead=lead, room=room)
+        def quantise_weight(side, first, count):
+            codes = place("w_codes%d%d" % (side, first), [P, count * P], U32)
             plane = place("w_plane%d%d" % (side, first), [P, count * P], U8)
             source = rounded[(side, first)][:, :count]
             nc.vector.quantize_mx(
@@ -149,26 +145,22 @@ def tile_picked_hub_relu_po_kernel(
         x_bytes = place("x_bytes", [P, S], U8)
         windows = {}
 
-        def node_product(side, t, first, count, copy=nc.scalar.copy):
+        def node_tile(side, t, width=BANK):
             codes, plane = weights[(side, t)]
-            if (side, t) not in windows:
-                windows[(side, t)] = place("window%d%d" % (side, t), [P, S], F32)
-            nodes = slice(first, first + count)
-            acc = next_bank([P, count])
-            nc.tensor.matmul_mx(
-                out=acc[:],
-                lhsT=codes.bitcast(FP8X4),
-                lhsT_scale=plane,
-                rhs=x_codes[:, nodes].bitcast(FP8X4),
-                rhs_scale=x_bytes[:, nodes],
-                start=True,
-                stop=True,
-            )
-            copy(windows[(side, t)][:, nodes], acc[:])
-
-        def node_tile(side, t):
-            for first in range(0, S, BANK):
-                node_product(side, t, first, BANK)
+            windows[(side, t)] = place("window%d%d" % (side, t), [P, S], F32)
+            for first in range(0, S, width):
+                nodes = slice(first, first + width)
+                acc = next_bank([P, width])
+                nc.tensor.matmul_mx(
+                    out=acc[:],
+                    lhsT=codes.bitcast(FP8X4),
+                    lhsT_scale=plane,
+                    rhs=x_codes[:, nodes].bitcast(FP8X4),
+                    rhs_scale=x_bytes[:, nodes],
+                    start=True,
+                    stop=True,
+                )
+                nc.scalar.copy(windows[(side, t)][:, nodes], acc[:])
 
         w3_dealt = {}
 
@@ -181,26 +173,26 @@ def tile_picked_hub_relu_po_kernel(
 
         def deal_w3_bytes(over):
             w3_dealt["bytes"] = place("w3_bytes", [P, H], U8, over)
-            nc.vector.tensor_copy(
-                w3_dealt["bytes"][:].rearrange("p (t m) -> p t m", t=PACK),
-                w3_plane[:].rearrange("p (m t) -> p t m", t=PACK),
-            )
+            by_tile = w3_dealt["bytes"][:].rearrange("p (t m) -> p t m", t=PACK)
+            by_column = w3_plane[:].rearrange("p (m t) -> p t m", t=PACK)
+            nc.gpsimd.tensor_copy(by_tile[:, PAIR:], by_column[:, PAIR:])
+            nc.vector.tensor_copy(by_tile[:, :PAIR], by_column[:, :PAIR])
 
-        sources, z_rounded, z_packed, results, accs, out_rounded = {}, {}, {}, {}, {}, {}
-        out_codes = {}
-        out_plane = place("out_plane", [P, S], U8)
+        sources, sums, z_rounded, z_packed = {}, {}, {}, {}
+        accs, results, out_rounded, out_codes = {}, {}, {}, {}
+        out_plane = place("out_plane", [P, QUARTER], U8)
         out_rows = out_0.rearrange("(p t) n -> p t n", t=PACK)
 
-        def gather_sources(chunks, t, over=None, skip=0, into=None, room=0):
+        def sources_tile(chunks, t, over=None, skip=0, room=0):
+            return place("sources%d%d" % (chunks[0], t), [P, span(chunks)[1]], F32, over, skip, room)[:]
+
+        def gather_sources(chunks, t, picked):
             first, count = span(chunks)
-            picked = place("sources%d%d" % (chunks[0], t), [P, count], F32, over, skip, room=room)[:] if into is None else into
             nc.vector.tensor_copy(picked, windows[(SOURCE, t)][:].indirect(entries(src_sb, first, count)))
             for low in range(len(chunks)):
                 for high in range(low + 1, len(chunks) + 1):
                     begin, width = span(chunks[low:high])
                     sources[(chunks[low:high], t)] = picked[:, begin - first : begin - first + width]
-
-        sums = {}
 
         def sums_tile(chunks, over=None, skip=0):
             first, count = span(chunks)
@@ -215,81 +207,60 @@ def tile_picked_hub_relu_po_kernel(
                 looked_up = windows[(TARGET, t)][:].indirect(entries(dst_sb, first, count))
                 nc.vector.tensor_tensor(sums[chunks][:, t, :], looked_up, sources[(chunks, t)], ADD)
 
-        def relu_round(c, over=None, on_vector=False, room=0):
-            z_rounded[c] = place("z_rounded%d" % c, [P, CHUNKS[c], PACK], BF16, over, room=room)
+        def relu_round(c, over=None, on_vector=False):
+            z_rounded[c] = place("z_rounded%d" % c, [P, CHUNKS[c], PACK], BF16, over)
             by_column, by_tile = interleaved(sums[(c,)], z_rounded[c][:])
             if on_vector:
                 nc.vector.tensor_scalar_max(by_column, by_tile, 0.0)
             else:
                 nc.scalar.activation(by_column, by_tile, RELU)
 
-        def quantise_z(c, room=0):
-            codes = place("z_codes%d" % c, [P, CHUNKS[c]], U32, room=room)
+        def quantise_z(c):
+            codes = place("z_codes%d" % c, [P, CHUNKS[c]], U32)
             plane = place("z_plane%d" % c, [P, CHUNKS[c]], U8)
             nc.vector.quantize_mx(
                 out=codes[:].bitcast(FP8X4), scales=plane[:], in_=z_rounded[c][:].rearrange("p n t -> p (n t)")
             )
             z_packed[c] = (codes, plane)
 
-        def edge_product(c):
+        def w3_product(acc, t, c, edges):
             codes, plane = z_packed[c]
-            results[c] = place("results%d" % c, [P, PACK, CHUNKS[c]], F32)
-            width = min(PART, CHUNKS[c])
-            for part in range(CHUNKS[c] // width):
-                edges = slice(part * width, (part + 1) * width)
-                acc = next_bank([P, PACK, width])
+            columns = slice(t * P, (t + 1) * P)
+            nc.tensor.matmul_mx(
+                out=acc,
+                lhsT=w3_dealt["codes"][:, columns].bitcast(FP8X4),
+                lhsT_scale=w3_dealt["bytes"][:, columns],
+                rhs=codes[:, edges].bitcast(FP8X4),
+                rhs_scale=plane[:, edges],
+                start=True,
+                stop=True,
+            )
+
+        def edge_product(c):
+            for part in range(CHUNKS[c] // PART):
+                accs[(c, part)] = next_bank([P, PACK, PART])
                 for t in range(PACK):
-                    cols = slice(t * P, (t + 1) * P)
-                    nc.tensor.matmul_mx(
-                        out=acc[:, t, :],
-                        lhsT=w3_dealt["codes"][:, cols].bitcast(FP8X4),
-                        lhsT_scale=w3_dealt["bytes"][:, cols],
-                        rhs=codes[:, edges].bitcast(FP8X4),
-                        rhs_scale=plane[:, edges],
-                        start=True,
-                        stop=True,
-                    )
-                accs[(c, part)] = acc
+                    w3_product(accs[(c, part)][:, t, :], t, c, slice(part * PART, (part + 1) * PART))
 
-        def copy_out(c, part):
-            nc.scalar.copy(results[c][:, :, part * PART : (part + 1) * PART], accs[(c, part)][:])
+        def store_results(first, held):
+            nc.sync.dma_start(out_rows[:, :, first : first + held.shape[2]], held)
 
-        def store_out(c, queue):
-            queue.dma_start(out_rows[:, :, FIRSTS[c] : FIRSTS[c] + CHUNKS[c]], results[c][:])
-
-        def store_part(c, part):
-            first = FIRSTS[c] + part * PART
-            nc.sync.dma_start(out_rows[:, :, first : first + PART], results[c][:, :, part * PART : (part + 1) * PART])
-
-        def round_out(c, part, copy):
-            if c not in out_rounded:
-                out_rounded[c] = place("out_rounded%d" % c, [P, CHUNKS[c], PACK], BF16)
-            copy(*interleaved(accs[(c, part)][:], out_rounded[c][:, part * PART : (part + 1) * PART, :]))
+        def copy_out(c, parts):
+            held = place("results%d%d" % (c, parts[0]), [P, PACK, len(parts) * PART], F32)
+            for u, part in enumerate(parts):
+                nc.scalar.copy(held[:, :, u * PART : (u + 1) * PART], accs[(c, part)][:])
+            results[(c, parts)] = held[:]
+            store_results(FIRSTS[c] + parts[0] * PART, held[:])
 
         def last_product(c):
-            codes, plane = z_packed[c]
-            results[c] = place("results%d" % c, [P, PACK, CHUNKS[c]], F32)
-            for pair in range(PACK // PAIR):
-                acc = next_bank([P, PAIR, CHUNKS[c]])
+            held = place("results%d0" % c, [P, PACK, PART], F32)
+            for first in range(0, PACK, PAIR):
+                acc = next_bank([P, PAIR, PART])
                 for u in range(PAIR):
-                    cols = slice((PAIR * pair + u) * P, (PAIR * pair + u + 1) * P)
-                    nc.tensor.matmul_mx(
-                        out=acc[:, u, :],
-                        lhsT=w3_dealt["codes"][:, cols].bitcast(FP8X4),
-                        lhsT_scale=w3_dealt["bytes"][:, cols],
-                        rhs=codes[:].bitcast(FP8X4),
-                        rhs_scale=plane[:],
-                        start=True,
-                        stop=True,
-                    )
-                tiles = slice(PAIR * pair, PAIR * (pair + 1))
-                nc.scalar.copy(results[c][:, tiles, :], acc[:])
-
-        def round_results(c, part, over=None):
-            if c not in out_rounded:
-                out_rounded[c] = place("out_rounded%d" % c, [P, CHUNKS[c], PACK], BF16, over)
-            edges = slice(part * PART, (part + 1) * PART)
-            nc.vector.tensor_copy(*interleaved(results[c][:, :, edges], out_rounded[c][:, edges, :]))
+                    w3_product(acc[:, u, :], first + u, c, slice(0, PART))
+                nc.scalar.copy(held[:, first : first + PAIR, :], acc[:])
+            results[(c, (0,))] = held[:]
+            store_results(FIRSTS[c], held[:])
 
         def rounded_tile(chunks, over=None, skip=0):
             first, count = span(chunks)
@@ -297,9 +268,16 @@ def tile_picked_hub_relu_po_kernel(
             for c in chunks:
                 out_rounded[c] = whole[:, FIRSTS[c] - first : FIRSTS[c] - first + CHUNKS[c], :]
 
-        def round_on_gpsimd(c, over=None, skip=0):
-            out_rounded[c] = place("out_rounded%d" % c, [P, CHUNKS[c], PACK], BF16, over, skip)
-            nc.gpsimd.tensor_scalar(out_rounded[c][:], results[c][:].rearrange("p t n -> p n t"), 1.0, -0.0, MULT, ADD)
+        def round_from_bank(c, part):
+            nc.scalar.copy(*interleaved(accs[(c, part)][:], out_rounded[c][:, part * PART : (part + 1) * PART, :]))
+
+        def round_on_vector(c, part):
+            edges = slice(part * PART, (part + 1) * PART)
+            nc.vector.tensor_copy(*interleaved(results[(c, (part,))], out_rounded[c][:, edges, :]))
+
+        def round_on_gpsimd(c, parts):
+            by_column = results[(c, parts)].rearrange("p t n -> p n t")
+            nc.gpsimd.tensor_scalar(out_rounded[c], by_column, 1.0, -0.0, MULT, ADD)
 
         def codes_tile(chunks, over=None, skip=0):
             first, count = span(chunks)
@@ -309,49 +287,54 @@ def tile_picked_hub_relu_po_kernel(
                 out_codes[(c,)] = codes[:, FIRSTS[c] - first : FIRSTS[c] - first + CHUNKS[c]]
 
         def quantise_out(c):
+            quarter, first = divmod(FIRSTS[c], QUARTER)
             nc.vector.quantize_mx(
                 out=out_codes[(c,)].bitcast(FP8X4),
-                scales=out_plane[:, FIRSTS[c] : FIRSTS[c] + CHUNKS[c]],
-                in_=out_rounded[c][:].rearrange("p n t -> p (n t)"),
+                scales=out_plane[PACK * quarter :, first : first + CHUNKS[c]],
+                in_=out_rounded[c].rearrange("p n t -> p (n t)"),
             )
-
-        def store_scales(chunks, queues):
-            first, count = span(chunks)
-            words = slice(first // PACK, (first + count) // PACK)
-            for q in range(QUADRANTS):
-                in_plane, in_dram = scale_rows(out_plane, out_2, q)
-                queues[q % len(queues)].dma_start(in_dram[:, words], in_plane[:, words])
 
         def store_codes(chunks):
             first, count = span(chunks)
             nc.sync.dma_start(as_words(out_1)[:, first : first + count], out_codes[chunks].bitcast(I32))
 
+        def store_scales(queues):
+            for q in range(QUADRANTS):
+                rows = out_2[0, PACK * q : PACK * (q + 1), :].rearrange("r (a n) -> a r n", n=QUARTER)
+                live = out_plane[QUADRANT * q : QUADRANT * q + PACK * PACK, :]
+                queues[q % len(queues)].dma_start(rows.bitcast(I32), live.bitcast(I32))
+
         every_tile = range(PACK)
+        part_bytes = PACK * PART * WIDTH[F32]
 
         nc.vector.tensor_copy(x_bytes[:], x_plane[:].indirect(offs_sb[:]))
         nc.vector.tensor_copy(x_codes[:], x_table[:].bitcast(U32).indirect(offs_sb[:]))
-        round_w1(0, 0, nc.scalar.copy)
-        round_w1(0, 1, nc.scalar.copy)
-        round_w1(1, 0, nc.vector.tensor_copy)
-        round_w1(1, 1, nc.scalar.copy)
+
+        tile0, last_pair = w1_tile(0, 1, room=H * WIDTH[I32]), w1_tile(PAIR, PAIR)
+        half = P // 2
+        nc.scalar.copy(tile0[:, half:, :, 0], w1_columns[:, half:, :, 0])
+        nc.vector.tensor_copy(tile0[:, :half, :, 0], w1_columns[:, :half, :, 0])
+        nc.scalar.copy(last_pair, w1_columns[:, :, :, PAIR:])
         quantise_weight(SOURCE, 0, 1)
-        deal_w3_words("w1_rounded0")
+        nc.vector.tensor_copy(w1_tile(1, 1, "w1_rounded0")[:, :, :, 0], w1_columns[:, :, :, 1])
         quantise_weight(SOURCE, 1, 1)
-        quantise_weight(SOURCE, 2, 2)
-        deal_w3_bytes("w1_raw1")
-        for first in range(0, S, 256):
-            node_product(SOURCE, 0, first, 256)
-        round_w2()
+        quantise_weight(SOURCE, PAIR, PAIR)
+        deal_w3_words("w1_rounded1")
+        node_tile(SOURCE, 0, PIECE)
+        round_w2("w3_table")
         for t in range(1, PACK):
             node_tile(SOURCE, t)
+
         sums_tile((0, 1))
-        sums[(2,)] = sums[(1,)]
-        gather_sources((0, 1, 2), 0, room=4096)
-        gather_sources((0, 1), 1)
+        gather_sources((0, 1, 2), 0, sources_tile((0, 1, 2), 0))
+        gather_sources((0, 1, 2), 1, sources_tile((0, 1, 2), 1, room=2 * part_bytes))
         quantise_weight(TARGET, 0, PACK)
-        gather_sources((0, 1), 2, "w2_raw")
-        gather_sources((0, 1, 2), 3, "w2_raw", 2048)
-        for t in range(PACK - 1):
+        gather_sources((0, 1), 2, sources_tile((0, 1), 2, "w2_raw"))
+        gather_sources((0, 1), 3, sources_tile((0, 1), 3, "w2_raw", part_bytes))
+        deal_w3_bytes("w2_rounded")
+        node_tile(TARGET, 0, PIECE)
+        add_targets((0, 1), (0,))
+        for t in (1, 2):
             node_tile(TARGET, t)
             add_targets((0, 1), (t,))
         node_tile(TARGET, 3)
@@ -359,61 +342,59 @@ def tile_picked_hub_relu_po_kernel(
         add_targets((1,), (3,))
 
         relu_round(0)
-        gather_sources((2,), 1, into=sources[((0,), 3)])
-        gather_sources((2,), 2, into=sources[((1,), 3)])
+        gather_sources((2,), 2, sources[((0,), 3)])
+        gather_sources((2,), 3, sources[((1,), 3)])
         quantise_z(0)
         edge_product(0)
         relu_round(1)
-        gather_sources((3, 4), 0, "z_rounded0")
+        sums[(2,)] = sums[(0,)]
+        add_targets((2,), (0,))
         quantise_z(1)
         edge_product(1)
-        add_targets((2,), (1, 2, 3, 0))
-        copy_out(0, 0)
-        copy_out(0, 1)
-        store_out(0, nc.sync)
-        copy_out(1, 0)
-        copy_out(1, 1)
-        store_out(1, nc.sync)
+        add_targets((2,), (2, 3, 1))
+        copy_out(0, (0, 1))
+        copy_out(1, (0, 1))
+
         relu_round(2)
-        gather_sources((3, 4), 1, into=sources[((2,), 1)])
-        gather_sources((3, 4), 2, into=sources[((2,), 2)])
-        gather_sources((3, 4), 3, into=sources[((2,), 3)])
+        for t in (0, 1):
+            gather_sources((3, 4), t, sources_tile((3, 4), t, "z_rounded1", t * part_bytes // 2))
+        for t in (2, 3):
+            gather_sources((3, 4), t, sources[((2,), t)])
         quantise_z(2)
         edge_product(2)
-        round_on_gpsimd(0, "sources00")
-        rounded_tile((1,), "sources00", 2048)
-        round_out(1, 0, nc.scalar.copy)
-        round_out(1, 1, nc.scalar.copy)
+        rounded_tile((0, 1), "sources01")
+        round_on_gpsimd(0, (0, 1))
+        round_from_bank(1, 0)
+        round_from_bank(1, 1)
         sums_tile((3,), "sums0")
-        sums_tile((4,), "sums0", 3072)
+        sums_tile((4,), "sums0", 2 * part_bytes)
         add_targets((3,), every_tile)
-        copy_out(2, 0)
-        store_part(2, 0)
-        relu_round(3, room=2048)
-        copy_out(2, 1)
-        store_part(2, 1)
+        copy_out(2, (0,))
+        relu_round(3)
+        copy_out(2, (1,))
         add_targets((4,), every_tile)
+
         quantise_z(3)
         edge_product(3)
-        round_out(2, 0, nc.scalar.copy)
+        rounded_tile((2,))
+        round_from_bank(2, 0)
         relu_round(4, "sums3", on_vector=True)
-        codes_tile((0,), "sums3", 1024)
+        codes_tile((0,), "sums3", part_bytes // 2)
         quantise_out(0)
         store_codes((0,))
         quantise_z(4)
-        copy_out(3, 0)
-        store_out(3, nc.sync)
-        round_results(2, 1)
-        codes_tile((1, 2), "z_rounded3")
+        copy_out(3, (0,))
+        codes_tile((1,), "z_rounded3")
         quantise_out(1)
+        store_codes((1,))
+        round_on_vector(2, 1)
         last_product(4)
-        store_out(4, nc.sync)
+        codes_tile((2, 3, 4))
         quantise_out(2)
-        store_codes((1, 2))
-        round_results(3, 0)
-        round_results(4, 0)
-        codes_tile((3, 4))
+        for c in (3, 4):
+            rounded_tile((c,))
+            round_on_vector(c, 0)
         quantise_out(3)
         quantise_out(4)
-        store_codes((3, 4))
-        store_scales((0, 1, 2, 3, 4), (nc.scalar, nc.sync))
+        store_codes((2, 3, 4))
+        store_scales((nc.scalar, nc.sync))

@@ -14,8 +14,8 @@ U8 = mybir.dt.uint8
 FP8X4 = mybir.dt.float8_e4m3fn_x4
 WIDTH = {F32: 4, I32: 4, U32: 4, BF16: 2, U8: 1}
 ADD = mybir.AluOpType.add
-MULT = mybir.AluOpType.mult
 RELU = mybir.ActivationFunctionType.Relu
+COPY = mybir.ActivationFunctionType.Copy
 
 P = 128
 PACK = 4
@@ -108,8 +108,8 @@ def tile_picked_hub_relu_po_kernel(
             nc.sync.dma_start(*scale_rows(x_plane, x_scales, q))
         nc.sync.dma_start(x_table[:], as_words(x_words))
         nc.sync.dma_start(w1_raw[:], w1.rearrange("(p j) c -> p j c", j=PACK))
-        nc.sync.dma_start(w3_table[:], as_words(w3_words))
         nc.sync.dma_start(w2_raw[:], w2.rearrange("(p j) c -> p j c", j=PACK))
+        nc.sync.dma_start(w3_table[:], as_words(w3_words))
         for q in range(QUADRANTS):
             nc.sync.dma_start(*scale_rows(w3_plane, w3_scales, q))
 
@@ -122,14 +122,11 @@ def tile_picked_hub_relu_po_kernel(
 
         w1_columns = w1_raw[:].rearrange("p j (m t) -> p m j t", t=PACK)
 
-        def round_w2(over):
-            dealt = place("w2_rounded", [P, PACK, P, PACK], BF16, over)
+        def round_w2(first, over=None):
+            dealt = place("w2_rounded%d" % first, [P, PAIR, P, PACK], BF16, over)
             by_row = w2_raw[:].rearrange("p j (m t) -> p m j t", t=PACK)
-            by_tile = dealt[:].rearrange("p t m j -> p m j t")
-            for first in range(0, PACK, PAIR):
-                tiles = slice(first, first + PAIR)
-                nc.gpsimd.tensor_scalar(by_tile[:, :, :, tiles], by_row[:, :, :, tiles], 1.0, 0.0, MULT, ADD)
-            rounded[(TARGET, 0)] = dealt[:]
+            nc.vector.tensor_copy(dealt[:].rearrange("p t m j -> p m j t"), by_row[:, :, :, first : first + PAIR])
+            rounded[(TARGET, first)] = dealt[:]
 
         def quantise_weight(side, first, count):
             codes = place("w_codes%d%d" % (side, first), [P, count * P], U32)
@@ -145,9 +142,9 @@ def tile_picked_hub_relu_po_kernel(
         x_bytes = place("x_bytes", [P, S], U8)
         windows = {}
 
-        def node_tile(side, t, width=BANK):
+        def node_tile(side, t, width=BANK, on_vector=False, over=None):
             codes, plane = weights[(side, t)]
-            windows[(side, t)] = place("window%d%d" % (side, t), [P, S], F32)
+            windows[(side, t)] = place("window%d%d" % (side, t), [P, S], F32, over)
             for first in range(0, S, width):
                 nodes = slice(first, first + width)
                 acc = next_bank([P, width])
@@ -160,7 +157,10 @@ def tile_picked_hub_relu_po_kernel(
                     start=True,
                     stop=True,
                 )
-                nc.scalar.copy(windows[(side, t)][:, nodes], acc[:])
+                if on_vector:
+                    nc.vector.tensor_copy(windows[(side, t)][:, nodes], acc[:])
+                else:
+                    nc.scalar.copy(windows[(side, t)][:, nodes], acc[:])
 
         w3_dealt = {}
 
@@ -174,9 +174,7 @@ def tile_picked_hub_relu_po_kernel(
         def deal_w3_bytes(over):
             w3_dealt["bytes"] = place("w3_bytes", [P, H], U8, over)
             by_tile = w3_dealt["bytes"][:].rearrange("p (t m) -> p t m", t=PACK)
-            by_column = w3_plane[:].rearrange("p (m t) -> p t m", t=PACK)
-            nc.gpsimd.tensor_copy(by_tile[:, PAIR:], by_column[:, PAIR:])
-            nc.vector.tensor_copy(by_tile[:, :PAIR], by_column[:, :PAIR])
+            nc.vector.tensor_copy(by_tile, w3_plane[:].rearrange("p (m t) -> p t m", t=PACK))
 
         sources, sums, z_rounded, z_packed = {}, {}, {}, {}
         accs, results, out_rounded, out_codes = {}, {}, {}, {}
@@ -186,9 +184,13 @@ def tile_picked_hub_relu_po_kernel(
         def sources_tile(chunks, t, over=None, skip=0, room=0):
             return place("sources%d%d" % (chunks[0], t), [P, span(chunks)[1]], F32, over, skip, room)[:]
 
-        def gather_sources(chunks, t, picked):
+        def gather_sources(chunks, t, picked, on_vector=False):
             first, count = span(chunks)
-            nc.vector.tensor_copy(picked, windows[(SOURCE, t)][:].indirect(entries(src_sb, first, count)))
+            looked_up = windows[(SOURCE, t)][:].indirect(entries(src_sb, first, count))
+            if on_vector:
+                nc.vector.tensor_copy(picked, looked_up)
+            else:
+                nc.scalar.activation(picked, looked_up, COPY)
             for low in range(len(chunks)):
                 for high in range(low + 1, len(chunks) + 1):
                     begin, width = span(chunks[low:high])
@@ -271,13 +273,9 @@ def tile_picked_hub_relu_po_kernel(
         def round_from_bank(c, part):
             nc.scalar.copy(*interleaved(accs[(c, part)][:], out_rounded[c][:, part * PART : (part + 1) * PART, :]))
 
-        def round_on_vector(c, part):
-            edges = slice(part * PART, (part + 1) * PART)
-            nc.vector.tensor_copy(*interleaved(results[(c, (part,))], out_rounded[c][:, edges, :]))
-
-        def round_on_gpsimd(c, parts):
-            by_column = results[(c, parts)].rearrange("p t n -> p n t")
-            nc.gpsimd.tensor_scalar(out_rounded[c], by_column, 1.0, -0.0, MULT, ADD)
+        def round_on_vector(c, parts):
+            edges = slice(parts[0] * PART, (parts[-1] + 1) * PART)
+            nc.vector.tensor_copy(*interleaved(results[(c, parts)], out_rounded[c][:, edges, :]))
 
         def codes_tile(chunks, over=None, skip=0):
             first, count = span(chunks)
@@ -305,7 +303,6 @@ def tile_picked_hub_relu_po_kernel(
                 queues[q % len(queues)].dma_start(rows.bitcast(I32), live.bitcast(I32))
 
         every_tile = range(PACK)
-        part_bytes = PACK * PART * WIDTH[F32]
 
         nc.vector.tensor_copy(x_bytes[:], x_plane[:].indirect(offs_sb[:]))
         nc.vector.tensor_copy(x_codes[:], x_table[:].bitcast(U32).indirect(offs_sb[:]))
@@ -319,81 +316,81 @@ def tile_picked_hub_relu_po_kernel(
         nc.vector.tensor_copy(w1_tile(1, 1, "w1_rounded0")[:, :, :, 0], w1_columns[:, :, :, 1])
         quantise_weight(SOURCE, 1, 1)
         quantise_weight(SOURCE, PAIR, PAIR)
-        deal_w3_words("w1_rounded1")
-        node_tile(SOURCE, 0, PIECE)
-        round_w2("w3_table")
-        for t in range(1, PACK):
-            node_tile(SOURCE, t)
 
+        round_w2(0)
+        round_w2(PAIR)
+        quantise_weight(TARGET, 0, PAIR)
+        quantise_weight(TARGET, PAIR, PAIR)
         sums_tile((0, 1))
-        gather_sources((0, 1, 2), 0, sources_tile((0, 1, 2), 0))
-        gather_sources((0, 1, 2), 1, sources_tile((0, 1, 2), 1, room=2 * part_bytes))
-        quantise_weight(TARGET, 0, PACK)
-        gather_sources((0, 1), 2, sources_tile((0, 1), 2, "w2_raw"))
-        gather_sources((0, 1), 3, sources_tile((0, 1), 3, "w2_raw", part_bytes))
-        deal_w3_bytes("w2_rounded")
-        node_tile(TARGET, 0, PIECE)
+        node_tile(SOURCE, 0, PIECE)
+        node_tile(SOURCE, 1)
+        node_tile(SOURCE, 2, on_vector=True)
+        gather_sources((0, 1), 0, sources_tile((0, 1), 0))
+        node_tile(TARGET, 0)
+        gather_sources((0, 1), 1, sources_tile((0, 1), 1), on_vector=True)
+        node_tile(TARGET, 1)
         add_targets((0, 1), (0,))
-        for t in (1, 2):
-            node_tile(TARGET, t)
-            add_targets((0, 1), (t,))
+        gather_sources((0, 1), 2, sources_tile((0, 1), 2))
+        add_targets((0, 1), (1,))
+        node_tile(SOURCE, 3)
+        node_tile(TARGET, 2, on_vector=True)
+        gather_sources((0, 1), 3, sources_tile((0, 1), 3))
+        deal_w3_words(None)
+        deal_w3_bytes(None)
         node_tile(TARGET, 3)
-        add_targets((0,), (3,))
-        add_targets((1,), (3,))
+        add_targets((0, 1), (2, 3))
 
-        relu_round(0)
-        gather_sources((2,), 2, sources[((0,), 3)])
-        gather_sources((2,), 3, sources[((1,), 3)])
+        for t in every_tile:
+            gather_sources((2,), t, sources_tile((2,), t))
+        relu_round(0, on_vector=True)
+        relu_round(1, on_vector=True)
         quantise_z(0)
         edge_product(0)
-        relu_round(1)
-        sums[(2,)] = sums[(0,)]
-        add_targets((2,), (0,))
         quantise_z(1)
         edge_product(1)
-        add_targets((2,), (2, 3, 1))
-        copy_out(0, (0, 1))
-        copy_out(1, (0, 1))
-
-        relu_round(2)
         for t in (0, 1):
-            gather_sources((3, 4), t, sources_tile((3, 4), t, "z_rounded1", t * part_bytes // 2))
+            gather_sources((3, 4), t, sources_tile((3, 4), t))
+        sums_tile((2,))
+        add_targets((2,), every_tile)
+        copy_out(0, (0, 1))
         for t in (2, 3):
-            gather_sources((3, 4), t, sources[((2,), t)])
+            gather_sources((3, 4), t, sources_tile((3, 4), t))
+        copy_out(1, (0, 1))
+        relu_round(2, on_vector=True)
+        sums_tile((3,))
+        sums_tile((4,))
+        add_targets((3,), (0,))
         quantise_z(2)
         edge_product(2)
-        rounded_tile((0, 1), "sources01")
-        round_on_gpsimd(0, (0, 1))
-        round_from_bank(1, 0)
-        round_from_bank(1, 1)
-        sums_tile((3,), "sums0")
-        sums_tile((4,), "sums0", 2 * part_bytes)
-        add_targets((3,), every_tile)
-        copy_out(2, (0,))
-        relu_round(3)
-        copy_out(2, (1,))
-        add_targets((4,), every_tile)
-
+        add_targets((3,), (1, 2, 3))
+        rounded_tile((0, 1))
+        round_from_bank(0, 0)
+        round_from_bank(0, 1)
+        copy_out(2, (0, 1))
+        relu_round(3, on_vector=True)
+        add_targets((4,), (0,))
         quantise_z(3)
         edge_product(3)
-        rounded_tile((2,))
-        round_from_bank(2, 0)
-        relu_round(4, "sums3", on_vector=True)
-        codes_tile((0,), "sums3", part_bytes // 2)
+        add_targets((4,), (1, 2, 3))
+        round_from_bank(1, 0)
+        round_from_bank(1, 1)
+        relu_round(4, on_vector=True)
+        codes_tile((0,))
         quantise_out(0)
         store_codes((0,))
         quantise_z(4)
         copy_out(3, (0,))
-        codes_tile((1,), "z_rounded3")
+        rounded_tile((2,))
+        round_on_vector(2, (0, 1))
+        codes_tile((1,))
         quantise_out(1)
         store_codes((1,))
-        round_on_vector(2, 1)
         last_product(4)
         codes_tile((2, 3, 4))
         quantise_out(2)
         for c in (3, 4):
             rounded_tile((c,))
-            round_on_vector(c, 0)
+            round_on_vector(c, (0,))
         quantise_out(3)
         quantise_out(4)
         store_codes((2, 3, 4))

@@ -117,7 +117,8 @@ def tile_picked_hub_relu_po_kernel(
 
         def w1_tile(t, count, over=None, room=0):
             dealt = place("w1_rounded%d" % t, [P, count, P, PACK], BF16, over, room=room)
-            rounded[(SOURCE, t)] = dealt[:]
+            for u in range(count):
+                rounded[(SOURCE, t + u)] = dealt[:, u:]
             return dealt[:].rearrange("p t m j -> p m j t")
 
         w1_columns = w1_raw[:].rearrange("p j (m t) -> p m j t", t=PACK)
@@ -142,7 +143,7 @@ def tile_picked_hub_relu_po_kernel(
         x_bytes = place("x_bytes", [P, S], U8)
         windows = {}
 
-        def node_tile(side, t, width=BANK, on_vector=False, over=None):
+        def node_tile(side, t, width=BANK, on_vector=(), over=None):
             codes, plane = weights[(side, t)]
             windows[(side, t)] = place("window%d%d" % (side, t), [P, S], F32, over)
             for first in range(0, S, width):
@@ -157,7 +158,7 @@ def tile_picked_hub_relu_po_kernel(
                     start=True,
                     stop=True,
                 )
-                if on_vector:
+                if first // width in on_vector:
                     nc.vector.tensor_copy(windows[(side, t)][:, nodes], acc[:])
                 else:
                     nc.scalar.copy(windows[(side, t)][:, nodes], acc[:])
@@ -176,6 +177,7 @@ def tile_picked_hub_relu_po_kernel(
             by_tile = w3_dealt["bytes"][:].rearrange("p (t m) -> p t m", t=PACK)
             nc.vector.tensor_copy(by_tile, w3_plane[:].rearrange("p (m t) -> p t m", t=PACK))
 
+        part_bytes = PACK * PART * WIDTH[F32]
         sources, sums, z_rounded, z_packed = {}, {}, {}, {}
         accs, results, out_rounded, out_codes = {}, {}, {}, {}
         out_plane = place("out_plane", [P, QUARTER], U8)
@@ -196,12 +198,18 @@ def tile_picked_hub_relu_po_kernel(
                     begin, width = span(chunks[low:high])
                     sources[(chunks[low:high], t)] = picked[:, begin - first : begin - first + width]
 
-        def sums_tile(chunks, over=None, skip=0):
-            first, count = span(chunks)
-            whole = place("sums%d" % chunks[0], [P, PACK, count], F32, over, skip)
-            sums[chunks] = whole[:]
-            for c in chunks:
-                sums[(c,)] = whole[:, :, FIRSTS[c] - first : FIRSTS[c] - first + CHUNKS[c]]
+        row = CHUNKS[0]
+        arena = place("arena", [P, (PAIR * len(CHUNKS) + PACK) * row], F32)
+
+        def arena_rows(c, first, count):
+            begin = (PAIR * (len(CHUNKS) - c) + first) * row
+            return arena[:, begin : begin + count * row].rearrange("p (t n) -> p t n", n=row)
+
+        for c in range(len(CHUNKS)):
+            sums[(c,)] = arena_rows(c, 0, PACK)[:, :, : CHUNKS[c]]
+
+        def late_sources(c, u):
+            return arena_rows(c, u - PAIR, 1)[:, 0, :]
 
         def add_targets(chunks, tiles):
             first, count = span(chunks)
@@ -218,7 +226,7 @@ def tile_picked_hub_relu_po_kernel(
                 nc.scalar.activation(by_column, by_tile, RELU)
 
         def quantise_z(c):
-            codes = place("z_codes%d" % c, [P, CHUNKS[c]], U32)
+            codes = place("z_codes%d" % c, [P, CHUNKS[c]], U32, room=part_bytes)
             plane = place("z_plane%d" % c, [P, CHUNKS[c]], U8)
             nc.vector.quantize_mx(
                 out=codes[:].bitcast(FP8X4), scales=plane[:], in_=z_rounded[c][:].rearrange("p n t -> p (n t)")
@@ -273,9 +281,9 @@ def tile_picked_hub_relu_po_kernel(
         def round_from_bank(c, part):
             nc.scalar.copy(*interleaved(accs[(c, part)][:], out_rounded[c][:, part * PART : (part + 1) * PART, :]))
 
-        def round_on_vector(c, parts):
-            edges = slice(parts[0] * PART, (parts[-1] + 1) * PART)
-            nc.vector.tensor_copy(*interleaved(results[(c, parts)], out_rounded[c][:, edges, :]))
+        def round_on_vector(c, parts, part):
+            held = results[(c, parts)][:, :, (part - parts[0]) * PART : (part - parts[0] + 1) * PART]
+            nc.vector.tensor_copy(*interleaved(held, out_rounded[c][:, part * PART : (part + 1) * PART, :]))
 
         def codes_tile(chunks, over=None, skip=0):
             first, count = span(chunks)
@@ -307,13 +315,12 @@ def tile_picked_hub_relu_po_kernel(
         nc.vector.tensor_copy(x_bytes[:], x_plane[:].indirect(offs_sb[:]))
         nc.vector.tensor_copy(x_codes[:], x_table[:].bitcast(U32).indirect(offs_sb[:]))
 
-        tile0, last_pair = w1_tile(0, 1, room=H * WIDTH[I32]), w1_tile(PAIR, PAIR)
         half = P // 2
-        nc.scalar.copy(tile0[:, half:, :, 0], w1_columns[:, half:, :, 0])
-        nc.vector.tensor_copy(tile0[:, :half, :, 0], w1_columns[:, :half, :, 0])
-        nc.scalar.copy(last_pair, w1_columns[:, :, :, PAIR:])
+        first_pair = w1_tile(0, PAIR)
+        nc.scalar.copy(first_pair[:, half:], w1_columns[:, half:, :, :PAIR])
+        nc.vector.tensor_copy(first_pair[:, :half], w1_columns[:, :half, :, :PAIR])
+        nc.scalar.copy(w1_tile(PAIR, PAIR), w1_columns[:, :, :, PAIR:])
         quantise_weight(SOURCE, 0, 1)
-        nc.vector.tensor_copy(w1_tile(1, 1, "w1_rounded0")[:, :, :, 0], w1_columns[:, :, :, 1])
         quantise_weight(SOURCE, 1, 1)
         quantise_weight(SOURCE, PAIR, PAIR)
 
@@ -321,76 +328,88 @@ def tile_picked_hub_relu_po_kernel(
         round_w2(PAIR)
         quantise_weight(TARGET, 0, PAIR)
         quantise_weight(TARGET, PAIR, PAIR)
-        sums_tile((0, 1))
         node_tile(SOURCE, 0, PIECE)
         node_tile(SOURCE, 1)
-        node_tile(SOURCE, 2, on_vector=True)
-        gather_sources((0, 1), 0, sources_tile((0, 1), 0))
+        node_tile(SOURCE, 2, on_vector=(0, 1))
+        for t in (0, 1):
+            gather_sources((0,), t, sources_tile((0,), t))
         node_tile(TARGET, 0)
-        gather_sources((0, 1), 1, sources_tile((0, 1), 1), on_vector=True)
-        node_tile(TARGET, 1)
-        add_targets((0, 1), (0,))
-        gather_sources((0, 1), 2, sources_tile((0, 1), 2))
-        add_targets((0, 1), (1,))
-        node_tile(SOURCE, 3)
-        node_tile(TARGET, 2, on_vector=True)
-        gather_sources((0, 1), 3, sources_tile((0, 1), 3))
         deal_w3_words(None)
-        deal_w3_bytes(None)
+        node_tile(SOURCE, 3, on_vector=(0, 1))
+        add_targets((0,), (0,))
+        node_tile(TARGET, 1)
+        node_tile(TARGET, 2, on_vector=(0, 1))
+        add_targets((0,), (1,))
+        for t in (2, 3):
+            gather_sources((0,), t, late_sources(0, t - PAIR))
+        add_targets((0,), (2,))
+        gather_sources((1,), 0, sources_tile((1,), 0, "sources00"))
         node_tile(TARGET, 3)
-        add_targets((0, 1), (2, 3))
-
-        for t in every_tile:
-            gather_sources((2,), t, sources_tile((2,), t))
+        add_targets((1,), (0,))
+        add_targets((0,), (3,))
+        deal_w3_bytes("w3_table")
+        gather_sources((1,), 1, sources_tile((1,), 1, "sources01"))
+        for t in (2, 3):
+            gather_sources((1,), t, late_sources(1, t - PAIR))
         relu_round(0, on_vector=True)
-        relu_round(1, on_vector=True)
+        add_targets((1,), (1,))
         quantise_z(0)
         edge_product(0)
+        add_targets((1,), (2, 3))
+        for t in (0, 1):
+            gather_sources((2,), t, sources_tile((2,), t, "sources1%d" % t))
+        for t in (2, 3):
+            gather_sources((2,), t, late_sources(2, t - PAIR))
+        copy_out(0, (0, 1))
+        add_targets((2,), (0,))
+        relu_round(1, on_vector=True)
+        add_targets((2,), (1,))
         quantise_z(1)
         edge_product(1)
+        add_targets((2,), (2, 3))
         for t in (0, 1):
-            gather_sources((3, 4), t, sources_tile((3, 4), t))
-        sums_tile((2,))
-        add_targets((2,), every_tile)
-        copy_out(0, (0, 1))
+            gather_sources((3, 4), t, sources_tile((3, 4), t, "sources2%d" % t))
         for t in (2, 3):
-            gather_sources((3, 4), t, sources_tile((3, 4), t))
+            gather_sources((3, 4), t, late_sources(3, t - PAIR))
         copy_out(1, (0, 1))
-        relu_round(2, on_vector=True)
-        sums_tile((3,))
-        sums_tile((4,))
-        add_targets((3,), (0,))
-        quantise_z(2)
-        edge_product(2)
-        add_targets((3,), (1, 2, 3))
-        rounded_tile((0, 1))
+        rounded_tile((0,))
         round_from_bank(0, 0)
         round_from_bank(0, 1)
+        add_targets((3,), (0,))
+        relu_round(2, on_vector=True)
+        add_targets((3,), (1,))
+        quantise_z(2)
+        edge_product(2)
+        add_targets((3,), (2, 3))
         copy_out(2, (0, 1))
-        relu_round(3, on_vector=True)
-        add_targets((4,), (0,))
-        quantise_z(3)
-        edge_product(3)
-        add_targets((4,), (1, 2, 3))
+        rounded_tile((1,), "z_codes2")
         round_from_bank(1, 0)
         round_from_bank(1, 1)
-        relu_round(4, on_vector=True)
-        codes_tile((0,))
+        add_targets((4,), (0,))
+        relu_round(3, on_vector=True)
+        add_targets((4,), (1,))
+        quantise_z(3)
+        edge_product(3)
+        add_targets((4,), (2, 3))
+        copy_out(3, (0,))
+        codes_tile((0,), "sources31")
         quantise_out(0)
         store_codes((0,))
-        quantise_z(4)
-        copy_out(3, (0,))
+        relu_round(4, on_vector=True)
         rounded_tile((2,))
-        round_on_vector(2, (0, 1))
-        codes_tile((1,))
+        round_on_vector(2, (0, 1), 0)
+        quantise_z(4)
+        last_product(4)
+        round_on_vector(2, (0, 1), 1)
+        codes_tile((1,), "z_rounded4")
         quantise_out(1)
         store_codes((1,))
-        last_product(4)
+        rounded_tile((3,))
+        round_on_vector(3, (0,), 0)
         codes_tile((2, 3, 4))
         quantise_out(2)
-        for c in (3, 4):
-            rounded_tile((c,))
-            round_on_vector(c, (0,))
+        rounded_tile((4,))
+        round_on_vector(4, (0,), 0)
         quantise_out(3)
         quantise_out(4)
         store_codes((2, 3, 4))

@@ -26,14 +26,17 @@ BANK = 512
 BANKS = 8
 PART = BANK // PACK
 PIECE = BANK // 2
+HALF = S // 2
 QUARTER = S // PACK
 LIST_ROWS = 16
 LINE_COLUMNS = 2
 LINE_WORDS = 4
 ALIGN = 64
 SOURCE, TARGET = 0, 1
-CHUNKS = (256, 256, 256, 128, 128)
+CHUNKS = (256, 384, 256, 128)
 FIRSTS = [sum(CHUNKS[:c]) for c in range(len(CHUNKS))]
+GATHERS = (256, 384, 384)
+ROW = max(GATHERS)
 
 
 def scale_rows(plane, scales, r):
@@ -55,10 +58,6 @@ def entries(offsets, first, count):
     return offsets[:, first // LIST_ROWS : (first + count) // LIST_ROWS]
 
 
-def span(chunks):
-    return FIRSTS[chunks[0]], sum(CHUNKS[c] for c in chunks)
-
-
 def tile_picked_hub_relu_po_kernel(
     tc, x_words, x_scales, w1, w2, w3_words, w3_scales, offs, src, dst, out_0, out_1, out_2
 ):
@@ -71,7 +70,7 @@ def tile_picked_hub_relu_po_kernel(
         starts = {}
         used = [0]
 
-        def place(name, shape, dtype, over=None, skip=0, room=0):
+        def place(name, shape, dtype, over=None, room=0):
             if over is None:
                 starts[name] = used[0]
                 size = WIDTH[dtype]
@@ -79,7 +78,7 @@ def tile_picked_hub_relu_po_kernel(
                     size = size * extent
                 used[0] = starts[name] + max(room, -(-size // ALIGN) * ALIGN)
             else:
-                starts[name] = starts[over] + skip
+                starts[name] = starts[over]
             return placed.tile(shape, dtype, name=name, tag=name, align_bytes=ALIGN, offset=starts[name])
 
         banks_taken = []
@@ -96,7 +95,7 @@ def tile_picked_hub_relu_po_kernel(
         x_plane = place("x_plane", [P, T], U8)
         w1_raw = place("w1_raw", [P, PACK, H], F32)
         w2_raw = place("w2_raw", [P, PACK, H], F32)
-        w3_table = place("w3_table", [P, H], I32, room=PACK * H * WIDTH[BF16])
+        w3_table = place("w3_table", [P, H], I32)
         w3_plane = place("w3_plane", [P, H], U8)
 
         nc.vector.memset(x_plane[:].bitcast(I32), 0)
@@ -113,26 +112,22 @@ def tile_picked_hub_relu_po_kernel(
         for q in range(QUADRANTS):
             nc.sync.dma_start(*scale_rows(w3_plane, w3_scales, q))
 
+        by_row = {
+            SOURCE: w1_raw[:].rearrange("p j (m t) -> p m j t", t=PACK),
+            TARGET: w2_raw[:].rearrange("p j (m t) -> p m j t", t=PACK),
+        }
         rounded, weights = {}, {}
 
-        def w1_tile(t, count, over=None, room=0):
-            dealt = place("w1_rounded%d" % t, [P, count, P, PACK], BF16, over, room=room)
-            for u in range(count):
-                rounded[(SOURCE, t + u)] = dealt[:, u:]
-            return dealt[:].rearrange("p t m j -> p m j t")
-
-        w1_columns = w1_raw[:].rearrange("p j (m t) -> p m j t", t=PACK)
-
-        def round_w2(first, over=None):
-            dealt = place("w2_rounded%d" % first, [P, PAIR, P, PACK], BF16, over)
-            by_row = w2_raw[:].rearrange("p j (m t) -> p m j t", t=PACK)
-            nc.vector.tensor_copy(dealt[:].rearrange("p t m j -> p m j t"), by_row[:, :, :, first : first + PAIR])
-            rounded[(TARGET, first)] = dealt[:]
+        def round_pair(side, first, copy, columns=slice(0, P), over=None):
+            if (side, first) not in rounded:
+                rounded[(side, first)] = place("w_rounded%d%d" % (side, first), [P, PAIR, P, PACK], BF16, over)
+            by_tile = rounded[(side, first)][:].rearrange("p t m j -> p m j t")
+            copy(by_tile[:, columns], by_row[side][:, columns, :, first : first + PAIR])
 
         def quantise_weight(side, first, count):
             codes = place("w_codes%d%d" % (side, first), [P, count * P], U32)
             plane = place("w_plane%d%d" % (side, first), [P, count * P], U8)
-            source = rounded[(side, first)][:, :count]
+            source = rounded[(side, first - first % PAIR)][:, first % PAIR : first % PAIR + count]
             nc.vector.quantize_mx(
                 out=codes[:].bitcast(FP8X4), scales=plane[:], in_=source.rearrange("p t m j -> p (t m j)")
             )
@@ -143,166 +138,157 @@ def tile_picked_hub_relu_po_kernel(
         x_bytes = place("x_bytes", [P, S], U8)
         windows = {}
 
-        def node_tile(side, t, width=BANK, on_vector=(), over=None):
+        def node_piece(side, t, first, width, copy, over=None):
             codes, plane = weights[(side, t)]
-            windows[(side, t)] = place("window%d%d" % (side, t), [P, S], F32, over)
+            if (side, t) not in windows:
+                windows[(side, t)] = place("window%d%d" % (side, t), [P, S], F32, over)
+            nodes = slice(first, first + width)
+            acc = next_bank([P, width])
+            nc.tensor.matmul_mx(
+                out=acc[:],
+                lhsT=codes.bitcast(FP8X4),
+                lhsT_scale=plane,
+                rhs=x_codes[:, nodes].bitcast(FP8X4),
+                rhs_scale=x_bytes[:, nodes],
+                start=True,
+                stop=True,
+            )
+            copy(windows[(side, t)][:, nodes], acc[:])
+
+        def node_tile(side, t, copy, width=BANK, over=None):
             for first in range(0, S, width):
-                nodes = slice(first, first + width)
-                acc = next_bank([P, width])
-                nc.tensor.matmul_mx(
-                    out=acc[:],
-                    lhsT=codes.bitcast(FP8X4),
-                    lhsT_scale=plane,
-                    rhs=x_codes[:, nodes].bitcast(FP8X4),
-                    rhs_scale=x_bytes[:, nodes],
-                    start=True,
-                    stop=True,
-                )
-                if first // width in on_vector:
-                    nc.vector.tensor_copy(windows[(side, t)][:, nodes], acc[:])
-                else:
-                    nc.scalar.copy(windows[(side, t)][:, nodes], acc[:])
+                node_piece(side, t, first, width, copy, over)
 
         w3_dealt = {}
 
-        def deal_w3_words(over):
+        def deal_w3_words(over=None):
             w3_dealt["codes"] = place("w3_codes", [P, H], I32, over)
             nc.vector.tensor_copy(
                 w3_dealt["codes"][:].rearrange("p (t g i) -> p g t i", t=PACK, i=LINE_WORDS),
                 w3_table[:].rearrange("p (g i t) -> p g t i", t=PACK, i=LINE_WORDS),
             )
 
-        def deal_w3_bytes(over):
+        def deal_w3_bytes(over=None):
             w3_dealt["bytes"] = place("w3_bytes", [P, H], U8, over)
-            by_tile = w3_dealt["bytes"][:].rearrange("p (t m) -> p t m", t=PACK)
-            nc.vector.tensor_copy(by_tile, w3_plane[:].rearrange("p (m t) -> p t m", t=PACK))
+            nc.vector.tensor_copy(
+                w3_dealt["bytes"][:].rearrange("p (t m) -> p t m", t=PACK),
+                w3_plane[:].rearrange("p (m t) -> p t m", t=PACK),
+            )
 
-        part_bytes = PACK * PART * WIDTH[F32]
-        sources, sums, z_rounded, z_packed = {}, {}, {}, {}
-        accs, results, out_rounded, out_codes = {}, {}, {}, {}
+        arena = place("arena", [P, PAIR * (len(CHUNKS) + 1) * ROW], F32)
+        arena_rows = arena[:].rearrange("p (r n) -> p r n", n=ROW)
+        first_row = [PAIR * (len(CHUNKS) - 1 - c) for c in range(len(CHUNKS))]
+        sums = [arena_rows[:, first_row[c] : first_row[c] + PACK, : CHUNKS[c]] for c in range(len(CHUNKS))]
+        sources, z_rounded, z_packed, accs, results, out_rounded, out_codes = {}, {}, {}, {}, {}, {}, {}
         out_plane = place("out_plane", [P, QUARTER], U8)
         out_rows = out_0.rearrange("(p t) n -> p t n", t=PACK)
 
-        def sources_tile(chunks, t, over=None, skip=0, room=0):
-            return place("sources%d%d" % (chunks[0], t), [P, span(chunks)[1]], F32, over, skip, room)[:]
-
-        def gather_sources(chunks, t, picked, on_vector=False):
-            first, count = span(chunks)
-            looked_up = windows[(SOURCE, t)][:].indirect(entries(src_sb, first, count))
-            if on_vector:
-                nc.vector.tensor_copy(picked, looked_up)
+        def gather_sources(c, t, over=None):
+            count = GATHERS[c]
+            if t >= PAIR:
+                picked = arena_rows[:, first_row[c + 1] + t - PAIR, :count]
             else:
-                nc.scalar.activation(picked, looked_up, COPY)
-            for low in range(len(chunks)):
-                for high in range(low + 1, len(chunks) + 1):
-                    begin, width = span(chunks[low:high])
-                    sources[(chunks[low:high], t)] = picked[:, begin - first : begin - first + width]
+                picked = place("sources%d%d" % (c, t), [P, count], F32, over, ROW * WIDTH[F32])[:]
+            looked_up = windows[(SOURCE, t)][:].indirect(entries(src_sb, FIRSTS[c], count))
+            nc.scalar.activation(picked, looked_up, COPY)
+            for u in range(c, len(CHUNKS)):
+                if FIRSTS[u] < FIRSTS[c] + count:
+                    sources[(u, t)] = picked[:, FIRSTS[u] - FIRSTS[c] : FIRSTS[u] - FIRSTS[c] + CHUNKS[u]]
 
-        row = CHUNKS[0]
-        arena = place("arena", [P, (PAIR * len(CHUNKS) + PACK) * row], F32)
+        def add_targets(c, t):
+            looked_up = windows[(TARGET, t)][:].indirect(entries(dst_sb, FIRSTS[c], CHUNKS[c]))
+            nc.vector.tensor_tensor(sums[c][:, t, :], looked_up, sources[(c, t)], ADD)
 
-        def arena_rows(c, first, count):
-            begin = (PAIR * (len(CHUNKS) - c) + first) * row
-            return arena[:, begin : begin + count * row].rearrange("p (t n) -> p t n", n=row)
+        def chunk_of(part):
+            return max(c for c in range(len(CHUNKS)) if FIRSTS[c] <= part * PART)
 
-        for c in range(len(CHUNKS)):
-            sums[(c,)] = arena_rows(c, 0, PACK)[:, :, : CHUNKS[c]]
-
-        def late_sources(c, u):
-            return arena_rows(c, u - PAIR, 1)[:, 0, :]
-
-        def add_targets(chunks, tiles):
-            first, count = span(chunks)
-            for t in tiles:
-                looked_up = windows[(TARGET, t)][:].indirect(entries(dst_sb, first, count))
-                nc.vector.tensor_tensor(sums[chunks][:, t, :], looked_up, sources[(chunks, t)], ADD)
-
-        def relu_round(c, over=None, on_vector=False):
-            z_rounded[c] = place("z_rounded%d" % c, [P, CHUNKS[c], PACK], BF16, over)
-            by_column, by_tile = interleaved(sums[(c,)], z_rounded[c][:])
-            if on_vector:
-                nc.vector.tensor_scalar_max(by_column, by_tile, 0.0)
-            else:
+        def relu_round(parts, over=None, scalar=False):
+            c, count = chunk_of(parts[0]), len(parts) * PART
+            first = parts[0] * PART - FIRSTS[c]
+            z_rounded[parts] = place("z_rounded%d" % parts[0], [P, count, PACK], BF16, over)
+            by_column, by_tile = interleaved(sums[c][:, :, first : first + count], z_rounded[parts][:])
+            if scalar:
                 nc.scalar.activation(by_column, by_tile, RELU)
+            else:
+                nc.vector.tensor_scalar_max(by_column, by_tile, 0.0)
 
-        def quantise_z(c):
-            codes = place("z_codes%d" % c, [P, CHUNKS[c]], U32, room=part_bytes)
-            plane = place("z_plane%d" % c, [P, CHUNKS[c]], U8)
+        def quantise_z(parts):
+            codes = place("z_codes%d" % parts[0], [P, len(parts) * PART], U32)
+            plane = place("z_plane%d" % parts[0], [P, len(parts) * PART], U8)
             nc.vector.quantize_mx(
-                out=codes[:].bitcast(FP8X4), scales=plane[:], in_=z_rounded[c][:].rearrange("p n t -> p (n t)")
+                out=codes[:].bitcast(FP8X4), scales=plane[:], in_=z_rounded[parts][:].rearrange("p n t -> p (n t)")
             )
-            z_packed[c] = (codes, plane)
+            for u, part in enumerate(parts):
+                z_packed[part] = (codes[:, u * PART : (u + 1) * PART], plane[:, u * PART : (u + 1) * PART])
 
-        def w3_product(acc, t, c, edges):
-            codes, plane = z_packed[c]
+        def w3_product(acc, t, part):
+            codes, plane = z_packed[part]
             columns = slice(t * P, (t + 1) * P)
             nc.tensor.matmul_mx(
                 out=acc,
                 lhsT=w3_dealt["codes"][:, columns].bitcast(FP8X4),
                 lhsT_scale=w3_dealt["bytes"][:, columns],
-                rhs=codes[:, edges].bitcast(FP8X4),
-                rhs_scale=plane[:, edges],
+                rhs=codes.bitcast(FP8X4),
+                rhs_scale=plane,
                 start=True,
                 stop=True,
             )
 
-        def edge_product(c):
-            for part in range(CHUNKS[c] // PART):
-                accs[(c, part)] = next_bank([P, PACK, PART])
+        def edge_products(parts):
+            for part in parts:
+                accs[part] = next_bank([P, PACK, PART])
                 for t in range(PACK):
-                    w3_product(accs[(c, part)][:, t, :], t, c, slice(part * PART, (part + 1) * PART))
+                    w3_product(accs[part][:, t, :], t, part)
 
-        def store_results(first, held):
-            nc.sync.dma_start(out_rows[:, :, first : first + held.shape[2]], held)
+        def store_results(part, held):
+            nc.sync.dma_start(out_rows[:, :, part * PART : part * PART + held.shape[2]], held)
 
-        def copy_out(c, parts):
-            held = place("results%d%d" % (c, parts[0]), [P, PACK, len(parts) * PART], F32)
+        def copy_out(parts, over=None):
+            held = place("results%d" % parts[0], [P, PACK, len(parts) * PART], F32, over)
             for u, part in enumerate(parts):
-                nc.scalar.copy(held[:, :, u * PART : (u + 1) * PART], accs[(c, part)][:])
-            results[(c, parts)] = held[:]
-            store_results(FIRSTS[c] + parts[0] * PART, held[:])
+                results[part] = held[:, :, u * PART : (u + 1) * PART]
+                nc.scalar.copy(results[part], accs[part][:])
+            results[parts] = held[:]
+            store_results(parts[0], held[:])
 
-        def last_product(c):
-            held = place("results%d0" % c, [P, PACK, PART], F32)
+        def last_product(part):
+            held = place("results%d" % part, [P, PACK, PART], F32)
             for first in range(0, PACK, PAIR):
                 acc = next_bank([P, PAIR, PART])
                 for u in range(PAIR):
-                    w3_product(acc[:, u, :], first + u, c, slice(0, PART))
+                    w3_product(acc[:, u, :], first + u, part)
                 nc.scalar.copy(held[:, first : first + PAIR, :], acc[:])
-            results[(c, (0,))] = held[:]
-            store_results(FIRSTS[c], held[:])
+            results[part] = held[:]
+            store_results(part, held[:])
 
-        def rounded_tile(chunks, over=None, skip=0):
-            first, count = span(chunks)
-            whole = place("out_rounded%d" % chunks[0], [P, count, PACK], BF16, over, skip)
-            for c in chunks:
-                out_rounded[c] = whole[:, FIRSTS[c] - first : FIRSTS[c] - first + CHUNKS[c], :]
+        def rounded_tile(parts, over=None):
+            whole = place("out_rounded%d" % parts[0], [P, len(parts) * PART, PACK], BF16, over)
+            out_rounded[parts] = whole[:]
+            for u, part in enumerate(parts):
+                out_rounded[part] = whole[:, u * PART : (u + 1) * PART, :]
 
-        def round_from_bank(c, part):
-            nc.scalar.copy(*interleaved(accs[(c, part)][:], out_rounded[c][:, part * PART : (part + 1) * PART, :]))
+        def round_from_bank(part):
+            nc.scalar.copy(*interleaved(accs[part][:], out_rounded[part]))
 
-        def round_on_vector(c, parts, part):
-            held = results[(c, parts)][:, :, (part - parts[0]) * PART : (part - parts[0] + 1) * PART]
-            nc.vector.tensor_copy(*interleaved(held, out_rounded[c][:, part * PART : (part + 1) * PART, :]))
+        def round_on_vector(parts):
+            nc.vector.tensor_copy(*interleaved(results[parts], out_rounded[parts]))
 
-        def codes_tile(chunks, over=None, skip=0):
-            first, count = span(chunks)
-            codes = place("out_codes%d" % chunks[0], [P, count], U32, over, skip)
-            out_codes[chunks] = codes[:]
-            for c in chunks:
-                out_codes[(c,)] = codes[:, FIRSTS[c] - first : FIRSTS[c] - first + CHUNKS[c]]
+        def codes_tile(parts, over=None):
+            out_codes[parts] = place("out_codes%d" % parts[0], [P, len(parts) * PART], U32, over)
 
-        def quantise_out(c):
-            quarter, first = divmod(FIRSTS[c], QUARTER)
+        def quantise_out(parts, stored):
+            quarter, first = divmod(parts[0] * PART, QUARTER)
+            begin, count = (parts[0] - stored[0]) * PART, len(parts) * PART
+            source = out_rounded[parts] if len(parts) > 1 else out_rounded[parts[0]]
             nc.vector.quantize_mx(
-                out=out_codes[(c,)].bitcast(FP8X4),
-                scales=out_plane[PACK * quarter :, first : first + CHUNKS[c]],
-                in_=out_rounded[c].rearrange("p n t -> p (n t)"),
+                out=out_codes[stored][:, begin : begin + count].bitcast(FP8X4),
+                scales=out_plane[PACK * quarter :, first : first + count],
+                in_=source.rearrange("p n t -> p (n t)"),
             )
 
-        def store_codes(chunks):
-            first, count = span(chunks)
-            nc.sync.dma_start(as_words(out_1)[:, first : first + count], out_codes[chunks].bitcast(I32))
+        def store_codes(parts):
+            columns = slice(parts[0] * PART, (parts[-1] + 1) * PART)
+            nc.sync.dma_start(as_words(out_1)[:, columns], out_codes[parts][:].bitcast(I32))
 
         def store_scales(queues):
             for q in range(QUADRANTS):
@@ -310,107 +296,98 @@ def tile_picked_hub_relu_po_kernel(
                 live = out_plane[QUADRANT * q : QUADRANT * q + PACK * PACK, :]
                 queues[q % len(queues)].dma_start(rows.bitcast(I32), live.bitcast(I32))
 
-        every_tile = range(PACK)
+        on_scalar, on_vector = nc.scalar.copy, nc.vector.tensor_copy
 
         nc.vector.tensor_copy(x_bytes[:], x_plane[:].indirect(offs_sb[:]))
         nc.vector.tensor_copy(x_codes[:], x_table[:].bitcast(U32).indirect(offs_sb[:]))
 
-        half = P // 2
-        first_pair = w1_tile(0, PAIR)
-        nc.scalar.copy(first_pair[:, half:], w1_columns[:, half:, :, :PAIR])
-        nc.vector.tensor_copy(first_pair[:, :half], w1_columns[:, :half, :, :PAIR])
-        nc.scalar.copy(w1_tile(PAIR, PAIR), w1_columns[:, :, :, PAIR:])
+        for first in (0, PAIR):
+            round_pair(SOURCE, first, on_scalar, slice(P // 2, P))
+            round_pair(SOURCE, first, on_vector, slice(0, P // 2))
         quantise_weight(SOURCE, 0, 1)
         quantise_weight(SOURCE, 1, 1)
         quantise_weight(SOURCE, PAIR, PAIR)
-
-        round_w2(0)
-        round_w2(PAIR)
-        quantise_weight(TARGET, 0, PAIR)
-        quantise_weight(TARGET, PAIR, PAIR)
-        node_tile(SOURCE, 0, PIECE)
-        node_tile(SOURCE, 1)
-        node_tile(SOURCE, 2, on_vector=(0, 1))
-        for t in (0, 1):
-            gather_sources((0,), t, sources_tile((0,), t))
-        node_tile(TARGET, 0)
-        deal_w3_words(None)
-        node_tile(SOURCE, 3, on_vector=(0, 1))
-        add_targets((0,), (0,))
-        node_tile(TARGET, 1)
-        node_tile(TARGET, 2, on_vector=(0, 1))
-        add_targets((0,), (1,))
-        for t in (2, 3):
-            gather_sources((0,), t, late_sources(0, t - PAIR))
-        add_targets((0,), (2,))
-        gather_sources((1,), 0, sources_tile((1,), 0, "sources00"))
-        node_tile(TARGET, 3)
-        add_targets((1,), (0,))
-        add_targets((0,), (3,))
-        deal_w3_bytes("w3_table")
-        gather_sources((1,), 1, sources_tile((1,), 1, "sources01"))
-        for t in (2, 3):
-            gather_sources((1,), t, late_sources(1, t - PAIR))
-        relu_round(0, on_vector=True)
-        add_targets((1,), (1,))
-        quantise_z(0)
-        edge_product(0)
-        add_targets((1,), (2, 3))
-        for t in (0, 1):
-            gather_sources((2,), t, sources_tile((2,), t, "sources1%d" % t))
-        for t in (2, 3):
-            gather_sources((2,), t, late_sources(2, t - PAIR))
-        copy_out(0, (0, 1))
-        add_targets((2,), (0,))
-        relu_round(1, on_vector=True)
-        add_targets((2,), (1,))
-        quantise_z(1)
-        edge_product(1)
-        add_targets((2,), (2, 3))
-        for t in (0, 1):
-            gather_sources((3, 4), t, sources_tile((3, 4), t, "sources2%d" % t))
-        for t in (2, 3):
-            gather_sources((3, 4), t, late_sources(3, t - PAIR))
-        copy_out(1, (0, 1))
-        rounded_tile((0,))
-        round_from_bank(0, 0)
-        round_from_bank(0, 1)
-        add_targets((3,), (0,))
-        relu_round(2, on_vector=True)
-        add_targets((3,), (1,))
-        quantise_z(2)
-        edge_product(2)
-        add_targets((3,), (2, 3))
-        copy_out(2, (0, 1))
-        rounded_tile((1,), "z_codes2")
-        round_from_bank(1, 0)
-        round_from_bank(1, 1)
-        add_targets((4,), (0,))
-        relu_round(3, on_vector=True)
-        add_targets((4,), (1,))
-        quantise_z(3)
-        edge_product(3)
-        add_targets((4,), (2, 3))
-        copy_out(3, (0,))
-        codes_tile((0,), "sources31")
-        quantise_out(0)
-        store_codes((0,))
-        relu_round(4, on_vector=True)
-        rounded_tile((2,))
-        round_on_vector(2, (0, 1), 0)
-        quantise_z(4)
-        last_product(4)
-        round_on_vector(2, (0, 1), 1)
-        codes_tile((1,), "z_rounded4")
-        quantise_out(1)
-        store_codes((1,))
-        rounded_tile((3,))
-        round_on_vector(3, (0,), 0)
-        codes_tile((2, 3, 4))
-        quantise_out(2)
-        rounded_tile((4,))
-        round_on_vector(4, (0,), 0)
-        quantise_out(3)
-        quantise_out(4)
-        store_codes((2, 3, 4))
+        for first in (0, PAIR):
+            round_pair(TARGET, first, on_vector)
+        for first in (0, PAIR):
+            quantise_weight(TARGET, first, PAIR)
+        node_tile(SOURCE, 0, on_scalar, PIECE)
+        node_tile(SOURCE, 1, on_scalar)
+        node_tile(SOURCE, 2, on_vector, over="w2_raw")
+        gather_sources(0, 0)
+        gather_sources(0, 1)
+        node_tile(TARGET, 0, on_scalar)
+        deal_w3_words()
+        node_tile(SOURCE, 3, on_vector, over="w_rounded10")
+        add_targets(0, 0)
+        node_tile(TARGET, 1, on_scalar)
+        node_tile(TARGET, 2, on_vector)
+        add_targets(0, 1)
+        gather_sources(0, 2)
+        gather_sources(0, 3)
+        add_targets(0, 2)
+        gather_sources(1, 0, "sources00")
+        node_piece(TARGET, 3, 0, BANK, on_vector)
+        node_piece(TARGET, 3, BANK, BANK, on_scalar)
+        add_targets(1, 0)
+        add_targets(0, 3)
+        deal_w3_bytes()
+        gather_sources(1, 1, "sources01")
+        gather_sources(1, 2)
+        gather_sources(1, 3)
+        relu_round((0, 1))
+        add_targets(1, 1)
+        quantise_z((0, 1))
+        edge_products((0, 1))
+        add_targets(1, 2)
+        add_targets(1, 3)
+        gather_sources(2, 0, "sources10")
+        gather_sources(2, 1, "sources11")
+        copy_out((0, 1))
+        gather_sources(2, 2)
+        gather_sources(2, 3)
+        add_targets(2, 0)
+        relu_round((2, 3))
+        relu_round((4,))
+        quantise_z((2, 3))
+        edge_products((2, 3))
+        add_targets(2, 1)
+        quantise_z((4,))
+        edge_products((4,))
+        add_targets(2, 2)
+        add_targets(2, 3)
+        rounded_tile((0, 1))
+        round_from_bank(0)
+        round_from_bank(1)
+        copy_out((2, 3, 4))
+        rounded_tile((2, 3))
+        round_from_bank(2)
+        round_from_bank(3)
+        rounded_tile((4, 5))
+        round_from_bank(4)
+        add_targets(3, 0)
+        relu_round((5, 6))
+        add_targets(3, 1)
+        quantise_z((5, 6))
+        edge_products((5, 6))
+        add_targets(3, 2)
+        add_targets(3, 3)
+        copy_out((5, 6))
+        codes_tile((0, 1, 2, 3), "sources21")
+        quantise_out((0, 1), (0, 1, 2, 3))
+        relu_round((7,))
+        quantise_out((2, 3), (0, 1, 2, 3))
+        store_codes((0, 1, 2, 3))
+        quantise_z((7,))
+        last_product(7)
+        round_on_vector(5)
+        rounded_tile((6,))
+        round_on_vector(6)
+        codes_tile((4, 5, 6, 7))
+        quantise_out((4, 5), (4, 5, 6, 7))
+        rounded_tile((7,))
+        round_on_vector(7)
+        quantise_out((6,), (4, 5, 6, 7))
+        quantise_out((7,), (4, 5, 6, 7))
+        store_codes((4, 5, 6, 7))
         store_scales((nc.scalar, nc.sync))

@@ -33,9 +33,9 @@ LINE_COLUMNS = 2
 LINE_WORDS = 4
 ALIGN = 64
 SOURCE, TARGET = 0, 1
-CHUNKS = (256, 384, 256, 128)
+CHUNKS = (640, 256, 128)
 FIRSTS = [sum(CHUNKS[:c]) for c in range(len(CHUNKS))]
-GATHERS = (256, 384, 384)
+GATHERS = (640, 384)
 ROW = max(GATHERS)
 
 
@@ -95,7 +95,7 @@ def tile_picked_hub_relu_po_kernel(
         x_plane = place("x_plane", [P, T], U8)
         w1_raw = place("w1_raw", [P, PACK, H], F32)
         w2_raw = place("w2_raw", [P, PACK, H], F32)
-        w3_table = place("w3_table", [P, H], I32)
+        w3_table = place("w3_table", [P, H], I32, room=ROW * WIDTH[F32])
         w3_plane = place("w3_plane", [P, H], U8)
 
         nc.vector.memset(x_plane[:].bitcast(I32), 0)
@@ -195,18 +195,22 @@ def tile_picked_hub_relu_po_kernel(
                 if FIRSTS[u] < FIRSTS[c] + count:
                     sources[(u, t)] = picked[:, FIRSTS[u] - FIRSTS[c] : FIRSTS[u] - FIRSTS[c] + CHUNKS[u]]
 
-        def add_targets(c, t):
-            looked_up = windows[(TARGET, t)][:].indirect(entries(dst_sb, FIRSTS[c], CHUNKS[c]))
-            nc.vector.tensor_tensor(sums[c][:, t, :], looked_up, sources[(c, t)], ADD)
+        def add_targets(c, t, first=0, count=None):
+            edges = slice(first, first + (count or CHUNKS[c]))
+            looked_up = windows[(TARGET, t)][:].indirect(entries(dst_sb, FIRSTS[c] + first, count or CHUNKS[c]))
+            nc.vector.tensor_tensor(sums[c][:, t, edges], looked_up, sources[(c, t)][:, edges], ADD)
 
         def chunk_of(part):
             return max(c for c in range(len(CHUNKS)) if FIRSTS[c] <= part * PART)
 
-        def relu_round(parts, over=None, scalar=False):
+        def relu_round(parts, group=None, scalar=False):
+            group = group or parts
+            if group not in z_rounded:
+                z_rounded[group] = place("z_rounded%d" % group[0], [P, len(group) * PART, PACK], BF16)
             c, count = chunk_of(parts[0]), len(parts) * PART
-            first = parts[0] * PART - FIRSTS[c]
-            z_rounded[parts] = place("z_rounded%d" % parts[0], [P, count, PACK], BF16, over)
-            by_column, by_tile = interleaved(sums[c][:, :, first : first + count], z_rounded[parts][:])
+            first, begin = parts[0] * PART - FIRSTS[c], (parts[0] - group[0]) * PART
+            held = z_rounded[group][:, begin : begin + count, :]
+            by_column, by_tile = interleaved(sums[c][:, :, first : first + count], held)
             if scalar:
                 nc.scalar.activation(by_column, by_tile, RELU)
             else:
@@ -315,47 +319,40 @@ def tile_picked_hub_relu_po_kernel(
         node_tile(SOURCE, 1, on_scalar)
         node_tile(SOURCE, 2, on_vector, over="w2_raw")
         gather_sources(0, 0)
-        gather_sources(0, 1)
         node_tile(TARGET, 0, on_scalar)
         deal_w3_words()
         node_tile(SOURCE, 3, on_vector, over="w_rounded10")
         add_targets(0, 0)
+        gather_sources(0, 1, "w3_table")
         node_tile(TARGET, 1, on_scalar)
         node_tile(TARGET, 2, on_vector)
         add_targets(0, 1)
         gather_sources(0, 2)
         gather_sources(0, 3)
-        add_targets(0, 2)
-        gather_sources(1, 0, "sources00")
         node_piece(TARGET, 3, 0, BANK, on_vector)
+        add_targets(0, 2)
         node_piece(TARGET, 3, BANK, BANK, on_scalar)
-        add_targets(1, 0)
-        add_targets(0, 3)
+        add_targets(0, 3, 0, QUARTER)
         deal_w3_bytes()
+        relu_round((0, 1))
+        add_targets(0, 3, QUARTER, CHUNKS[0] - QUARTER)
+        quantise_z((0, 1))
+        edge_products((0, 1))
+        gather_sources(1, 0, "sources00")
         gather_sources(1, 1, "sources01")
         gather_sources(1, 2)
         gather_sources(1, 3)
-        relu_round((0, 1))
-        add_targets(1, 1)
-        quantise_z((0, 1))
-        edge_products((0, 1))
-        add_targets(1, 2)
-        add_targets(1, 3)
-        gather_sources(2, 0, "sources10")
-        gather_sources(2, 1, "sources11")
+        relu_round((4,), scalar=True)
         copy_out((0, 1))
-        gather_sources(2, 2)
-        gather_sources(2, 3)
-        add_targets(2, 0)
+        add_targets(1, 0)
         relu_round((2, 3))
-        relu_round((4,))
+        add_targets(1, 1)
         quantise_z((2, 3))
         edge_products((2, 3))
-        add_targets(2, 1)
         quantise_z((4,))
         edge_products((4,))
-        add_targets(2, 2)
-        add_targets(2, 3)
+        add_targets(1, 2)
+        add_targets(1, 3)
         rounded_tile((0, 1))
         round_from_bank(0)
         round_from_bank(1)
@@ -363,23 +360,23 @@ def tile_picked_hub_relu_po_kernel(
         rounded_tile((2, 3))
         round_from_bank(2)
         round_from_bank(3)
-        rounded_tile((4, 5))
-        round_from_bank(4)
-        add_targets(3, 0)
+        add_targets(2, 0)
         relu_round((5, 6))
-        add_targets(3, 1)
+        add_targets(2, 1)
         quantise_z((5, 6))
         edge_products((5, 6))
-        add_targets(3, 2)
-        add_targets(3, 3)
+        add_targets(2, 2)
+        add_targets(2, 3)
         copy_out((5, 6))
-        codes_tile((0, 1, 2, 3), "sources21")
+        codes_tile((0, 1, 2, 3), "sources11")
         quantise_out((0, 1), (0, 1, 2, 3))
         relu_round((7,))
-        quantise_out((2, 3), (0, 1, 2, 3))
-        store_codes((0, 1, 2, 3))
+        rounded_tile((4, 5))
+        round_on_vector(4)
         quantise_z((7,))
         last_product(7)
+        quantise_out((2, 3), (0, 1, 2, 3))
+        store_codes((0, 1, 2, 3))
         round_on_vector(5)
         rounded_tile((6,))
         round_on_vector(6)

@@ -329,9 +329,8 @@ def tile_picked_hub_relu_po_kernel(
         add_targets(0, 1)
         gather_sources(0, 2)
         gather_sources(0, 3)
-        node_piece(TARGET, 3, 0, BANK, on_vector)
         add_targets(0, 2)
-        node_piece(TARGET, 3, BANK, BANK, on_scalar)
+        node_tile(TARGET, 3, on_scalar)
         add_targets(0, 3, 0, QUARTER)
         deal_w3_bytes()
         relu_round((0, 1))

from contextlib import ExitStack

import concourse.mybir as mybir

K, T, S, H = 512, 2048, 1024, 512
FLOPS = 2 * K * H * S * 2 + 2 * H * H * S

F32 = mybir.dt.float32
BF16 = mybir.dt.bfloat16
I32 = mybir.dt.int32
U32 = mybir.dt.uint32
U16 = mybir.dt.uint16
U8 = mybir.dt.uint8
FP8X4 = mybir.dt.float8_e4m3fn_x4
WIDTH = {F32: 4, I32: 4, U32: 4, BF16: 2, U8: 1}
ADD = mybir.AluOpType.add
RELU = mybir.ActivationFunctionType.Relu
COPY = mybir.ActivationFunctionType.Copy

P = 128
PACK = 4
PAIR = 2
QUADRANTS = 4
QUADRANT = P // QUADRANTS
BANK = 512
BANKS = 8
PART = BANK // PACK
PIECE = BANK // 2
HALF = S // 2
QUARTER = S // PACK
LIST_ROWS = 16
LINE_COLUMNS = 2
LINE_WORDS = 4
ALIGN = 64
SOURCE, TARGET = 0, 1
CHUNKS = (640, 256, 128)
FIRSTS = [sum(CHUNKS[:c]) for c in range(len(CHUNKS))]
GATHERS = (640, 384)
ROW = max(GATHERS)


def scale_rows(plane, scales, r):
    return plane[r:P:QUADRANT, :].bitcast(I32), scales[0, r::QUADRANTS, :].bitcast(I32)


def as_words(packed):
    return packed[0].rearrange("p n j -> p (n j)").bitcast(I32)


def interleaved(by_tile, by_column):
    return (
        by_column.rearrange("p (g i) t -> p g t i", i=LINE_COLUMNS),
        by_tile.rearrange("p t (g i) -> p g t i", i=LINE_COLUMNS),
    )


def entries(offsets, first, count):
    return offsets[:, first // LIST_ROWS : (first + count) // LIST_ROWS]


def tile_picked_hub_relu_po_kernel(
    tc, x_words, x_scales, w1, w2, w3_words, w3_scales, offs, src, dst, out_0, out_1, out_2
):
    nc = tc.nc
    with ExitStack() as ctx:
        lists = ctx.enter_context(tc.tile_pool(name="lists", bufs=1))
        placed = ctx.enter_context(tc.tile_pool(name="placed", bufs=1))
        psum = ctx.enter_context(tc.psum_pool(name="psum", bufs=1))

        starts = {}
        used = [0]

        def place(name, shape, dtype, over=None, room=0):
            if over is None:
                starts[name] = used[0]
                size = WIDTH[dtype]
                for extent in shape[1:]:
                    size = size * extent
                used[0] = starts[name] + max(room, -(-size // ALIGN) * ALIGN)
            else:
                starts[name] = starts[over]
            return placed.tile(shape, dtype, name=name, tag=name, align_bytes=ALIGN, offset=starts[name])

        banks_taken = []

        def next_bank(shape):
            name = "bank%d" % (len(banks_taken) % BANKS)
            banks_taken.append(name)
            return psum.tile(shape, F32, name=name, tag=name)

        offs_sb = lists.tile([P, S // LIST_ROWS], U16, name="offs_sb")
        src_sb = lists.tile([P, S // LIST_ROWS], U16, name="src_sb")
        dst_sb = lists.tile([P, S // LIST_ROWS], U16, name="dst_sb")
        x_table = place("x_table", [P, T], I32)
        x_plane = place("x_plane", [P, T], U8)
        w1_raw = place("w1_raw", [P, PACK, H], F32)
        w2_raw = place("w2_raw", [P, PACK, H], F32)
        w3_table = place("w3_table", [P, H], I32, room=ROW * WIDTH[F32])
        w3_plane = place("w3_plane", [P, H], U8)

        nc.vector.memset(x_plane[:].bitcast(I32), 0)
        nc.vector.memset(w3_plane[:].bitcast(I32), 0)
        nc.sync.dma_start(offs_sb[:], offs)
        nc.sync.dma_start(src_sb[:], src)
        nc.sync.dma_start(dst_sb[:], dst)
        for q in range(QUADRANTS):
            nc.sync.dma_start(*scale_rows(x_plane, x_scales, q))
        nc.sync.dma_start(x_table[:], as_words(x_words))
        nc.sync.dma_start(w1_raw[:], w1.rearrange("(p j) c -> p j c", j=PACK))
        nc.sync.dma_start(w2_raw[:], w2.rearrange("(p j) c -> p j c", j=PACK))
        nc.sync.dma_start(w3_table[:], as_words(w3_words))
        for q in range(QUADRANTS):
            nc.sync.dma_start(*scale_rows(w3_plane, w3_scales, q))

        by_row = {
            SOURCE: w1_raw[:].rearrange("p j (m t) -> p m j t", t=PACK),
            TARGET: w2_raw[:].rearrange("p j (m t) -> p m j t", t=PACK),
        }
        rounded, weights = {}, {}

        def round_pair(side, first, copy, columns=slice(0, P), over=None):
            if (side, first) not in rounded:
                rounded[(side, first)] = place("w_rounded%d%d" % (side, first), [P, PAIR, P, PACK], BF16, over)
            by_tile = rounded[(side, first)][:].rearrange("p t m j -> p m j t")
            copy(by_tile[:, columns], by_row[side][:, columns, :, first : first + PAIR])

        def quantise_weight(side, first, count):
            codes = place("w_codes%d%d" % (side, first), [P, count * P], U32)
            plane = place("w_plane%d%d" % (side, first), [P, count * P], U8)
            source = rounded[(side, first - first % PAIR)][:, first % PAIR : first % PAIR + count]
            nc.vector.quantize_mx(
                out=codes[:].bitcast(FP8X4), scales=plane[:], in_=source.rearrange("p t m j -> p (t m j)")
            )
            for u in range(count):
                weights[(side, first + u)] = (codes[:, u * P : (u + 1) * P], plane[:, u * P : (u + 1) * P])

        x_codes = place("x_codes", [P, S], U32)
        x_bytes = place("x_bytes", [P, S], U8)
        windows = {}

        def node_piece(side, t, first, width, copy, over=None):
            codes, plane = weights[(side, t)]
            if (side, t) not in windows:
                windows[(side, t)] = place("window%d%d" % (side, t), [P, S], F32, over)
            nodes = slice(first, first + width)
            acc = next_bank([P, width])
            nc.tensor.matmul_mx(
                out=acc[:],
                lhsT=codes.bitcast(FP8X4),
                lhsT_scale=plane,
                rhs=x_codes[:, nodes].bitcast(FP8X4),
                rhs_scale=x_bytes[:, nodes],
                start=True,
                stop=True,
            )
            copy(windows[(side, t)][:, nodes], acc[:])

        def node_tile(side, t, copy, width=BANK, over=None):
            for first in range(0, S, width):
                node_piece(side, t, first, width, copy, over)

        w3_dealt = {}

        def deal_w3_words(over=None):
            w3_dealt["codes"] = place("w3_codes", [P, H], I32, over)
            nc.vector.tensor_copy(
                w3_dealt["codes"][:].rearrange("p (t g i) -> p g t i", t=PACK, i=LINE_WORDS),
                w3_table[:].rearrange("p (g i t) -> p g t i", t=PACK, i=LINE_WORDS),
            )

        def deal_w3_bytes(over=None):
            w3_dealt["bytes"] = place("w3_bytes", [P, H], U8, over)
            nc.vector.tensor_copy(
                w3_dealt["bytes"][:].rearrange("p (t m) -> p t m", t=PACK),
                w3_plane[:].rearrange("p (m t) -> p t m", t=PACK),
            )

        arena = place("arena", [P, PAIR * (len(CHUNKS) + 1) * ROW], F32)
        arena_rows = arena[:].rearrange("p (r n) -> p r n", n=ROW)
        first_row = [PAIR * (len(CHUNKS) - 1 - c) for c in range(len(CHUNKS))]
        sums = [arena_rows[:, first_row[c] : first_row[c] + PACK, : CHUNKS[c]] for c in range(len(CHUNKS))]
        sources, z_rounded, z_packed, accs, results, out_rounded, out_codes = {}, {}, {}, {}, {}, {}, {}
        out_plane = place("out_plane", [P, QUARTER], U8)
        out_rows = out_0.rearrange("(p t) n -> p t n", t=PACK)

        def gather_sources(c, t, over=None):
            count = GATHERS[c]
            if t >= PAIR:
                picked = arena_rows[:, first_row[c + 1] + t - PAIR, :count]
            else:
                picked = place("sources%d%d" % (c, t), [P, count], F32, over, ROW * WIDTH[F32])[:]
            looked_up = windows[(SOURCE, t)][:].indirect(entries(src_sb, FIRSTS[c], count))
            nc.scalar.activation(picked, looked_up, COPY)
            for u in range(c, len(CHUNKS)):
                if FIRSTS[u] < FIRSTS[c] + count:
                    sources[(u, t)] = picked[:, FIRSTS[u] - FIRSTS[c] : FIRSTS[u] - FIRSTS[c] + CHUNKS[u]]

        def add_targets(c, t, first=0, count=None):
            edges = slice(first, first + (count or CHUNKS[c]))
            looked_up = windows[(TARGET, t)][:].indirect(entries(dst_sb, FIRSTS[c] + first, count or CHUNKS[c]))
            nc.vector.tensor_tensor(sums[c][:, t, edges], looked_up, sources[(c, t)][:, edges], ADD)

        def chunk_of(part):
            return max(c for c in range(len(CHUNKS)) if FIRSTS[c] <= part * PART)

        def relu_round(parts, group=None, scalar=False):
            group = group or parts
            if group not in z_rounded:
                z_rounded[group] = place("z_rounded%d" % group[0], [P, len(group) * PART, PACK], BF16)
            c, count = chunk_of(parts[0]), len(parts) * PART
            first, begin = parts[0] * PART - FIRSTS[c], (parts[0] - group[0]) * PART
            held = z_rounded[group][:, begin : begin + count, :]
            by_column, by_tile = interleaved(sums[c][:, :, first : first + count], held)
            if scalar:
                nc.scalar.activation(by_column, by_tile, RELU)
            else:
                nc.vector.tensor_scalar_max(by_column, by_tile, 0.0)

        def quantise_z(parts):
            codes = place("z_codes%d" % parts[0], [P, len(parts) * PART], U32)
            plane = place("z_plane%d" % parts[0], [P, len(parts) * PART], U8)
            nc.vector.quantize_mx(
                out=codes[:].bitcast(FP8X4), scales=plane[:], in_=z_rounded[parts][:].rearrange("p n t -> p (n t)")
            )
            for u, part in enumerate(parts):
                z_packed[part] = (codes[:, u * PART : (u + 1) * PART], plane[:, u * PART : (u + 1) * PART])

        def w3_product(acc, t, part):
            codes, plane = z_packed[part]
            columns = slice(t * P, (t + 1) * P)
            nc.tensor.matmul_mx(
                out=acc,
                lhsT=w3_dealt["codes"][:, columns].bitcast(FP8X4),
                lhsT_scale=w3_dealt["bytes"][:, columns],
                rhs=codes.bitcast(FP8X4),
                rhs_scale=plane,
                start=True,
                stop=True,
            )

        def edge_products(parts):
            for part in parts:
                accs[part] = next_bank([P, PACK, PART])
                for t in range(PACK):
                    w3_product(accs[part][:, t, :], t, part)

        def store_results(part, held):
            nc.sync.dma_start(out_rows[:, :, part * PART : part * PART + held.shape[2]], held)

        def copy_out(parts, over=None):
            held = place("results%d" % parts[0], [P, PACK, len(parts) * PART], F32, over)
            for u, part in enumerate(parts):
                results[part] = held[:, :, u * PART : (u + 1) * PART]
                nc.scalar.copy(results[part], accs[part][:])
            results[parts] = held[:]
            store_results(parts[0], held[:])

        def last_product(part):
            held = place("results%d" % part, [P, PACK, PART], F32)
            for first in range(0, PACK, PAIR):
                acc = next_bank([P, PAIR, PART])
                for u in range(PAIR):
                    w3_product(acc[:, u, :], first + u, part)
                nc.scalar.copy(held[:, first : first + PAIR, :], acc[:])
            results[part] = held[:]
            store_results(part, held[:])

        def rounded_tile(parts, over=None):
            whole = place("out_rounded%d" % parts[0], [P, len(parts) * PART, PACK], BF16, over)
            out_rounded[parts] = whole[:]
            for u, part in enumerate(parts):
                out_rounded[part] = whole[:, u * PART : (u + 1) * PART, :]

        def round_from_bank(part):
            nc.scalar.copy(*interleaved(accs[part][:], out_rounded[part]))

        def round_on_vector(parts):
            nc.vector.tensor_copy(*interleaved(results[parts], out_rounded[parts]))

        def codes_tile(parts, over=None):
            out_codes[parts] = place("out_codes%d" % parts[0], [P, len(parts) * PART], U32, over)

        def quantise_out(parts, stored):
            quarter, first = divmod(parts[0] * PART, QUARTER)
            begin, count = (parts[0] - stored[0]) * PART, len(parts) * PART
            source = out_rounded[parts] if len(parts) > 1 else out_rounded[parts[0]]
            nc.vector.quantize_mx(
                out=out_codes[stored][:, begin : begin + count].bitcast(FP8X4),
                scales=out_plane[PACK * quarter :, first : first + count],
                in_=source.rearrange("p n t -> p (n t)"),
            )

        def store_codes(parts):
            columns = slice(parts[0] * PART, (parts[-1] + 1) * PART)
            nc.sync.dma_start(as_words(out_1)[:, columns], out_codes[parts][:].bitcast(I32))

        def store_scales(queues):
            for q in range(QUADRANTS):
                rows = out_2[0, PACK * q : PACK * (q + 1), :].rearrange("r (a n) -> a r n", n=QUARTER)
                live = out_plane[QUADRANT * q : QUADRANT * q + PACK * PACK, :]
                queues[q % len(queues)].dma_start(rows.bitcast(I32), live.bitcast(I32))

        on_scalar, on_vector = nc.scalar.copy, nc.vector.tensor_copy

        nc.vector.tensor_copy(x_bytes[:], x_plane[:].indirect(offs_sb[:]))
        nc.vector.tensor_copy(x_codes[:], x_table[:].bitcast(U32).indirect(offs_sb[:]))

        for first in (0, PAIR):
            round_pair(SOURCE, first, on_scalar, slice(P // 2, P))
            round_pair(SOURCE, first, on_vector, slice(0, P // 2))
        quantise_weight(SOURCE, 0, 1)
        quantise_weight(SOURCE, 1, 1)
        quantise_weight(SOURCE, PAIR, PAIR)
        for first in (0, PAIR):
            round_pair(TARGET, first, on_vector)
        for first in (0, PAIR):
            quantise_weight(TARGET, first, PAIR)
        node_tile(SOURCE, 0, on_scalar, PIECE)
        node_tile(SOURCE, 1, on_scalar)
        node_tile(SOURCE, 2, on_vector, over="w2_raw")
        gather_sources(0, 0)
        node_tile(TARGET, 0, on_scalar)
        deal_w3_words()
        node_tile(SOURCE, 3, on_vector, over="w_rounded10")
        add_targets(0, 0)
        gather_sources(0, 1, "w3_table")
        node_tile(TARGET, 1, on_scalar)
        node_tile(TARGET, 2, on_vector)
        add_targets(0, 1)
        gather_sources(0, 2)
        gather_sources(0, 3)
        add_targets(0, 2)
        node_tile(TARGET, 3, on_scalar)
        add_targets(0, 3, 0, QUARTER)
        deal_w3_bytes()
        relu_round((0, 1))
        add_targets(0, 3, QUARTER, CHUNKS[0] - QUARTER)
        quantise_z((0, 1))
        edge_products((0, 1))
        gather_sources(1, 0, "sources00")
        gather_sources(1, 1, "sources01")
        gather_sources(1, 2)
        gather_sources(1, 3)
        relu_round((4,), scalar=True)
        copy_out((0, 1))
        add_targets(1, 0)
        relu_round((2, 3))
        add_targets(1, 1)
        quantise_z((2, 3))
        edge_products((2, 3))
        quantise_z((4,))
        edge_products((4,))
        add_targets(1, 2)
        add_targets(1, 3)
        rounded_tile((0, 1))
        round_from_bank(0)
        round_from_bank(1)
        copy_out((2, 3, 4))
        rounded_tile((2, 3))
        round_from_bank(2)
        round_from_bank(3)
        add_targets(2, 0)
        relu_round((5, 6))
        add_targets(2, 1)
        quantise_z((5, 6))
        edge_products((5, 6))
        add_targets(2, 2)
        add_targets(2, 3)
        copy_out((5, 6))
        codes_tile((0, 1, 2, 3), "sources11")
        quantise_out((0, 1), (0, 1, 2, 3))
        relu_round((7,))
        rounded_tile((4, 5))
        round_on_vector(4)
        quantise_z((7,))
        last_product(7)
        quantise_out((2, 3), (0, 1, 2, 3))
        store_codes((0, 1, 2, 3))
        round_on_vector(5)
        rounded_tile((6,))
        round_on_vector(6)
        codes_tile((4, 5, 6, 7))
        quantise_out((4, 5), (4, 5, 6, 7))
        rounded_tile((7,))
        round_on_vector(7)
        quantise_out((6,), (4, 5, 6, 7))
        quantise_out((7,), (4, 5, 6, 7))
        store_codes((4, 5, 6, 7))
        store_scales((nc.scalar, nc.sync))
